import numpy as np
import ml_dtypes


def mxq(x, axis, fmt="e4m3"):
    dtype, down = {"e4m3": (ml_dtypes.float8_e4m3fn, 7), "e5m2": (ml_dtypes.float8_e5m2, 14)}[fmt]
    v = np.moveaxis(np.asarray(x, np.float32).astype(ml_dtypes.bfloat16).astype(np.float64), axis, -1)
    blocks = v.reshape(v.shape[:-1] + (-1, 32))
    amax = np.abs(blocks).max(-1, keepdims=True)
    byte = np.maximum(np.where(amax > 0, np.frexp(amax)[1] - 1 + 127, 0) - down, 1)
    scale = np.exp2(byte - 127.0)
    codes = (blocks / scale).astype(np.float32).astype(dtype).astype(np.float64)
    return np.moveaxis((codes * scale).reshape(v.shape), -1, axis)


WIDE = False


def mx_kscale(k):
    if not WIDE:
        return np.ones(k)
    levels = np.array([10, -10, 5, -5, 0])
    if k % 512:
        return np.exp2(np.random.permutation(np.resize(levels, k // 32))).repeat(32)
    a = np.empty((k // 512, 16))
    for p in range(k // 512):
        a[p, :8] = np.random.permutation(np.resize(levels, 8))
        for g in range(8):
            far = levels[np.abs(levels - a[p, g]) >= 10]
            a[p, g + 8] = far[np.random.randint(len(far))]
    return np.exp2(a.ravel()).repeat(32)


def f64(x):
    return np.asarray(x).astype(np.float64)


def striped(idx):
    return np.tile(idx.reshape(-1, 16).T, (8, 1)).astype(np.uint16)


def unstriped(offs):
    return offs[:16].T.reshape(-1).astype(np.int64)


def striped8(idx):
    return np.concatenate([x.reshape(-1, 16).T for x in idx]).astype(np.uint16)


def runs(offs, k):
    lists = np.stack([offs[16 * r : 16 * r + 16].T.reshape(-1) for r in range(8)]).astype(np.int64)
    return lists[np.arange(k) % 512 // 64]


def pack_weight(w):
    k, n = w.shape
    w = f64(np.asarray(w, np.float32).astype(ml_dtypes.bfloat16)).reshape(k // 32, 32, n)
    amax = np.abs(w).max(1)
    byte = np.clip(np.where(amax > 0, np.frexp(amax)[1] - 1 + 127 - 7, 1), 1, 254)
    scaled = (w * np.exp2(127.0 - byte)[:, None, :]).reshape(k, n).astype(np.float32)
    words = np.ascontiguousarray(scaled.reshape(k // 512, 128, 4, n).transpose(0, 1, 3, 2)).astype(ml_dtypes.float8_e4m3fn).view(np.uint8)
    return words, np.ascontiguousarray(byte.astype(np.uint8).reshape(k // 512, 16, n))


def unpack_weight(words, scales):
    g, p, n, _ = words.shape
    vals = np.ascontiguousarray(words).view(ml_dtypes.float8_e4m3fn).astype(np.float64) * np.repeat(np.exp2(scales.astype(np.float64) - 127.0), 8, axis=1)[..., None]
    return vals.transpose(0, 1, 3, 2).reshape(g * 512, n)

def planes(y):
    n, m = y.shape
    v = y.astype(np.float32).astype(ml_dtypes.bfloat16).astype(np.float64).reshape(n // 32, 32, m)
    top = np.abs(v).max(1)
    byte = np.clip(np.where(top > 0, np.frexp(top)[1] - 1 + 127 - 7, 1), 1, 254)
    codes = (v * np.exp2(127.0 - byte)[:, None, :]).reshape(n, m).astype(np.float32).astype(ml_dtypes.float8_e4m3fn).view(np.uint8)
    words = codes.reshape(n // 512, 128, 4, m).transpose(0, 1, 3, 2)
    return np.ascontiguousarray(words), np.ascontiguousarray(byte.astype(np.uint8).reshape(n // 512, 16, m))


K, T, S, N, H = 512, 2048, 512, 512, 512
P = 2 ** 7


def setup_inputs():
    n = np.random.standard_normal
    s = mx_kscale(K)[:, None]
    u = mx_kscale(H)
    packed_xT = pack_weight(n((K, T)) * s)
    packed_w1 = pack_weight(n((K, H)) / np.sqrt(K) / s)
    packed_w2 = pack_weight(n((H, N)) / np.sqrt(2 * H) / u[:, None])
    packed_w3 = pack_weight(n((H, N)) / np.sqrt(2 * H) / u[:, None])
    return {
        "x_words": packed_xT[0],
        "x_scales": packed_xT[1],
        "w1_words": packed_w1[0],
        "w1_scales": packed_w1[1],
        "g1": np.tile(np.random.uniform(0.1, 0.8, S), (P, 1)).astype(np.float32),
        "g2": np.tile(np.random.uniform(0.1, 0.8, S), (P, 1)).astype(np.float32),
        "g3": np.tile(np.random.uniform(0.1, 0.8, S), (P, 1)).astype(np.float32),
        "c2": (np.random.uniform(0.5, 1.5, (H, 1)) * u[:, None]).astype(np.float32),
        "c1": (np.random.uniform(0.5, 1.5, (H, 1)) * u[:, None]).astype(np.float32),
        "w2_words": packed_w2[0],
        "w2_scales": packed_w2[1],
        "w3_words": packed_w3[0],
        "w3_scales": packed_w3[1],
        "offs": striped(np.random.permutation(T)[:S]),
        "p1": striped8(np.stack([np.random.permutation(S) for _ in range(8)])),
        "p2": striped8(np.stack([np.random.permutation(S) for _ in range(8)])),
        "p3": striped8(np.stack([np.random.permutation(S) for _ in range(8)])),
    }


def reference(x_words, x_scales, w1_words, w1_scales, g1, g2, g3, c2, c1, w2_words, w2_scales, w3_words, w3_scales, offs, p1, p2, p3):
    xq = unpack_weight(x_words, x_scales)[:, unstriped(offs)]
    y = unpack_weight(w1_words, w1_scales).T @ xq
    a = f64(g1)[:1] * (y[np.arange(H)[:, None], runs(p1, H)]) + f64(g2)[:1] * (y[np.arange(H)[:, None], runs(p2, H)]) + f64(g3)[:1] * (y[np.arange(H)[:, None], runs(p3, H)])
    z2 = f64(c1) * a
    z = f64(c2) * ((a) ** 2)
    out_0 = unpack_weight(w2_words, w2_scales).T @ mxq(z2, 0, "e4m3") + unpack_weight(w3_words, w3_scales).T @ mxq(z, 0, "e4m3")
    return (out_0,) + planes(out_0)

@@ -1,0 +1,271 @@
+from contextlib import ExitStack
+
+import concourse.mybir as mybir
+from concourse.masks import make_identity
+
+K, T, S, N, H = 512, 2048, 512, 512, 512
+FLOPS = 3 * 2 * 512 * 512 * 512
+
+F32 = mybir.dt.float32
+BF16 = mybir.dt.bfloat16
+I32 = mybir.dt.int32
+U32 = mybir.dt.uint32
+U16 = mybir.dt.uint16
+U8 = mybir.dt.uint8
+FP8X4 = mybir.dt.float8_e4m3fn_x4
+MULT = mybir.AluOpType.mult
+ADD = mybir.AluOpType.add
+COPY = mybir.ActivationFunctionType.Copy
+SQUARE = mybir.ActivationFunctionType.Square
+
+P = 128
+PACK = 4
+B = 128
+BLOCKS = S // B
+LIST_COLS = B // 16
+
+
+def tile_picked_ace8_none_po_kernel(
+    tc, x_words, x_scales, w1_words, w1_scales, g1, g2, g3, c2, c1,
+    w2_words, w2_scales, w3_words, w3_scales, offs, p1, p2, p3, out_0, out_1, out_2,
+):
+    nc = tc.nc
+    with ExitStack() as ctx:
+        keep = ctx.enter_context(tc.tile_pool(name="keep", bufs=1))
+        psum = ctx.enter_context(tc.psum_pool(name="psum", bufs=1))
+
+        def sb(name, shape, dtype, tag=None):
+            return keep.tile(shape, dtype, name=name, tag=tag or name, align_bytes=64)
+
+        def bank(name, number):
+            return psum.tile([P, 512], F32, name=name, tag="bank%d" % number)
+
+        def words_of(w):
+            return w[0].rearrange("p n t -> p (n t)").bitcast(I32)
+
+        def load_scales(queue, tile, first, src):
+            for q in range(4):
+                queue.dma_start(
+                    out=tile[32 * q + first : 32 * q + first + 4, :].bitcast(I32),
+                    in_=src[0, 4 * q : 4 * q + 4, :].bitcast(I32),
+                )
+
+        def fill_scales(queue, tile, src):
+            for q in range(4):
+                queue.dma_start(
+                    out=tile[32 * q : 32 * q + 32, :].bitcast(I32),
+                    in_=src[0, 4 * q : 4 * q + 4, :].bitcast(I32).unsqueeze(0).broadcast_to([8, 4, src.shape[2] // 4]),
+                )
+
+        def deal(dst, src, t0, t1):
+            nc.vector.tensor_copy(
+                out=dst[:].rearrange("p (t m) -> p t m", t=PACK)[:, t0:t1, :],
+                in_=src[:].rearrange("p (m t) -> p t m", t=PACK)[:, t0:t1, :],
+            )
+
+        def deal_bytes(dst, src):
+            nc.vector.tensor_copy(
+                out=dst[:].rearrange("p (t m) -> p m t", t=PACK),
+                in_=src[:].rearrange("p (m t) -> p m t", t=PACK),
+            )
+
+        offs_sb = sb("offs_sb", [P, S // 16], U16)
+        lists = [sb("list%d" % n, [P, S // 16], U16) for n in range(3)]
+        xw = sb("xw", [P, T], I32)
+        xs = sb("xs", [P, T], U8)
+        w_raw = [sb("w_raw%d" % i, [P, H], I32) for i in range(3)]
+        s_raw = sb("s_raw", [P, H], U8)
+        gates = [sb("gate%d" % n, [P, S], F32) for n in range(3)]
+        c1_sb = sb("c1_sb", [P, PACK], F32)
+        c2_sb = sb("c2_sb", [P, PACK], F32)
+        ident = sb("ident", [P, P], F32)
+
+        nc.sync.dma_start(out=xw[:], in_=words_of(x_words))
+        nc.sync.dma_start(offs_sb[:], offs)
+        fill_scales(nc.scalar, xs, x_scales)
+        fill_scales(nc.scalar, s_raw, w1_scales)
+        nc.sync.dma_start(out=w_raw[0][:], in_=words_of(w1_words))
+        nc.sync.dma_start(lists[0][:], p1)
+        nc.sync.dma_start(out=w_raw[1][:], in_=words_of(w2_words))
+        nc.sync.dma_start(lists[1][:], p2)
+        nc.sync.dma_start(out=gates[0][:], in_=g1)
+        nc.sync.dma_start(lists[2][:], p3)
+        nc.sync.dma_start(out=w_raw[2][:], in_=words_of(w3_words))
+        nc.sync.dma_start(out=gates[1][:], in_=g2)
+        nc.sync.dma_start(out=gates[2][:], in_=g3)
+        nc.gpsimd.dma_start(out=c1_sb[:], in_=c1.rearrange("(p t) o -> p (t o)", t=PACK))
+        nc.gpsimd.dma_start(out=c2_sb[:], in_=c2.rearrange("(p t) o -> p (t o)", t=PACK))
+        make_identity(nc, ident[:])
+        warm = sb("warm", [P, 1], F32)
+        nc.scalar.activation(warm[:], ident[:, 0:1], SQUARE)
+
+        xg_s = sb("xg_s", [P, S], U8)
+        xg_w = sb("xg_w", [P, S], U32)
+        w_dealt = [sb("w_dealt%d" % i, [P, H], I32) for i in range(3)]
+        s1 = sb("s1", [P, H], U8)
+        s23 = sb("s23", [P, N], U8)
+        nc.vector.tensor_copy(out=xg_s[:], in_=xs[:].indirect(offs_sb[:]))
+        deal_bytes(s1, s_raw)
+        load_scales(nc.sync, s_raw, 4, w2_scales)
+        load_scales(nc.sync, s_raw, 8, w3_scales)
+        half = S // 2
+        nc.vector.tensor_copy(out=xg_w[:, :half], in_=xw[:].bitcast(U32).indirect(offs_sb[:, : half // 16]))
+        deal(w_dealt[0], w_raw[0], 0, 2)
+        nc.vector.tensor_copy(out=xg_w[:, half:], in_=xw[:].bitcast(U32).indirect(offs_sb[:, half // 16 :]))
+        deal(w_dealt[0], w_raw[0], 2, 4)
+
+        y = []
+        for t in range(PACK):
+            y_ps = bank("y_ps%d" % t, t)
+            y_t = sb("y%d" % t, [P, S], F32)
+            spans = [(0, half), (half, S)] if t == 0 else [(0, S)]
+            for lo, hi in spans:
+                nc.tensor.matmul_mx(
+                    out=y_ps[:, lo:hi],
+                    lhsT=w_dealt[0][:, t * P : (t + 1) * P].bitcast(FP8X4),
+                    lhsT_scale=s1[:, t * P : (t + 1) * P],
+                    rhs=xg_w[:, lo:hi].bitcast(FP8X4),
+                    rhs_scale=xg_s[:, lo:hi],
+                    start=True,
+                    stop=True,
+                )
+            nc.scalar.copy(out=y_t[:], in_=y_ps[:])
+            y.append(y_t)
+        deal(w_dealt[1], w_raw[1], 0, 4)
+        deal(w_dealt[2], w_raw[2], 0, 4)
+        deal_bytes(s23, s_raw)
+
+        out_codes = sb("out_codes", [P, S], U32)
+        out_scales = sb("out_scales", [P, S], U8)
+        out_rows = out_0.rearrange("(p t) j -> p t j", t=PACK)
+        out_words = words_of(out_1)
+
+        planes, zi, out_ps = {}, {}, {}
+
+        def gather(dst, b, t, n):
+            nc.vector.tensor_tensor(
+                dst,
+                y[t][:].indirect(lists[n][:, b * LIST_COLS : (b + 1) * LIST_COLS]),
+                gates[n][:, b * B : (b + 1) * B],
+                MULT,
+            )
+
+        def front(b, u, terms):
+            summed = bank("summed%d%d" % (b, u), 4)
+            for e in range(2):
+                for n in range(3):
+                    gather(terms[:, e, n, :], b, 2 * u + e, n)
+                    nc.tensor.matmul(
+                        summed[:, e * P : (e + 1) * P], terms[:, e, n, :], ident[:],
+                        start=(n == 0), stop=(n == 2), is_transpose=True,
+                    )
+            turned = sb("turned%d%d" % (b, u), [P, 2 * P], F32)
+            nc.scalar.copy(out=turned[:], in_=summed[:, : 2 * P])
+            a_ps = bank("a_ps%d%d" % (b, u), 5 + u)
+            for e in range(2):
+                nc.tensor.transpose(a_ps[:, e * B : (e + 1) * B], turned[:, e * P : (e + 1) * P], ident[:])
+            return a_ps
+
+        def scale_planes(b, u, a_ps):
+            if b not in planes:
+                planes[b] = sb("planes%d" % b, [P, 2, PACK, B], BF16)
+            sq = sb("sq%d%d" % (b, u), [P, 2 * B], F32)
+            for e in range(2):
+                t = 2 * u + e
+                nc.scalar.activation(planes[b][:, 0, t, :], a_ps[:, e * B : (e + 1) * B], COPY, scale=c1_sb[:, t : t + 1])
+            nc.scalar.activation(sq[:], a_ps[:, : 2 * B], SQUARE)
+            for e in range(2):
+                t = 2 * u + e
+                nc.scalar.activation(planes[b][:, 1, t, :], sq[:, e * B : (e + 1) * B], COPY, scale=c2_sb[:, t : t + 1])
+
+        def second(b, on_scalar, tag):
+            zi[b] = sb("zi%d" % b, [P, 2, B, PACK], BF16, tag)
+            src = planes[b][:].rearrange("p z t j -> p z j t")
+            if on_scalar:
+                nc.scalar.copy(out=zi[b][:], in_=src)
+            else:
+                nc.vector.tensor_copy(out=zi[b][:], in_=src)
+            codes = sb("z_codes%d" % b, [P, 2 * B], U32)
+            scales = sb("z_scales%d" % b, [P, 2 * B], U8)
+            nc.vector.quantize_mx(
+                out=codes[:].bitcast(FP8X4), scales=scales[:], in_=zi[b][:].rearrange("p z j t -> p (z j t)")
+            )
+            out_ps[b] = bank("out_ps%d" % b, b)
+            for t in range(PACK):
+                for z in range(2):
+                    nc.tensor.matmul_mx(
+                        out=out_ps[b][:, t * B : (t + 1) * B],
+                        lhsT=w_dealt[1 + z][:, t * P : (t + 1) * P].bitcast(FP8X4),
+                        lhsT_scale=s23[4 + 4 * z : P, t * P : (t + 1) * P],
+                        rhs=codes[:, z * B : (z + 1) * B].bitcast(FP8X4),
+                        rhs_scale=scales[:, z * B : (z + 1) * B],
+                        start=(z == 0),
+                        stop=(z == 1),
+                    )
+
+        def leave(b, on_scalar):
+            cols = slice(b * B, (b + 1) * B)
+            res = sb("res%d" % b, [P, PACK, B], F32)
+            res_i = sb("res_i%d" % b, [P, B, PACK], BF16)
+            nc.scalar.copy(out=res[:].rearrange("p t j -> p (t j)"), in_=out_ps[b][:])
+            nc.sync.dma_start(out=out_rows[:, :, cols], in_=res[:])
+            if on_scalar:
+                nc.scalar.copy(out=res_i[:], in_=out_ps[b][:].rearrange("p (t j) -> p j t", t=PACK))
+            else:
+                nc.vector.tensor_copy(out=res_i[:], in_=res[:].rearrange("p t j -> p j t"))
+            nc.vector.quantize_mx(
+                out=out_codes[:, cols].bitcast(FP8X4), scales=out_scales[:, cols],
+                in_=res_i[:].rearrange("p j t -> p (j t)"),
+            )
+            nc.sync.dma_start(out=out_words[:, cols], in_=out_codes[:, cols].bitcast(I32))
+
+        def terms_tile(name, units, tag=None):
+            return sb(name, [P, units, 2, 3, B], F32, tag)
+
+        early = terms_tile("early", 5)
+        a = front(0, 0, early[:, 0])
+        scale_planes(0, 0, a)
+        a = front(0, 1, early[:, 1])
+        scale_planes(0, 1, a)
+        a = front(1, 0, early[:, 2])
+        second(0, True, "tie0")
+        scale_planes(1, 0, a)
+        a = front(1, 1, early[:, 3])
+        scale_planes(1, 1, a)
+        a = front(2, 0, early[:, 4])
+        second(1, True, "tie1")
+        scale_planes(2, 0, a)
+        middle = terms_tile("middle", 2, "tie0")
+        a = front(2, 1, middle[:, 0])
+        leave(0, True)
+        scale_planes(2, 1, a)
+        a = front(3, 0, middle[:, 1])
+        scale_planes(3, 0, a)
+
+        last = sb("last", [P, 3, 2, B], F32, "tie1")
+        part = sb("part", [P, 2, B], F32)
+        a_sb = sb("a_sb", [P, 2, B], F32)
+        for n in range(2):
+            for e in range(2):
+                gather(last[:, n, e, :], 3, 2 + e, n)
+        gather(last[:, 2, 0, :], 3, 2, 2)
+        nc.vector.tensor_tensor(part[:], last[:, 0], last[:, 1], ADD)
+        gather(last[:, 2, 1, :], 3, 3, 2)
+        nc.vector.tensor_tensor(a_sb[:], part[:], last[:, 2], ADD)
+        second(2, False, None)
+        for e in range(2):
+            t = 2 + e
+            nc.vector.tensor_scalar(planes[3][:, 0, t, :], a_sb[:, e, :], c1_sb[:, t : t + 1], None, MULT)
+            nc.vector.scalar_tensor_tensor(
+                planes[3][:, 1, t, :], a_sb[:, e, :], c2_sb[:, t : t + 1], a_sb[:, e, :], MULT, MULT
+            )
+        second(3, False, None)
+        leave(1, False)
+        leave(2, False)
+        leave(3, False)
+        for q in range(4):
+            queue = nc.sync if q % 2 == 0 else nc.scalar
+            queue.dma_start(
+                out=out_2[0, 4 * q : 4 * q + 4, :].bitcast(I32),
+                in_=out_scales[32 * q : 32 * q + 4, :].bitcast(I32),
+            )

@@ -43,16 +43,16 @@ def tile_picked_ace8_none_po_kernel(
         def words_of(w):
             return w[0].rearrange("p n t -> p (n t)").bitcast(I32)
 
-        def load_scales(queue, tile, first, src):
+        def load_scales(queues, tile, first, src):
             for q in range(4):
-                queue.dma_start(
+                queues[q].dma_start(
                     out=tile[32 * q + first : 32 * q + first + 4, :].bitcast(I32),
                     in_=src[0, 4 * q : 4 * q + 4, :].bitcast(I32),
                 )
 
-        def fill_scales(queue, tile, src):
+        def fill_scales(queues, tile, src):
             for q in range(4):
-                queue.dma_start(
+                queues[q].dma_start(
                     out=tile[32 * q : 32 * q + 32, :].bitcast(I32),
                     in_=src[0, 4 * q : 4 * q + 4, :].bitcast(I32).unsqueeze(0).broadcast_to([8, 4, src.shape[2] // 4]),
                 )
@@ -60,7 +60,7 @@ def tile_picked_ace8_none_po_kernel(
         def deal(dst, src, t0, t1):
             nc.vector.tensor_copy(
                 out=dst[:].rearrange("p (t m) -> p t m", t=PACK)[:, t0:t1, :],
-                in_=src[:].rearrange("p (m t) -> p t m", t=PACK)[:, t0:t1, :],
+                in_=src.rearrange("p (m t) -> p t m", t=PACK)[:, t0:t1, :],
             )
 
         def deal_bytes(dst, src):
@@ -79,49 +79,48 @@ def tile_picked_ace8_none_po_kernel(
         c1_sb = sb("c1_sb", [P, PACK], F32)
         c2_sb = sb("c2_sb", [P, PACK], F32)
         ident = sb("ident", [P, P], F32)
+        warm = sb("warm", [P, 1], F32)
 
-        nc.sync.dma_start(out=xw[:], in_=words_of(x_words))
+        fill_scales([nc.sync, nc.scalar] * 2, xs, x_scales)
         nc.sync.dma_start(offs_sb[:], offs)
-        fill_scales(nc.scalar, xs, x_scales)
-        fill_scales(nc.scalar, s_raw, w1_scales)
+        nc.sync.dma_start(out=xw[:], in_=words_of(x_words))
+        fill_scales([nc.scalar] * 4, s_raw, w1_scales)
         nc.sync.dma_start(out=w_raw[0][:], in_=words_of(w1_words))
         nc.sync.dma_start(lists[0][:], p1)
-        nc.sync.dma_start(out=w_raw[1][:], in_=words_of(w2_words))
-        nc.sync.dma_start(lists[1][:], p2)
         nc.sync.dma_start(out=gates[0][:], in_=g1)
-        nc.sync.dma_start(lists[2][:], p3)
-        nc.sync.dma_start(out=w_raw[2][:], in_=words_of(w3_words))
+        nc.sync.dma_start(lists[1][:], p2)
         nc.sync.dma_start(out=gates[1][:], in_=g2)
+        nc.sync.dma_start(lists[2][:], p3)
         nc.sync.dma_start(out=gates[2][:], in_=g3)
+        nc.sync.dma_start(out=w_raw[1][:], in_=words_of(w2_words))
+        nc.sync.dma_start(out=w_raw[2][:], in_=words_of(w3_words))
+        make_identity(nc, ident[:])
+        nc.scalar.activation(warm[:], ident[:, 0:1], SQUARE)
         nc.gpsimd.dma_start(out=c1_sb[:], in_=c1.rearrange("(p t) o -> p (t o)", t=PACK))
         nc.gpsimd.dma_start(out=c2_sb[:], in_=c2.rearrange("(p t) o -> p (t o)", t=PACK))
-        make_identity(nc, ident[:])
-        warm = sb("warm", [P, 1], F32)
-        nc.scalar.activation(warm[:], ident[:, 0:1], SQUARE)
 
         xg_s = sb("xg_s", [P, S], U8)
         xg_w = sb("xg_w", [P, S], U32)
         w_dealt = [sb("w_dealt%d" % i, [P, H], I32) for i in range(3)]
         s1 = sb("s1", [P, H], U8)
-        s23 = sb("s23", [P, N], U8)
         nc.vector.tensor_copy(out=xg_s[:], in_=xs[:].indirect(offs_sb[:]))
         deal_bytes(s1, s_raw)
-        load_scales(nc.sync, s_raw, 4, w2_scales)
-        load_scales(nc.sync, s_raw, 8, w3_scales)
+        load_scales([nc.sync] * 4, s_raw, 4, w2_scales)
+        load_scales([nc.sync] * 4, s_raw, 8, w3_scales)
         half = S // 2
         nc.vector.tensor_copy(out=xg_w[:, :half], in_=xw[:].bitcast(U32).indirect(offs_sb[:, : half // 16]))
-        deal(w_dealt[0], w_raw[0], 0, 2)
+        deal(w_dealt[0], w_raw[0][:], 0, 2)
         nc.vector.tensor_copy(out=xg_w[:, half:], in_=xw[:].bitcast(U32).indirect(offs_sb[:, half // 16 :]))
-        deal(w_dealt[0], w_raw[0], 2, 4)
+        deal(w_dealt[0], w_raw[0][:], 2, 4)
 
         y = []
         for t in range(PACK):
-            y_ps = bank("y_ps%d" % t, t)
             y_t = sb("y%d" % t, [P, S], F32)
             spans = [(0, half), (half, S)] if t == 0 else [(0, S)]
             for lo, hi in spans:
+                y_ps = bank("y_ps%d_%d" % (t, lo), t if lo == 0 else 7)
                 nc.tensor.matmul_mx(
-                    out=y_ps[:, lo:hi],
+                    out=y_ps[:, : hi - lo],
                     lhsT=w_dealt[0][:, t * P : (t + 1) * P].bitcast(FP8X4),
                     lhsT_scale=s1[:, t * P : (t + 1) * P],
                     rhs=xg_w[:, lo:hi].bitcast(FP8X4),
@@ -129,11 +128,13 @@ def tile_picked_ace8_none_po_kernel(
                     start=True,
                     stop=True,
                 )
-            nc.scalar.copy(out=y_t[:], in_=y_ps[:])
+                if lo == 0:
+                    nc.scalar.copy(out=y_t[:, lo:hi], in_=y_ps[:, : hi - lo])
+                else:
+                    nc.vector.tensor_copy(out=y_t[:, lo:hi], in_=y_ps[:, : hi - lo])
             y.append(y_t)
-        deal(w_dealt[1], w_raw[1], 0, 4)
-        deal(w_dealt[2], w_raw[2], 0, 4)
-        deal_bytes(s23, s_raw)
+        deal(w_dealt[1], w_raw[1][:], 0, 4)
+        deal(w_dealt[2], w_raw[2][:], 0, 4)
 
         out_codes = sb("out_codes", [P, S], U32)
         out_scales = sb("out_scales", [P, S], U8)
@@ -142,127 +143,186 @@ def tile_picked_ace8_none_po_kernel(
 
         planes, zi, out_ps = {}, {}, {}
 
-        def gather(dst, b, t, n):
+        def gather(dst, b, t, n, blocks=1):
             nc.vector.tensor_tensor(
                 dst,
-                y[t][:].indirect(lists[n][:, b * LIST_COLS : (b + 1) * LIST_COLS]),
-                gates[n][:, b * B : (b + 1) * B],
+                y[t][:].indirect(lists[n][:, b * LIST_COLS : (b + blocks) * LIST_COLS]),
+                gates[n][:, b * B : (b + blocks) * B],
                 MULT,
             )
 
-        def front(b, u, terms):
+        def front(b, u, terms, number):
             summed = bank("summed%d%d" % (b, u), 4)
             for e in range(2):
                 for n in range(3):
-                    gather(terms[:, e, n, :], b, 2 * u + e, n)
+                    gather(terms[e][:, n, :], b, 2 * u + e, n)
                     nc.tensor.matmul(
-                        summed[:, e * P : (e + 1) * P], terms[:, e, n, :], ident[:],
+                        summed[:, e * P : (e + 1) * P], terms[e][:, n, :], ident[:],
                         start=(n == 0), stop=(n == 2), is_transpose=True,
                     )
             turned = sb("turned%d%d" % (b, u), [P, 2 * P], F32)
             nc.scalar.copy(out=turned[:], in_=summed[:, : 2 * P])
-            a_ps = bank("a_ps%d%d" % (b, u), 5 + u)
+            a_ps = bank("a_ps%d%d" % (b, u), number)
             for e in range(2):
                 nc.tensor.transpose(a_ps[:, e * B : (e + 1) * B], turned[:, e * P : (e + 1) * P], ident[:])
             return a_ps
 
-        def scale_planes(b, u, a_ps):
-            if b not in planes:
-                planes[b] = sb("planes%d" % b, [P, 2, PACK, B], BF16)
-            sq = sb("sq%d%d" % (b, u), [P, 2 * B], F32)
-            for e in range(2):
-                t = 2 * u + e
-                nc.scalar.activation(planes[b][:, 0, t, :], a_ps[:, e * B : (e + 1) * B], COPY, scale=c1_sb[:, t : t + 1])
+        def wide_front(t, terms, number):
+            summed = [bank("summed_w%d%d" % (t, h), 4 + 3 * h) for h in range(2)]
+            for n in range(3):
+                gather(terms[:, n, :], 0, t, n, 2)
+                for h in range(2):
+                    nc.tensor.matmul(
+                        summed[h][:, :P], terms[:, n, h * B : (h + 1) * B], ident[:],
+                        start=(n == 0), stop=(n == 2), is_transpose=True,
+                    )
+            turned = sb("turned_w%d" % t, [P, 2 * P], F32)
+            for h in range(2):
+                nc.scalar.copy(out=turned[:, h * P : (h + 1) * P], in_=summed[h][:, :P])
+            a_ps = bank("a_ps_w%d" % t, number)
+            for h in range(2):
+                nc.tensor.transpose(a_ps[:, h * B : (h + 1) * B], turned[:, h * P : (h + 1) * P], ident[:])
+            return a_ps
+
+        def scale_planes(u, a_ps, name, plane_of):
+            sq = sb(name, [P, 2 * B], F32)
             nc.scalar.activation(sq[:], a_ps[:, : 2 * B], SQUARE)
             for e in range(2):
                 t = 2 * u + e
-                nc.scalar.activation(planes[b][:, 1, t, :], sq[:, e * B : (e + 1) * B], COPY, scale=c2_sb[:, t : t + 1])
+                nc.scalar.activation(plane_of(0, t), a_ps[:, e * B : (e + 1) * B], COPY, scale=c1_sb[:, t : t + 1])
+            for e in range(2):
+                t = 2 * u + e
+                nc.scalar.activation(plane_of(1, t), sq[:, e * B : (e + 1) * B], COPY, scale=c2_sb[:, t : t + 1])
 
-        def second(b, on_scalar, tag):
-            zi[b] = sb("zi%d" % b, [P, 2, B, PACK], BF16, tag)
-            src = planes[b][:].rearrange("p z t j -> p z j t")
-            if on_scalar:
-                nc.scalar.copy(out=zi[b][:], in_=src)
-            else:
-                nc.vector.tensor_copy(out=zi[b][:], in_=src)
-            codes = sb("z_codes%d" % b, [P, 2 * B], U32)
-            scales = sb("z_scales%d" % b, [P, 2 * B], U8)
-            nc.vector.quantize_mx(
-                out=codes[:].bitcast(FP8X4), scales=scales[:], in_=zi[b][:].rearrange("p z j t -> p (z j t)")
+        def planes_of(b):
+            if b not in planes:
+                planes[b] = sb("planes%d" % b, [P, 2, PACK, B], BF16)
+            return lambda z, t: planes[b][:, z, t, :]
+
+        def product(dst, t, codes, scales, order):
+            for z in order:
+                nc.tensor.matmul_mx(
+                    out=dst,
+                    lhsT=w_dealt[1 + z][:, t * P : (t + 1) * P].bitcast(FP8X4),
+                    lhsT_scale=s23[4 + 4 * z : P, t * P : (t + 1) * P],
+                    rhs=codes[z].bitcast(FP8X4),
+                    rhs_scale=scales[z],
+                    start=(z == order[0]),
+                    stop=(z == order[1]),
+                )
+
+        def weave(b, z, copy, tag=None):
+            if b not in zi:
+                zi[b] = sb("zi%d" % b, [P, 2, B, PACK], BF16, tag)
+            copy(
+                out=zi[b][:, z].rearrange("p (c i) t -> p c t i", i=4),
+                in_=planes[b][:, z, :, :].rearrange("p t (c i) -> p c t i", i=4),
             )
-            out_ps[b] = bank("out_ps%d" % b, b)
-            for t in range(PACK):
-                for z in range(2):
-                    nc.tensor.matmul_mx(
-                        out=out_ps[b][:, t * B : (t + 1) * B],
-                        lhsT=w_dealt[1 + z][:, t * P : (t + 1) * P].bitcast(FP8X4),
-                        lhsT_scale=s23[4 + 4 * z : P, t * P : (t + 1) * P],
-                        rhs=codes[:, z * B : (z + 1) * B].bitcast(FP8X4),
-                        rhs_scale=scales[:, z * B : (z + 1) * B],
-                        start=(z == 0),
-                        stop=(z == 1),
-                    )
 
-        def leave(b, on_scalar):
+        def quantize(name, src, width):
+            codes = sb(name + "_codes", [P, width], U32)
+            scales = sb(name + "_scales", [P, width], U8)
+            nc.vector.quantize_mx(out=codes[:].bitcast(FP8X4), scales=scales[:], in_=src)
+            return codes, scales
+
+        def second(b, number, codes, scales):
+            out_ps[b] = bank("out_ps%d" % b, number)
+            for t in range(PACK):
+                product(out_ps[b][:, t * B : (t + 1) * B], t, codes, scales, (0, 1))
+
+        def leave(b, tag, on_scalar, tag_i=None):
             cols = slice(b * B, (b + 1) * B)
-            res = sb("res%d" % b, [P, PACK, B], F32)
-            res_i = sb("res_i%d" % b, [P, B, PACK], BF16)
+            res = sb("res%d" % b, [P, PACK, B], F32, tag)
+            res_i = sb("res_i%d" % b, [P, B, PACK], BF16, tag_i)
             nc.scalar.copy(out=res[:].rearrange("p t j -> p (t j)"), in_=out_ps[b][:])
             nc.sync.dma_start(out=out_rows[:, :, cols], in_=res[:])
             if on_scalar:
                 nc.scalar.copy(out=res_i[:], in_=out_ps[b][:].rearrange("p (t j) -> p j t", t=PACK))
             else:
-                nc.vector.tensor_copy(out=res_i[:], in_=res[:].rearrange("p t j -> p j t"))
+                nc.vector.tensor_copy(
+                    out=res_i[:].rearrange("p (c i) t -> p c t i", i=4),
+                    in_=res[:].rearrange("p t (c i) -> p c t i", i=4),
+                )
             nc.vector.quantize_mx(
                 out=out_codes[:, cols].bitcast(FP8X4), scales=out_scales[:, cols],
                 in_=res_i[:].rearrange("p j t -> p (j t)"),
             )
-            nc.sync.dma_start(out=out_words[:, cols], in_=out_codes[:, cols].bitcast(I32))
 
-        def terms_tile(name, units, tag=None):
-            return sb(name, [P, units, 2, 3, B], F32, tag)
+        wide = sb("wide", [P, 2, PACK, 2 * B], BF16)
+        planes[0], planes[1] = wide[:, :, :, :B], wide[:, :, :, B:]
+        early = sb("early", [P, PACK, 3, 2 * B], F32)
+        for t in range(PACK):
+            a = wide_front(t, early[:, t], 5 + t % 2)
+            sq = sb("sq_w%d" % t, [P, 2 * B], F32)
+            nc.scalar.activation(sq[:], a[:, : 2 * B], SQUARE)
+            nc.scalar.activation(wide[:, 0, t, :], a[:, : 2 * B], COPY, scale=c1_sb[:, t : t + 1])
+            nc.scalar.activation(wide[:, 1, t, :], sq[:], COPY, scale=c2_sb[:, t : t + 1])
+        first = sb("first", [P, 5, 3, B], F32)
+        a = front(2, 0, (first[:, 0], first[:, 1]), 5)
+        weave(0, 0, nc.scalar.copy, "tie0")
+        weave(0, 1, nc.scalar.copy)
+        scale_planes(0, a, "sq20", planes_of(2))
+        a = front(2, 1, (first[:, 2], first[:, 3]), 6)
+        weave(1, 0, nc.scalar.copy, "tie1")
+        scale_planes(1, a, "sq21", planes_of(2))
+        codes, scales = quantize("q0", zi[0][:].rearrange("p z j t -> p (z j t)"), 2 * B)
+        s23 = sb("s23", [P, N], U8, "sq_w3")
+        deal_bytes(s23, s_raw)
+        second(0, 6, (codes[:, :B], codes[:, B:]), (scales[:, :B], scales[:, B:]))
+        late = sb("late", [P, 3, B], F32, "tie0")
+        a = front(3, 0, (first[:, 4], late[:]), 0)
+        weave(1, 1, nc.vector.tensor_copy)
+        codes, scales = quantize("q1", zi[1][:].rearrange("p z j t -> p (z j t)"), 2 * B)
+        second(1, 4, (codes[:, :B], codes[:, B:]), (scales[:, :B], scales[:, B:]))
+        weave(2, 0, nc.scalar.copy, "tie2")
+        weave(2, 1, nc.vector.tensor_copy)
+        codes, scales = quantize("q2", zi[2][:].rearrange("p z j t -> p (z j t)"), 2 * B)
+        second(2, 1, (codes[:, :B], codes[:, B:]), (scales[:, :B], scales[:, B:]))
+        z_last = [sb("z_last%d" % z, [P, B, PACK], BF16) for z in range(2)]
+        scale_planes(0, a, "sq30", lambda z, t: z_last[z][:, :, t])
 
-        early = terms_tile("early", 5)
-        a = front(0, 0, early[:, 0])
-        scale_planes(0, 0, a)
-        a = front(0, 1, early[:, 1])
-        scale_planes(0, 1, a)
-        a = front(1, 0, early[:, 2])
-        second(0, True, "tie0")
-        scale_planes(1, 0, a)
-        a = front(1, 1, early[:, 3])
-        scale_planes(1, 1, a)
-        a = front(2, 0, early[:, 4])
-        second(1, True, "tie1")
-        scale_planes(2, 0, a)
-        middle = terms_tile("middle", 2, "tie0")
-        a = front(2, 1, middle[:, 0])
-        leave(0, True)
-        scale_planes(2, 1, a)
-        a = front(3, 0, middle[:, 1])
-        scale_planes(3, 0, a)
-
-        last = sb("last", [P, 3, 2, B], F32, "tie1")
-        part = sb("part", [P, 2, B], F32)
+        leave(0, None, False)
+        five = sb("five", [P, 5, B], F32, "tie1")
+        sixth = sb("sixth", [P, B], F32, "tie2")
+        part = sb("part", [P, 2, B], F32, "a_part")
         a_sb = sb("a_sb", [P, 2, B], F32)
         for n in range(2):
             for e in range(2):
-                gather(last[:, n, e, :], 3, 2 + e, n)
-        gather(last[:, 2, 0, :], 3, 2, 2)
-        nc.vector.tensor_tensor(part[:], last[:, 0], last[:, 1], ADD)
-        gather(last[:, 2, 1, :], 3, 3, 2)
-        nc.vector.tensor_tensor(a_sb[:], part[:], last[:, 2], ADD)
-        second(2, False, None)
-        for e in range(2):
+                gather(five[:, 2 * n + e, :], 3, 2 + e, n)
+        gather(five[:, 4, :], 3, 2, 2)
+        nc.vector.tensor_tensor(part[:], five[:, 0:2], five[:, 2:4], ADD)
+        gather(sixth[:], 3, 3, 2)
+        for e, term in enumerate((five[:, 4, :], sixth[:])):
             t = 2 + e
-            nc.vector.tensor_scalar(planes[3][:, 0, t, :], a_sb[:, e, :], c1_sb[:, t : t + 1], None, MULT)
+            nc.vector.tensor_tensor(a_sb[:, e, :], part[:, e, :], term, ADD)
+            nc.scalar.activation(z_last[0][:, :, t], a_sb[:, e, :], COPY, scale=c1_sb[:, t : t + 1])
             nc.vector.scalar_tensor_tensor(
-                planes[3][:, 1, t, :], a_sb[:, e, :], c2_sb[:, t : t + 1], a_sb[:, e, :], MULT, MULT
+                z_last[1][:, :, t], a_sb[:, e, :], c2_sb[:, t : t + 1], a_sb[:, e, :], MULT, MULT
             )
-        second(3, False, None)
-        leave(1, False)
-        leave(2, False)
-        leave(3, False)
+        q_z = quantize("q3z", z_last[1][:].rearrange("p j t -> p (j t)"), B)
+        q_z2 = quantize("q3z2", z_last[0][:].rearrange("p j t -> p (j t)"), B)
+        codes, scales = (q_z2[0][:], q_z[0][:]), (q_z2[1][:], q_z[1][:])
+        leave(1, "a_part", False)
+        leave(2, "a_sb", True)
+        nc.sync.dma_start(out=out_words[:, : 3 * B], in_=out_codes[:, : 3 * B].bitcast(I32))
+        cols = slice(3 * B, 4 * B)
+        res_i = sb("res_i3", [P, B, PACK], BF16)
+        for u in range(2):
+            pair_ps = bank("pair_ps%d" % u, 2 + u)
+            for e in range(2):
+                product(pair_ps[:, e * B : (e + 1) * B], 2 * u + e, codes, scales, (1, 0))
+            pair = sb("res3%d" % u, [P, 2, B], F32)
+            nc.vector.tensor_copy(
+                out=res_i[:, :, 2 * u : 2 * u + 2],
+                in_=pair_ps[:, : 2 * B].rearrange("p (e j) -> p j e", e=2),
+            )
+            nc.scalar.copy(out=pair[:].rearrange("p e j -> p (e j)"), in_=pair_ps[:, : 2 * B])
+            nc.scalar.dma_start(out=out_rows[:, 2 * u : 2 * u + 2, cols], in_=pair[:])
+        nc.vector.quantize_mx(
+            out=out_codes[:, cols].bitcast(FP8X4), scales=out_scales[:, cols],
+            in_=res_i[:].rearrange("p j t -> p (j t)"),
+        )
+        nc.sync.dma_start(out=out_words[:, cols], in_=out_codes[:, cols].bitcast(I32))
         for q in range(4):
             queue = nc.sync if q % 2 == 0 else nc.scalar
             queue.dma_start(

@@ -22,7 +22,8 @@ P = 128
 PACK = 4
 B = 128
 BLOCKS = S // B
-LIST_COLS = B // 16
+HALF = S // 2
+TERMS = 3
 
 
 def tile_picked_ace8_none_po_kernel(
@@ -59,8 +60,8 @@ def tile_picked_ace8_none_po_kernel(
 
         def deal(dst, src, t0, t1):
             nc.vector.tensor_copy(
-                out=dst[:].rearrange("p (t m) -> p t m", t=PACK)[:, t0:t1, :],
-                in_=src.rearrange("p (m t) -> p t m", t=PACK)[:, t0:t1, :],
+                out=dst[:].rearrange("p (t c i) -> p c t i", t=PACK, i=4)[:, :, t0:t1, :],
+                in_=src[:].rearrange("p (c i t) -> p c t i", t=PACK, i=4)[:, :, t0:t1, :],
             )
 
         def deal_bytes(dst, src):
@@ -70,32 +71,34 @@ def tile_picked_ace8_none_po_kernel(
             )
 
         offs_sb = sb("offs_sb", [P, S // 16], U16)
-        lists = [sb("list%d" % n, [P, S // 16], U16) for n in range(3)]
+        lists = [sb("list%d" % n, [P, S // 16], U16) for n in range(TERMS)]
         xw = sb("xw", [P, T], I32)
         xs = sb("xs", [P, T], U8)
         w_raw = [sb("w_raw%d" % i, [P, H], I32) for i in range(3)]
         s_raw = sb("s_raw", [P, H], U8)
-        gates = [sb("gate%d" % n, [P, S], F32) for n in range(3)]
+        gates = [sb("gate%d" % n, [P, S], F32) for n in range(TERMS)]
+        gate_cols = [sb("gate_col%d" % n, [P, BLOCKS], F32) for n in range(TERMS)]
         c1_sb = sb("c1_sb", [P, PACK], F32)
         c2_sb = sb("c2_sb", [P, PACK], F32)
+        eye = sb("eye", [P, P], F32)
         ident = sb("ident", [P, P], F32)
-        warm = sb("warm", [P, 1], F32)
 
         fill_scales([nc.sync, nc.scalar] * 2, xs, x_scales)
         nc.sync.dma_start(offs_sb[:], offs)
         nc.sync.dma_start(out=xw[:], in_=words_of(x_words))
-        fill_scales([nc.scalar] * 4, s_raw, w1_scales)
+        fill_scales([nc.scalar, nc.scalar, nc.gpsimd, nc.gpsimd], s_raw, w1_scales)
         nc.sync.dma_start(out=w_raw[0][:], in_=words_of(w1_words))
-        nc.sync.dma_start(lists[0][:], p1)
-        nc.sync.dma_start(out=gates[0][:], in_=g1)
-        nc.sync.dma_start(lists[1][:], p2)
-        nc.sync.dma_start(out=gates[1][:], in_=g2)
-        nc.sync.dma_start(lists[2][:], p3)
-        nc.sync.dma_start(out=gates[2][:], in_=g3)
+        for n, (p, g) in enumerate(((p1, g1), (p2, g2), (p3, g3))):
+            nc.sync.dma_start(lists[n][:], p)
+            nc.sync.dma_start(out=gates[n][:], in_=g)
         nc.sync.dma_start(out=w_raw[1][:], in_=words_of(w2_words))
         nc.sync.dma_start(out=w_raw[2][:], in_=words_of(w3_words))
-        make_identity(nc, ident[:])
-        nc.scalar.activation(warm[:], ident[:, 0:1], SQUARE)
+        make_identity(nc, eye[:])
+        nc.scalar.activation(ident[:], eye[:], SQUARE)
+        for n, g in enumerate((g1, g2, g3)):
+            nc.gpsimd.dma_start(
+                out=gate_cols[n][:], in_=g[0, :].rearrange("(b p) -> p b", p=P), allow_slow_non_contiguous=True
+            )
         nc.gpsimd.dma_start(out=c1_sb[:], in_=c1.rearrange("(p t) o -> p (t o)", t=PACK))
         nc.gpsimd.dma_start(out=c2_sb[:], in_=c2.rearrange("(p t) o -> p (t o)", t=PACK))
 
@@ -107,18 +110,17 @@ def tile_picked_ace8_none_po_kernel(
         deal_bytes(s1, s_raw)
         load_scales([nc.sync] * 4, s_raw, 4, w2_scales)
         load_scales([nc.sync] * 4, s_raw, 8, w3_scales)
-        half = S // 2
-        nc.vector.tensor_copy(out=xg_w[:, :half], in_=xw[:].bitcast(U32).indirect(offs_sb[:, : half // 16]))
-        deal(w_dealt[0], w_raw[0][:], 0, 2)
-        nc.vector.tensor_copy(out=xg_w[:, half:], in_=xw[:].bitcast(U32).indirect(offs_sb[:, half // 16 :]))
-        deal(w_dealt[0], w_raw[0][:], 2, 4)
+        nc.vector.tensor_copy(out=xg_w[:, :HALF], in_=xw[:].bitcast(U32).indirect(offs_sb[:, : HALF // 16]))
+        deal(w_dealt[0], w_raw[0], 0, 2)
+        nc.vector.tensor_copy(out=xg_w[:, HALF:], in_=xw[:].bitcast(U32).indirect(offs_sb[:, HALF // 16 :]))
+        deal(w_dealt[0], w_raw[0], 2, 4)
 
         y = []
         for t in range(PACK):
             y_t = sb("y%d" % t, [P, S], F32)
-            spans = [(0, half), (half, S)] if t == 0 else [(0, S)]
+            spans = [(0, HALF), (HALF, S)] if t == 0 else [(0, S)]
             for lo, hi in spans:
-                y_ps = bank("y_ps%d_%d" % (t, lo), t if lo == 0 else 7)
+                y_ps = bank("y_ps%d_%d" % (t, lo), t if lo == 0 else 4)
                 nc.tensor.matmul_mx(
                     out=y_ps[:, : hi - lo],
                     lhsT=w_dealt[0][:, t * P : (t + 1) * P].bitcast(FP8X4),
@@ -133,196 +135,151 @@ def tile_picked_ace8_none_po_kernel(
                 else:
                     nc.vector.tensor_copy(out=y_t[:, lo:hi], in_=y_ps[:, : hi - lo])
             y.append(y_t)
-        deal(w_dealt[1], w_raw[1][:], 0, 4)
-        deal(w_dealt[2], w_raw[2][:], 0, 4)
 
         out_codes = sb("out_codes", [P, S], U32)
         out_scales = sb("out_scales", [P, S], U8)
         out_rows = out_0.rearrange("(p t) j -> p t j", t=PACK)
         out_words = words_of(out_1)
+        s23 = sb("s23", [P, N], U8)
 
-        planes, zi, out_ps = {}, {}, {}
+        a_ps = [None] * BLOCKS
 
-        def gather(dst, b, t, n, blocks=1):
-            nc.vector.tensor_tensor(
-                dst,
-                y[t][:].indirect(lists[n][:, b * LIST_COLS : (b + blocks) * LIST_COLS]),
-                gates[n][:, b * B : (b + blocks) * B],
-                MULT,
-            )
+        def sums_of(b):
+            if a_ps[b] is None:
+                a_ps[b] = bank("a_ps%d" % b, 4 + b)
+            return a_ps[b]
 
-        def front(b, u, terms, number):
-            summed = bank("summed%d%d" % (b, u), 4)
-            for e in range(2):
-                for n in range(3):
-                    gather(terms[e][:, n, :], b, 2 * u + e, n)
+        def picks(t, n, b, blocks):
+            return y[t][:].indirect(lists[n][:, b * B // 16 : (b + blocks) * B // 16])
+
+        def gated_unit(t, b, blocks, number):
+            terms = sb("terms%d%d" % (t, b), [P, TERMS, blocks * B], F32)
+            summed = bank("summed%d%d" % (t, b), number)
+            for n in range(TERMS):
+                nc.vector.tensor_tensor(
+                    terms[:, n, :], picks(t, n, b, blocks), gates[n][:, b * B : (b + blocks) * B], MULT
+                )
+                for h in range(blocks):
                     nc.tensor.matmul(
-                        summed[:, e * P : (e + 1) * P], terms[e][:, n, :], ident[:],
-                        start=(n == 0), stop=(n == 2), is_transpose=True,
+                        summed[:, h * P : (h + 1) * P], terms[:, n, h * B : (h + 1) * B], ident[:],
+                        start=(n == 0 and h == 0), stop=(n == TERMS - 1 and h == blocks - 1), is_transpose=True,
                     )
-            turned = sb("turned%d%d" % (b, u), [P, 2 * P], F32)
-            nc.scalar.copy(out=turned[:], in_=summed[:, : 2 * P])
-            a_ps = bank("a_ps%d%d" % (b, u), number)
-            for e in range(2):
-                nc.tensor.transpose(a_ps[:, e * B : (e + 1) * B], turned[:, e * P : (e + 1) * P], ident[:])
-            return a_ps
-
-        def wide_front(t, terms, number):
-            summed = [bank("summed_w%d%d" % (t, h), 4 + 3 * h) for h in range(2)]
-            for n in range(3):
-                gather(terms[:, n, :], 0, t, n, 2)
-                for h in range(2):
-                    nc.tensor.matmul(
-                        summed[h][:, :P], terms[:, n, h * B : (h + 1) * B], ident[:],
-                        start=(n == 0), stop=(n == 2), is_transpose=True,
-                    )
-            turned = sb("turned_w%d" % t, [P, 2 * P], F32)
-            for h in range(2):
-                nc.scalar.copy(out=turned[:, h * P : (h + 1) * P], in_=summed[h][:, :P])
-            a_ps = bank("a_ps_w%d" % t, number)
-            for h in range(2):
-                nc.tensor.transpose(a_ps[:, h * B : (h + 1) * B], turned[:, h * P : (h + 1) * P], ident[:])
-            return a_ps
-
-        def scale_planes(u, a_ps, name, plane_of):
-            sq = sb(name, [P, 2 * B], F32)
-            nc.scalar.activation(sq[:], a_ps[:, : 2 * B], SQUARE)
-            for e in range(2):
-                t = 2 * u + e
-                nc.scalar.activation(plane_of(0, t), a_ps[:, e * B : (e + 1) * B], COPY, scale=c1_sb[:, t : t + 1])
-            for e in range(2):
-                t = 2 * u + e
-                nc.scalar.activation(plane_of(1, t), sq[:, e * B : (e + 1) * B], COPY, scale=c2_sb[:, t : t + 1])
-
-        def planes_of(b):
-            if b not in planes:
-                planes[b] = sb("planes%d" % b, [P, 2, PACK, B], BF16)
-            return lambda z, t: planes[b][:, z, t, :]
-
-        def product(dst, t, codes, scales, order):
-            for z in order:
-                nc.tensor.matmul_mx(
-                    out=dst,
-                    lhsT=w_dealt[1 + z][:, t * P : (t + 1) * P].bitcast(FP8X4),
-                    lhsT_scale=s23[4 + 4 * z : P, t * P : (t + 1) * P],
-                    rhs=codes[z].bitcast(FP8X4),
-                    rhs_scale=scales[z],
-                    start=(z == order[0]),
-                    stop=(z == order[1]),
+            turned = sb("turned%d%d" % (t, b), [P, blocks * P], F32)
+            nc.scalar.copy(out=turned[:], in_=summed[:, : blocks * P])
+            for h in range(blocks):
+                nc.tensor.transpose(
+                    sums_of(b + h)[:, t * B : (t + 1) * B], turned[:, h * P : (h + 1) * P], ident[:]
                 )
 
-        def weave(b, z, copy, tag=None):
-            if b not in zi:
-                zi[b] = sb("zi%d" % b, [P, 2, B, PACK], BF16, tag)
-            copy(
-                out=zi[b][:, z].rearrange("p (c i) t -> p c t i", i=4),
-                in_=planes[b][:, z, :, :].rearrange("p t (c i) -> p c t i", i=4),
-            )
+        def plain_gathers(t, b, blocks, numbers):
+            terms = sb("terms%d%d" % (t, b), [P, TERMS, blocks * B], F32)
+            apart = [bank("apart%d%d%d" % (t, b, h), numbers[h]) for h in range(blocks)]
+            for n in range(TERMS):
+                nc.scalar.activation(terms[:, n, :], picks(t, n, b, blocks), COPY)
+                for h in range(blocks):
+                    nc.tensor.transpose(apart[h][:, n * P : (n + 1) * P], terms[:, n, h * B : (h + 1) * B], ident[:])
+            return apart
 
-        def quantize(name, src, width):
-            codes = sb(name + "_codes", [P, width], U32)
-            scales = sb(name + "_scales", [P, width], U8)
-            nc.vector.quantize_mx(out=codes[:].bitcast(FP8X4), scales=scales[:], in_=src)
-            return codes, scales
+        def plain_sums(t, b, apart):
+            for h in range(len(apart)):
+                turned = sb("turned%d%d%d" % (t, b, h), [P, TERMS, P], F32)
+                for n in range(TERMS):
+                    nc.scalar.activation(
+                        turned[:, n, :], apart[h][:, n * P : (n + 1) * P], COPY,
+                        scale=gate_cols[n][:, b + h : b + h + 1],
+                    )
+                for n in range(TERMS):
+                    nc.tensor.matmul(
+                        sums_of(b + h)[:, t * B : (t + 1) * B], turned[:, n, :], ident[:],
+                        start=(n == 0), stop=(n == TERMS - 1), is_transpose=True,
+                    )
 
-        def second(b, number, codes, scales):
-            out_ps[b] = bank("out_ps%d" % b, number)
-            for t in range(PACK):
-                product(out_ps[b][:, t * B : (t + 1) * B], t, codes, scales, (0, 1))
+        def plain_unit(t, b, blocks, numbers):
+            plain_sums(t, b, plain_gathers(t, b, blocks, numbers))
 
-        def leave(b, tag, on_scalar, tag_i=None):
+        def added_unit(t, b, a_sb):
+            terms = sb("terms%d%d" % (t, b), [P, TERMS + 1, B], F32)
+            for n in range(TERMS):
+                nc.vector.tensor_tensor(terms[:, n, :], picks(t, n, b, 1), gates[n][:, b * B : (b + 1) * B], MULT)
+            nc.vector.tensor_tensor(terms[:, TERMS, :], terms[:, 0, :], terms[:, 1, :], ADD)
+            nc.vector.tensor_tensor(a_sb[:, t, :], terms[:, TERMS, :], terms[:, 2, :], ADD)
+
+        def orders_from_bank(b):
+            a = a_ps[b][:].rearrange("p (t j) -> p j t", t=PACK)
+            sq = sb("sq%d" % b, [P, B, PACK], F32)
+            zi = sb("zi%d" % b, [P, 2, B, PACK], BF16)
+            nc.scalar.activation(sq[:], a, SQUARE)
+            nc.vector.tensor_tensor(zi[:, 0], a, c1_sb[:].unsqueeze(1).broadcast_to([P, B, PACK]), MULT)
+            nc.vector.tensor_tensor(zi[:, 1], sq[:], c2_sb[:].unsqueeze(1).broadcast_to([P, B, PACK]), MULT)
+            return zi
+
+        def orders_from_planes(b, a_sb):
+            sq = sb("sq%d" % b, [P, PACK, B], F32)
+            zi = sb("zi%d" % b, [P, 2, B, PACK], BF16)
+            nc.scalar.activation(sq[:], a_sb[:], SQUARE)
+            for z, (src, c) in enumerate(((a_sb, c1_sb), (sq, c2_sb))):
+                nc.vector.tensor_tensor(
+                    zi[:, z].rearrange("p (c i) t -> p c t i", i=4),
+                    src[:].rearrange("p t (c i) -> p c t i", i=4),
+                    c[:].unsqueeze(1).unsqueeze(3).broadcast_to([P, B // 4, PACK, 4]),
+                    MULT,
+                )
+            return zi
+
+        def finish(b, zi):
             cols = slice(b * B, (b + 1) * B)
-            res = sb("res%d" % b, [P, PACK, B], F32, tag)
-            res_i = sb("res_i%d" % b, [P, B, PACK], BF16, tag_i)
-            nc.scalar.copy(out=res[:].rearrange("p t j -> p (t j)"), in_=out_ps[b][:])
+            codes = sb("codes%d" % b, [P, 2 * B], U32)
+            scales = sb("scales%d" % b, [P, 2 * B], U8)
+            nc.vector.quantize_mx(
+                out=codes[:].bitcast(FP8X4), scales=scales[:], in_=zi[:].rearrange("p z j t -> p (z j t)")
+            )
+            out_ps = bank("out_ps%d" % b, 4 + b)
+            for t in range(PACK):
+                for z in range(2):
+                    nc.tensor.matmul_mx(
+                        out=out_ps[:, t * B : (t + 1) * B],
+                        lhsT=w_dealt[1 + z][:, t * P : (t + 1) * P].bitcast(FP8X4),
+                        lhsT_scale=s23[4 + 4 * z : P, t * P : (t + 1) * P],
+                        rhs=codes[:, z * B : (z + 1) * B].bitcast(FP8X4),
+                        rhs_scale=scales[:, z * B : (z + 1) * B],
+                        start=(z == 0),
+                        stop=(z == 1),
+                    )
+            res = sb("res%d" % b, [P, PACK, B], F32)
+            res_i = sb("res_i%d" % b, [P, B, PACK], BF16)
+            nc.scalar.copy(out=res[:].rearrange("p t j -> p (t j)"), in_=out_ps[:])
             nc.sync.dma_start(out=out_rows[:, :, cols], in_=res[:])
-            if on_scalar:
-                nc.scalar.copy(out=res_i[:], in_=out_ps[b][:].rearrange("p (t j) -> p j t", t=PACK))
-            else:
-                nc.vector.tensor_copy(
-                    out=res_i[:].rearrange("p (c i) t -> p c t i", i=4),
-                    in_=res[:].rearrange("p t (c i) -> p c t i", i=4),
-                )
+            nc.vector.tensor_copy(
+                out=res_i[:].rearrange("p (c i) t -> p c t i", i=4),
+                in_=res[:].rearrange("p t (c i) -> p c t i", i=4),
+            )
             nc.vector.quantize_mx(
                 out=out_codes[:, cols].bitcast(FP8X4), scales=out_scales[:, cols],
                 in_=res_i[:].rearrange("p j t -> p (j t)"),
             )
 
-        wide = sb("wide", [P, 2, PACK, 2 * B], BF16)
-        planes[0], planes[1] = wide[:, :, :, :B], wide[:, :, :, B:]
-        early = sb("early", [P, PACK, 3, 2 * B], F32)
-        for t in range(PACK):
-            a = wide_front(t, early[:, t], 5 + t % 2)
-            sq = sb("sq_w%d" % t, [P, 2 * B], F32)
-            nc.scalar.activation(sq[:], a[:, : 2 * B], SQUARE)
-            nc.scalar.activation(wide[:, 0, t, :], a[:, : 2 * B], COPY, scale=c1_sb[:, t : t + 1])
-            nc.scalar.activation(wide[:, 1, t, :], sq[:], COPY, scale=c2_sb[:, t : t + 1])
-        first = sb("first", [P, 5, 3, B], F32)
-        a = front(2, 0, (first[:, 0], first[:, 1]), 5)
-        weave(0, 0, nc.scalar.copy, "tie0")
-        weave(0, 1, nc.scalar.copy)
-        scale_planes(0, a, "sq20", planes_of(2))
-        a = front(2, 1, (first[:, 2], first[:, 3]), 6)
-        weave(1, 0, nc.scalar.copy, "tie1")
-        scale_planes(1, a, "sq21", planes_of(2))
-        codes, scales = quantize("q0", zi[0][:].rearrange("p z j t -> p (z j t)"), 2 * B)
-        s23 = sb("s23", [P, N], U8, "sq_w3")
+        a_last = sb("a_last", [P, PACK, B], F32)
+        gated_unit(0, 0, 2, 0)
+        plain_unit(1, 0, 2, (1, 3))
+        gated_unit(2, 0, 2, 2)
+        gated_unit(3, 0, 2, 0)
+        plain_unit(1, 2, 1, (1,))
+        plain_unit(0, 2, 1, (3,))
+        deal(w_dealt[1], w_raw[1], 0, 4)
+        deal(w_dealt[2], w_raw[2], 0, 4)
         deal_bytes(s23, s_raw)
-        second(0, 6, (codes[:, :B], codes[:, B:]), (scales[:, :B], scales[:, B:]))
-        late = sb("late", [P, 3, B], F32, "tie0")
-        a = front(3, 0, (first[:, 4], late[:]), 0)
-        weave(1, 1, nc.vector.tensor_copy)
-        codes, scales = quantize("q1", zi[1][:].rearrange("p z j t -> p (z j t)"), 2 * B)
-        second(1, 4, (codes[:, :B], codes[:, B:]), (scales[:, :B], scales[:, B:]))
-        weave(2, 0, nc.scalar.copy, "tie2")
-        weave(2, 1, nc.vector.tensor_copy)
-        codes, scales = quantize("q2", zi[2][:].rearrange("p z j t -> p (z j t)"), 2 * B)
-        second(2, 1, (codes[:, :B], codes[:, B:]), (scales[:, :B], scales[:, B:]))
-        z_last = [sb("z_last%d" % z, [P, B, PACK], BF16) for z in range(2)]
-        scale_planes(0, a, "sq30", lambda z, t: z_last[z][:, :, t])
-
-        leave(0, None, False)
-        five = sb("five", [P, 5, B], F32, "tie1")
-        sixth = sb("sixth", [P, B], F32, "tie2")
-        part = sb("part", [P, 2, B], F32, "a_part")
-        a_sb = sb("a_sb", [P, 2, B], F32)
-        for n in range(2):
-            for e in range(2):
-                gather(five[:, 2 * n + e, :], 3, 2 + e, n)
-        gather(five[:, 4, :], 3, 2, 2)
-        nc.vector.tensor_tensor(part[:], five[:, 0:2], five[:, 2:4], ADD)
-        gather(sixth[:], 3, 3, 2)
-        for e, term in enumerate((five[:, 4, :], sixth[:])):
-            t = 2 + e
-            nc.vector.tensor_tensor(a_sb[:, e, :], part[:, e, :], term, ADD)
-            nc.scalar.activation(z_last[0][:, :, t], a_sb[:, e, :], COPY, scale=c1_sb[:, t : t + 1])
-            nc.vector.scalar_tensor_tensor(
-                z_last[1][:, :, t], a_sb[:, e, :], c2_sb[:, t : t + 1], a_sb[:, e, :], MULT, MULT
-            )
-        q_z = quantize("q3z", z_last[1][:].rearrange("p j t -> p (j t)"), B)
-        q_z2 = quantize("q3z2", z_last[0][:].rearrange("p j t -> p (j t)"), B)
-        codes, scales = (q_z2[0][:], q_z[0][:]), (q_z2[1][:], q_z[1][:])
-        leave(1, "a_part", False)
-        leave(2, "a_sb", True)
+        added_unit(0, 3, a_last)
+        finish(0, orders_from_bank(0))
+        plain_unit(2, 2, 1, (2,))
+        added_unit(1, 3, a_last)
+        finish(1, orders_from_bank(1))
+        plain_unit(3, 2, 1, (0,))
+        added_unit(2, 3, a_last)
+        added_unit(3, 3, a_last)
+        finish(2, orders_from_bank(2))
         nc.sync.dma_start(out=out_words[:, : 3 * B], in_=out_codes[:, : 3 * B].bitcast(I32))
-        cols = slice(3 * B, 4 * B)
-        res_i = sb("res_i3", [P, B, PACK], BF16)
-        for u in range(2):
-            pair_ps = bank("pair_ps%d" % u, 2 + u)
-            for e in range(2):
-                product(pair_ps[:, e * B : (e + 1) * B], 2 * u + e, codes, scales, (1, 0))
-            pair = sb("res3%d" % u, [P, 2, B], F32)
-            nc.vector.tensor_copy(
-                out=res_i[:, :, 2 * u : 2 * u + 2],
-                in_=pair_ps[:, : 2 * B].rearrange("p (e j) -> p j e", e=2),
-            )
-            nc.scalar.copy(out=pair[:].rearrange("p e j -> p (e j)"), in_=pair_ps[:, : 2 * B])
-            nc.scalar.dma_start(out=out_rows[:, 2 * u : 2 * u + 2, cols], in_=pair[:])
-        nc.vector.quantize_mx(
-            out=out_codes[:, cols].bitcast(FP8X4), scales=out_scales[:, cols],
-            in_=res_i[:].rearrange("p j t -> p (j t)"),
-        )
-        nc.sync.dma_start(out=out_words[:, cols], in_=out_codes[:, cols].bitcast(I32))
+        finish(3, orders_from_planes(3, a_last))
+        nc.sync.dma_start(out=out_words[:, 3 * B :], in_=out_codes[:, 3 * B :].bitcast(I32))
         for q in range(4):
             queue = nc.sync if q % 2 == 0 else nc.scalar
             queue.dma_start(

@@ -51,23 +51,16 @@ def tile_picked_ace8_none_po_kernel(
                     in_=src[0, 4 * q : 4 * q + 4, :].bitcast(I32),
                 )
 
-        def fill_scales(queues, tile, src):
-            for q in range(4):
-                queues[q].dma_start(
-                    out=tile[32 * q : 32 * q + 32, :].bitcast(I32),
-                    in_=src[0, 4 * q : 4 * q + 4, :].bitcast(I32).unsqueeze(0).broadcast_to([8, 4, src.shape[2] // 4]),
-                )
-
         def deal(dst, src, t0, t1):
             nc.vector.tensor_copy(
                 out=dst[:].rearrange("p (t c i) -> p c t i", t=PACK, i=4)[:, :, t0:t1, :],
                 in_=src[:].rearrange("p (c i t) -> p c t i", t=PACK, i=4)[:, :, t0:t1, :],
             )
 
-        def deal_bytes(dst, src):
+        def deal_bytes(dst, src, t0, t1):
             nc.vector.tensor_copy(
-                out=dst[:].rearrange("p (t m) -> p m t", t=PACK),
-                in_=src[:].rearrange("p (m t) -> p m t", t=PACK),
+                out=dst[:].rearrange("p (t m) -> p m t", t=PACK)[:, :, t0:t1],
+                in_=src[:].rearrange("p (m t) -> p m t", t=PACK)[:, :, t0:t1],
             )
 
         offs_sb = sb("offs_sb", [P, S // 16], U16)
@@ -76,44 +69,48 @@ def tile_picked_ace8_none_po_kernel(
         xs = sb("xs", [P, T], U8)
         w_raw = [sb("w_raw%d" % i, [P, H], I32) for i in range(3)]
         s_raw = sb("s_raw", [P, H], U8)
-        gates = [sb("gate%d" % n, [P, S], F32) for n in range(TERMS)]
-        gate_cols = [sb("gate_col%d" % n, [P, BLOCKS], F32) for n in range(TERMS)]
+        gates = [sb("gate%d" % n, [P, S - B], F32) for n in range(TERMS)]
+        gate_cols = [sb("gate_col%d" % n, [P, BLOCKS - 1], F32) for n in range(TERMS)]
         c1_sb = sb("c1_sb", [P, PACK], F32)
         c2_sb = sb("c2_sb", [P, PACK], F32)
         eye = sb("eye", [P, P], F32)
         ident = sb("ident", [P, P], F32)
 
-        fill_scales([nc.sync, nc.scalar] * 2, xs, x_scales)
+        nc.vector.memset(xs[:].bitcast(I32), 0)
+        nc.vector.memset(s_raw[:].bitcast(I32), 0)
         nc.sync.dma_start(offs_sb[:], offs)
         nc.sync.dma_start(out=xw[:], in_=words_of(x_words))
-        fill_scales([nc.scalar, nc.scalar, nc.gpsimd, nc.gpsimd], s_raw, w1_scales)
+        load_scales([nc.sync] * 4, xs, 0, x_scales)
         nc.sync.dma_start(out=w_raw[0][:], in_=words_of(w1_words))
+        load_scales([nc.sync] * 4, s_raw, 0, w1_scales)
         for n, (p, g) in enumerate(((p1, g1), (p2, g2), (p3, g3))):
             nc.sync.dma_start(lists[n][:], p)
-            nc.sync.dma_start(out=gates[n][:], in_=g)
+            nc.sync.dma_start(out=gates[n][:], in_=g[:, B:])
         nc.sync.dma_start(out=w_raw[1][:], in_=words_of(w2_words))
         nc.sync.dma_start(out=w_raw[2][:], in_=words_of(w3_words))
-        make_identity(nc, eye[:])
-        nc.scalar.activation(ident[:], eye[:], SQUARE)
         for n, g in enumerate((g1, g2, g3)):
-            nc.gpsimd.dma_start(
-                out=gate_cols[n][:], in_=g[0, :].rearrange("(b p) -> p b", p=P), allow_slow_non_contiguous=True
+            nc.sync.dma_start(
+                out=gate_cols[n][:], in_=g[0, : S - B].rearrange("(b p) -> p b", p=P), allow_slow_non_contiguous=True
             )
         nc.gpsimd.dma_start(out=c1_sb[:], in_=c1.rearrange("(p t) o -> p (t o)", t=PACK))
         nc.gpsimd.dma_start(out=c2_sb[:], in_=c2.rearrange("(p t) o -> p (t o)", t=PACK))
+        make_identity(nc, eye[:])
+        nc.scalar.activation(ident[:], eye[:], SQUARE)
 
         xg_s = sb("xg_s", [P, S], U8)
         xg_w = sb("xg_w", [P, S], U32)
         w_dealt = [sb("w_dealt%d" % i, [P, H], I32) for i in range(3)]
         s1 = sb("s1", [P, H], U8)
-        nc.vector.tensor_copy(out=xg_s[:], in_=xs[:].indirect(offs_sb[:]))
-        deal_bytes(s1, s_raw)
+        nc.vector.tensor_copy(out=xg_w[:, :HALF], in_=xw[:].bitcast(U32).indirect(offs_sb[:, : HALF // 16]))
+        nc.vector.tensor_copy(out=xg_s[:, :HALF], in_=xs[:].indirect(offs_sb[:, : HALF // 16]))
+        deal(w_dealt[0], w_raw[0], 0, 1)
+        deal_bytes(s1, s_raw, 0, 1)
+        nc.vector.tensor_copy(out=xg_w[:, HALF:], in_=xw[:].bitcast(U32).indirect(offs_sb[:, HALF // 16 :]))
+        nc.vector.tensor_copy(out=xg_s[:, HALF:], in_=xs[:].indirect(offs_sb[:, HALF // 16 :]))
+        deal(w_dealt[0], w_raw[0], 1, 4)
+        deal_bytes(s1, s_raw, 1, 4)
         load_scales([nc.sync] * 4, s_raw, 4, w2_scales)
         load_scales([nc.sync] * 4, s_raw, 8, w3_scales)
-        nc.vector.tensor_copy(out=xg_w[:, :HALF], in_=xw[:].bitcast(U32).indirect(offs_sb[:, : HALF // 16]))
-        deal(w_dealt[0], w_raw[0], 0, 2)
-        nc.vector.tensor_copy(out=xg_w[:, HALF:], in_=xw[:].bitcast(U32).indirect(offs_sb[:, HALF // 16 :]))
-        deal(w_dealt[0], w_raw[0], 2, 4)
 
         y = []
         for t in range(PACK):
@@ -157,7 +154,7 @@ def tile_picked_ace8_none_po_kernel(
             summed = bank("summed%d%d" % (t, b), number)
             for n in range(TERMS):
                 nc.vector.tensor_tensor(
-                    terms[:, n, :], picks(t, n, b, blocks), gates[n][:, b * B : (b + blocks) * B], MULT
+                    terms[:, n, :], picks(t, n, b, blocks), gates[n][:, (b - 1) * B : (b - 1 + blocks) * B], MULT
                 )
                 for h in range(blocks):
                     nc.tensor.matmul(
@@ -180,9 +177,9 @@ def tile_picked_ace8_none_po_kernel(
                     nc.tensor.transpose(apart[h][:, n * P : (n + 1) * P], terms[:, n, h * B : (h + 1) * B], ident[:])
             return apart
 
-        def plain_sums(t, b, apart):
+        def plain_sums(t, b, apart, tag=None):
             for h in range(len(apart)):
-                turned = sb("turned%d%d%d" % (t, b, h), [P, TERMS, P], F32)
+                turned = sb("turned%d%d%d" % (t, b, h), [P, TERMS, P], F32, tag)
                 for n in range(TERMS):
                     nc.scalar.activation(
                         turned[:, n, :], apart[h][:, n * P : (n + 1) * P], COPY,
@@ -194,13 +191,13 @@ def tile_picked_ace8_none_po_kernel(
                         start=(n == 0), stop=(n == TERMS - 1), is_transpose=True,
                     )
 
-        def plain_unit(t, b, blocks, numbers):
-            plain_sums(t, b, plain_gathers(t, b, blocks, numbers))
+        def plain_unit(t, b, blocks, numbers, tag=None):
+            plain_sums(t, b, plain_gathers(t, b, blocks, numbers), tag)
 
         def added_unit(t, b, a_sb):
             terms = sb("terms%d%d" % (t, b), [P, TERMS + 1, B], F32)
             for n in range(TERMS):
-                nc.vector.tensor_tensor(terms[:, n, :], picks(t, n, b, 1), gates[n][:, b * B : (b + 1) * B], MULT)
+                nc.vector.tensor_tensor(terms[:, n, :], picks(t, n, b, 1), gates[n][:, (b - 1) * B : b * B], MULT)
             nc.vector.tensor_tensor(terms[:, TERMS, :], terms[:, 0, :], terms[:, 1, :], ADD)
             nc.vector.tensor_tensor(a_sb[:, t, :], terms[:, TERMS, :], terms[:, 2, :], ADD)
 
@@ -226,14 +223,13 @@ def tile_picked_ace8_none_po_kernel(
                 )
             return zi
 
-        def finish(b, zi):
-            cols = slice(b * B, (b + 1) * B)
+        def multiply(b, zi, number):
             codes = sb("codes%d" % b, [P, 2 * B], U32)
             scales = sb("scales%d" % b, [P, 2 * B], U8)
             nc.vector.quantize_mx(
                 out=codes[:].bitcast(FP8X4), scales=scales[:], in_=zi[:].rearrange("p z j t -> p (z j t)")
             )
-            out_ps = bank("out_ps%d" % b, 4 + b)
+            out_ps = bank("out_ps%d" % b, number)
             for t in range(PACK):
                 for z in range(2):
                     nc.tensor.matmul_mx(
@@ -245,41 +241,54 @@ def tile_picked_ace8_none_po_kernel(
                         start=(z == 0),
                         stop=(z == 1),
                     )
-            res = sb("res%d" % b, [P, PACK, B], F32)
+            return out_ps
+
+        def leave(b, out_ps, tag=None, on_scalar=False):
+            cols = slice(b * B, (b + 1) * B)
+            res = sb("res%d" % b, [P, PACK, B], F32, tag)
             res_i = sb("res_i%d" % b, [P, B, PACK], BF16)
             nc.scalar.copy(out=res[:].rearrange("p t j -> p (t j)"), in_=out_ps[:])
             nc.sync.dma_start(out=out_rows[:, :, cols], in_=res[:])
-            nc.vector.tensor_copy(
-                out=res_i[:].rearrange("p (c i) t -> p c t i", i=4),
-                in_=res[:].rearrange("p t (c i) -> p c t i", i=4),
-            )
+            if on_scalar:
+                nc.scalar.copy(out=res_i[:], in_=out_ps[:].rearrange("p (t j) -> p j t", t=PACK))
+            else:
+                nc.vector.tensor_copy(
+                    out=res_i[:].rearrange("p (c i) t -> p c t i", i=4),
+                    in_=res[:].rearrange("p t (c i) -> p c t i", i=4),
+                )
             nc.vector.quantize_mx(
                 out=out_codes[:, cols].bitcast(FP8X4), scales=out_scales[:, cols],
                 in_=res_i[:].rearrange("p j t -> p (j t)"),
             )
 
         a_last = sb("a_last", [P, PACK, B], F32)
-        gated_unit(0, 0, 2, 0)
-        plain_unit(1, 0, 2, (1, 3))
-        gated_unit(2, 0, 2, 2)
-        gated_unit(3, 0, 2, 0)
-        plain_unit(1, 2, 1, (1,))
-        plain_unit(0, 2, 1, (3,))
+        gated_unit(0, 1, 2, 0)
+        plain_unit(1, 1, 2, (1, 3))
+        gated_unit(2, 1, 2, 2)
+        gated_unit(3, 1, 2, 0)
+        plain_unit(1, 0, 1, (1,))
+        plain_unit(0, 0, 1, (3,))
+        plain_unit(2, 0, 1, (2,))
+        plain_unit(3, 0, 1, (0,), "tie_a")
         deal(w_dealt[1], w_raw[1], 0, 4)
         deal(w_dealt[2], w_raw[2], 0, 4)
-        deal_bytes(s23, s_raw)
-        added_unit(0, 3, a_last)
-        finish(0, orders_from_bank(0))
-        plain_unit(2, 2, 1, (2,))
-        added_unit(1, 3, a_last)
-        finish(1, orders_from_bank(1))
-        plain_unit(3, 2, 1, (0,))
-        added_unit(2, 3, a_last)
-        added_unit(3, 3, a_last)
-        finish(2, orders_from_bank(2))
-        nc.sync.dma_start(out=out_words[:, : 3 * B], in_=out_codes[:, : 3 * B].bitcast(I32))
-        finish(3, orders_from_planes(3, a_last))
-        nc.sync.dma_start(out=out_words[:, 3 * B :], in_=out_codes[:, 3 * B :].bitcast(I32))
+        deal_bytes(s23, s_raw, 0, 4)
+        for t in range(PACK):
+            added_unit(t, 3, a_last)
+        z1 = orders_from_bank(1)
+        z2 = orders_from_bank(2)
+        o1 = multiply(1, z1, 5)
+        z3 = orders_from_planes(3, a_last)
+        o2 = multiply(2, z2, 6)
+        z0 = orders_from_bank(0)
+        o3 = multiply(3, z3, 7)
+        leave(1, o1, "tie_a")
+        o0 = multiply(0, z0, 4)
+        leave(2, o2)
+        leave(3, o3)
+        nc.sync.dma_start(out=out_words[:, B:], in_=out_codes[:, B:].bitcast(I32))
+        leave(0, o0)
+        nc.sync.dma_start(out=out_words[:, :B], in_=out_codes[:, :B].bitcast(I32))
         for q in range(4):
             queue = nc.sync if q % 2 == 0 else nc.scalar
             queue.dma_start(

@@ -15,7 +15,10 @@ U8 = mybir.dt.uint8
 FP8X4 = mybir.dt.float8_e4m3fn_x4
 MULT = mybir.AluOpType.mult
 ADD = mybir.AluOpType.add
+MAX = mybir.AluOpType.max
+MIN = mybir.AluOpType.min
 COPY = mybir.ActivationFunctionType.Copy
+SQRT = mybir.ActivationFunctionType.Sqrt
 SQUARE = mybir.ActivationFunctionType.Square
 
 P = 128
@@ -53,13 +56,13 @@ def tile_picked_ace8_none_po_kernel(
 
         def deal(dst, src, t0, t1):
             nc.vector.tensor_copy(
-                out=dst[:].rearrange("p (t c i) -> p c t i", t=PACK, i=4)[:, :, t0:t1, :],
-                in_=src[:].rearrange("p (c i t) -> p c t i", t=PACK, i=4)[:, :, t0:t1, :],
+                out=dst[:].rearrange("p (t c i) -> p c t i", t=t1 - t0, i=4),
+                in_=src.rearrange("p (c i t) -> p c t i", t=PACK, i=4)[:, :, t0:t1, :],
             )
 
         def deal_bytes(dst, src, t0, t1):
             nc.vector.tensor_copy(
-                out=dst[:].rearrange("p (t m) -> p m t", t=PACK)[:, :, t0:t1],
+                out=dst[:].rearrange("p (t m) -> p m t", t=t1 - t0),
                 in_=src[:].rearrange("p (m t) -> p m t", t=PACK)[:, :, t0:t1],
             )
 
@@ -67,71 +70,100 @@ def tile_picked_ace8_none_po_kernel(
         lists = [sb("list%d" % n, [P, S // 16], U16) for n in range(TERMS)]
         xw = sb("xw", [P, T], I32)
         xs = sb("xs", [P, T], U8)
-        w_raw = [sb("w_raw%d" % i, [P, H], I32) for i in range(3)]
-        s_raw = sb("s_raw", [P, H], U8)
-        gates = [sb("gate%d" % n, [P, S - B], F32) for n in range(TERMS)]
-        gate_cols = [sb("gate_col%d" % n, [P, BLOCKS - 1], F32) for n in range(TERMS)]
+        w1_raw = sb("w1_raw", [P, H], I32)
+        s1_raw = sb("s1_raw", [P, H], U8)
         c1_sb = sb("c1_sb", [P, PACK], F32)
         c2_sb = sb("c2_sb", [P, PACK], F32)
-        eye = sb("eye", [P, P], F32)
         ident = sb("ident", [P, P], F32)
 
         nc.vector.memset(xs[:].bitcast(I32), 0)
-        nc.vector.memset(s_raw[:].bitcast(I32), 0)
+        nc.vector.memset(s1_raw[:].bitcast(I32), 0)
+        nc.scalar.dma_start(out=c2_sb[:], in_=c2.rearrange("(p t) o -> p (t o)", t=PACK))
+        nc.scalar.dma_start(out=c1_sb[:], in_=c1.rearrange("(p t) o -> p (t o)", t=PACK))
         nc.sync.dma_start(offs_sb[:], offs)
+        for n, p in enumerate((p1, p2, p3)):
+            nc.sync.dma_start(lists[n][:], p)
         nc.sync.dma_start(out=xw[:], in_=words_of(x_words))
         load_scales([nc.sync] * 4, xs, 0, x_scales)
-        nc.sync.dma_start(out=w_raw[0][:], in_=words_of(w1_words))
-        load_scales([nc.sync] * 4, s_raw, 0, w1_scales)
-        for n, (p, g) in enumerate(((p1, g1), (p2, g2), (p3, g3))):
-            nc.sync.dma_start(lists[n][:], p)
-            nc.sync.dma_start(out=gates[n][:], in_=g[:, B:])
-        nc.sync.dma_start(out=w_raw[1][:], in_=words_of(w2_words))
-        nc.sync.dma_start(out=w_raw[2][:], in_=words_of(w3_words))
+        load_scales([nc.sync] * 4, s1_raw, 0, w1_scales)
+        nc.sync.dma_start(out=w1_raw[:], in_=words_of(w1_words))
+        make_identity(nc, ident[:])
+
+        def small(name, dtype=F32):
+            return sb(name, [P, PACK], dtype)
+
+        size, held, guess, inv_guess, other, twice, root, inv_held = (
+            small(name) for name in ("size", "held", "guess", "inv_guess", "other", "twice", "root", "inv_held")
+        )
+        first, sign = small("first"), small("sign", BF16)
+        nc.vector.scalar_tensor_tensor(size[:], c2_sb[:], -1.0, c2_sb[:], MULT, MAX)
+        nc.vector.tensor_scalar(held[:], size[:], 2.0**-100, 2.0**100, MAX, MIN)
+        nc.scalar.activation(guess[:], held[:], SQRT)
+        nc.vector.reciprocal(inv_held[:], held[:])
+        nc.vector.tensor_tensor(sign[:], c2_sb[:], inv_held[:], MULT)
+        nc.vector.reciprocal(inv_guess[:], guess[:])
+        nc.vector.tensor_tensor(other[:], held[:], inv_guess[:], MULT)
+        nc.vector.tensor_tensor(twice[:], other[:], guess[:], ADD)
+        nc.vector.tensor_scalar(root[:], twice[:], 0.5, None, MULT)
+        w23_raw = sb("w23_raw", [P, 2, H], I32, "size")
+        nc.sync.dma_start(out=w23_raw[:, 0, :], in_=words_of(w2_words))
+        nc.sync.dma_start(out=w23_raw[:, 1, :], in_=words_of(w3_words))
+
+        xg_w = [sb("xg_w%d" % h, [P, HALF], U32) for h in range(2)]
+        xg_s = [sb("xg_s%d" % h, [P, HALF], U8) for h in range(2)]
+        w1_first = sb("w1_first", [P, P], I32)
+        s1_first, s1_rest = sb("s1_first", [P, P], U8), sb("s1_rest", [P, H - P], U8)
+        w_dealt = [sb("w_dealt%d" % i, [P, N], I32) for i in range(2)]
+        picked = [offs_sb[:, h * HALF // 16 : (h + 1) * HALF // 16] for h in range(2)]
+        for h in range(2):
+            nc.vector.tensor_copy(out=xg_w[h][:], in_=xw[:].bitcast(U32).indirect(picked[h]))
+        deal(w1_first, w1_raw[:], 0, 1)
+        for h in range(2):
+            nc.vector.tensor_copy(out=xg_s[h][:], in_=xs[:].indirect(picked[h]))
+        deal_bytes(s1_first, s1_raw, 0, 1)
+        deal_bytes(s1_rest, s1_raw, 1, PACK)
+        w1_rest = sb("w1_rest", [P, H - P], I32, "s1_raw")
+        deal(w1_rest, w1_raw[:], 1, PACK)
+        gate_rows = sb("gate_rows", [P, TERMS, S - B], F32, "xw")
+        gates = [gate_rows[:, n, :] for n in range(TERMS)]
+        for n, g in enumerate((g1, g2, g3)):
+            nc.sync.dma_start(out=gates[n], in_=g[:, B:])
+        deal(w_dealt[0], w23_raw[:, 0, :], 0, PACK)
+        deal(w_dealt[1], w23_raw[:, 1, :], 0, PACK)
+        gate_tile = sb("gate_tile", [P, TERMS, 8], F32, "xs")
+        gate_cols = [gate_tile[:, n, : BLOCKS - 1] for n in range(TERMS)]
         for n, g in enumerate((g1, g2, g3)):
             nc.sync.dma_start(
-                out=gate_cols[n][:], in_=g[0, : S - B].rearrange("(b p) -> p b", p=P), allow_slow_non_contiguous=True
+                out=gate_cols[n], in_=g[0, : S - B].rearrange("(b p) -> p b", p=P), allow_slow_non_contiguous=True
             )
-        nc.gpsimd.dma_start(out=c1_sb[:], in_=c1.rearrange("(p t) o -> p (t o)", t=PACK))
-        nc.gpsimd.dma_start(out=c2_sb[:], in_=c2.rearrange("(p t) o -> p (t o)", t=PACK))
-        make_identity(nc, eye[:])
-        nc.scalar.activation(ident[:], eye[:], SQUARE)
-
-        xg_s = sb("xg_s", [P, S], U8)
-        xg_w = sb("xg_w", [P, S], U32)
-        w_dealt = [sb("w_dealt%d" % i, [P, H], I32) for i in range(3)]
-        s1 = sb("s1", [P, H], U8)
-        nc.vector.tensor_copy(out=xg_w[:, :HALF], in_=xw[:].bitcast(U32).indirect(offs_sb[:, : HALF // 16]))
-        nc.vector.tensor_copy(out=xg_s[:, :HALF], in_=xs[:].indirect(offs_sb[:, : HALF // 16]))
-        deal(w_dealt[0], w_raw[0], 0, 1)
-        deal_bytes(s1, s_raw, 0, 1)
-        nc.vector.tensor_copy(out=xg_w[:, HALF:], in_=xw[:].bitcast(U32).indirect(offs_sb[:, HALF // 16 :]))
-        nc.vector.tensor_copy(out=xg_s[:, HALF:], in_=xs[:].indirect(offs_sb[:, HALF // 16 :]))
-        deal(w_dealt[0], w_raw[0], 1, 4)
-        deal_bytes(s1, s_raw, 1, 4)
-        load_scales([nc.sync] * 4, s_raw, 4, w2_scales)
-        load_scales([nc.sync] * 4, s_raw, 8, w3_scales)
+        s_raw = sb("s_raw", [P, N], U8, "w1_raw")
+        nc.gpsimd.memset(s_raw[:].bitcast(I32), 0)
+        load_scales([nc.sync] * 4, s_raw, 0, w2_scales)
+        load_scales([nc.sync] * 4, s_raw, 4, w3_scales)
 
         y = []
         for t in range(PACK):
             y_t = sb("y%d" % t, [P, S], F32)
-            spans = [(0, HALF), (HALF, S)] if t == 0 else [(0, S)]
-            for lo, hi in spans:
-                y_ps = bank("y_ps%d_%d" % (t, lo), t if lo == 0 else 4)
+            rest = slice((t - 1) * P, t * P)
+            w1_t, s1_t = (w1_first[:], s1_first[:]) if t == 0 else (w1_rest[:, rest], s1_rest[:, rest])
+            y_ps = bank("y_ps%d" % t, t)
+            for h in range(2):
+                cols = slice(h * HALF, (h + 1) * HALF)
+                if t == 0 and h == 1:
+                    y_ps = bank("y_ps0_late", 4)
                 nc.tensor.matmul_mx(
-                    out=y_ps[:, : hi - lo],
-                    lhsT=w_dealt[0][:, t * P : (t + 1) * P].bitcast(FP8X4),
-                    lhsT_scale=s1[:, t * P : (t + 1) * P],
-                    rhs=xg_w[:, lo:hi].bitcast(FP8X4),
-                    rhs_scale=xg_s[:, lo:hi],
-                    start=True,
-                    stop=True,
+                    out=y_ps[:, cols], lhsT=w1_t.bitcast(FP8X4), lhsT_scale=s1_t,
+                    rhs=xg_w[h][:].bitcast(FP8X4), rhs_scale=xg_s[h][:], start=True, stop=True,
                 )
-                if lo == 0:
-                    nc.scalar.copy(out=y_t[:, lo:hi], in_=y_ps[:, : hi - lo])
-                else:
-                    nc.vector.tensor_copy(out=y_t[:, lo:hi], in_=y_ps[:, : hi - lo])
+                if t == 0:
+                    nc.scalar.activation(y_t[:, cols], y_ps[:, cols], COPY, scale=root[:, t : t + 1])
+            if t > 0:
+                nc.scalar.activation(y_t[:], y_ps[:], COPY, scale=root[:, t : t + 1])
             y.append(y_t)
+
+        inv_root = sb("inv_root", [P, PACK], F32, "w1_first")
+        nc.vector.reciprocal(inv_root[:], root[:])
+        nc.vector.tensor_tensor(first[:], c1_sb[:], inv_root[:], MULT)
 
         out_codes = sb("out_codes", [P, S], U32)
         out_scales = sb("out_scales", [P, S], U8)
@@ -149,8 +181,8 @@ def tile_picked_ace8_none_po_kernel(
         def picks(t, n, b, blocks):
             return y[t][:].indirect(lists[n][:, b * B // 16 : (b + blocks) * B // 16])
 
-        def gated_unit(t, b, blocks, number):
-            terms = sb("terms%d%d" % (t, b), [P, TERMS, blocks * B], F32)
+        def gated_gathers(t, b, blocks, number, tag=None):
+            terms = sb("terms%d%d" % (t, b), [P, TERMS, blocks * B], F32, tag)
             summed = bank("summed%d%d" % (t, b), number)
             for n in range(TERMS):
                 nc.vector.tensor_tensor(
@@ -161,15 +193,18 @@ def tile_picked_ace8_none_po_kernel(
                         summed[:, h * P : (h + 1) * P], terms[:, n, h * B : (h + 1) * B], ident[:],
                         start=(n == 0 and h == 0), stop=(n == TERMS - 1 and h == blocks - 1), is_transpose=True,
                     )
-            turned = sb("turned%d%d" % (t, b), [P, blocks * P], F32)
+            return summed
+
+        def gated_sums(t, b, blocks, summed, tag=None):
+            turned = sb("turned%d%d" % (t, b), [P, blocks * P], F32, tag)
             nc.scalar.copy(out=turned[:], in_=summed[:, : blocks * P])
             for h in range(blocks):
                 nc.tensor.transpose(
                     sums_of(b + h)[:, t * B : (t + 1) * B], turned[:, h * P : (h + 1) * P], ident[:]
                 )
 
-        def plain_gathers(t, b, blocks, numbers):
-            terms = sb("terms%d%d" % (t, b), [P, TERMS, blocks * B], F32)
+        def plain_gathers(t, b, blocks, numbers, tag=None):
+            terms = sb("terms%d%d" % (t, b), [P, TERMS, blocks * B], F32, tag)
             apart = [bank("apart%d%d%d" % (t, b, h), numbers[h]) for h in range(blocks)]
             for n in range(TERMS):
                 nc.scalar.activation(terms[:, n, :], picks(t, n, b, blocks), COPY)
@@ -178,49 +213,56 @@ def tile_picked_ace8_none_po_kernel(
             return apart
 
         def plain_sums(t, b, apart, tag=None):
-            for h in range(len(apart)):
-                turned = sb("turned%d%d%d" % (t, b, h), [P, TERMS, P], F32, tag)
-                for n in range(TERMS):
-                    nc.scalar.activation(
-                        turned[:, n, :], apart[h][:, n * P : (n + 1) * P], COPY,
-                        scale=gate_cols[n][:, b + h : b + h + 1],
-                    )
-                for n in range(TERMS):
-                    nc.tensor.matmul(
-                        sums_of(b + h)[:, t * B : (t + 1) * B], turned[:, n, :], ident[:],
-                        start=(n == 0), stop=(n == TERMS - 1), is_transpose=True,
-                    )
-
-        def plain_unit(t, b, blocks, numbers, tag=None):
-            plain_sums(t, b, plain_gathers(t, b, blocks, numbers), tag)
-
-        def added_unit(t, b, a_sb):
-            terms = sb("terms%d%d" % (t, b), [P, TERMS + 1, B], F32)
+            turned = sb("turned%d%d" % (t, b), [P, TERMS, P], F32, tag)
             for n in range(TERMS):
-                nc.vector.tensor_tensor(terms[:, n, :], picks(t, n, b, 1), gates[n][:, (b - 1) * B : b * B], MULT)
-            nc.vector.tensor_tensor(terms[:, TERMS, :], terms[:, 0, :], terms[:, 1, :], ADD)
-            nc.vector.tensor_tensor(a_sb[:, t, :], terms[:, TERMS, :], terms[:, 2, :], ADD)
+                nc.scalar.activation(
+                    turned[:, n, :], apart[:, n * P : (n + 1) * P], COPY, scale=gate_cols[n][:, b : b + 1]
+                )
+            for n in range(TERMS):
+                nc.tensor.matmul(
+                    sums_of(b)[:, t * B : (t + 1) * B], turned[:, n, :], ident[:],
+                    start=(n == 0), stop=(n == TERMS - 1), is_transpose=True,
+                )
 
-        def orders_from_bank(b):
+        def square(b, tag=None):
+            sq = sb("sq%d" % b, [P, B, PACK], BF16, tag)
+            nc.scalar.activation(sq[:], a_ps[b][:].rearrange("p (t j) -> p j t", t=PACK), SQUARE)
+            return sq
+
+        def signed(zi, sq):
+            nc.vector.tensor_tensor(zi[:, 1], sq[:], sign[:].unsqueeze(1).broadcast_to([P, B, PACK]), MULT)
+
+        def orders(b, sq, tag=None):
             a = a_ps[b][:].rearrange("p (t j) -> p j t", t=PACK)
-            sq = sb("sq%d" % b, [P, B, PACK], F32)
-            zi = sb("zi%d" % b, [P, 2, B, PACK], BF16)
-            nc.scalar.activation(sq[:], a, SQUARE)
-            nc.vector.tensor_tensor(zi[:, 0], a, c1_sb[:].unsqueeze(1).broadcast_to([P, B, PACK]), MULT)
-            nc.vector.tensor_tensor(zi[:, 1], sq[:], c2_sb[:].unsqueeze(1).broadcast_to([P, B, PACK]), MULT)
+            zi = sb("zi%d" % b, [P, 2, B, PACK], BF16, tag)
+            nc.vector.tensor_tensor(zi[:, 0], a, first[:].unsqueeze(1).broadcast_to([P, B, PACK]), MULT)
+            signed(zi, sq)
             return zi
 
+        def added_block(b, tag):
+            terms = sb("planes", [P, TERMS, PACK, B], F32, tag)
+            pair = sb("pair", [P, PACK, B], F32)
+            total = sb("total", [P, PACK, B], F32)
+            for n in range(TERMS):
+                for t in range(PACK):
+                    nc.vector.tensor_tensor(
+                        terms[:, n, t, :], picks(t, n, b, 1), gates[n][:, (b - 1) * B : b * B], MULT
+                    )
+                if n == 1:
+                    nc.vector.tensor_tensor(pair[:], terms[:, 0], terms[:, 1], ADD)
+            nc.vector.tensor_tensor(total[:], pair[:], terms[:, 2], ADD)
+            return total
+
         def orders_from_planes(b, a_sb):
-            sq = sb("sq%d" % b, [P, PACK, B], F32)
+            sq = sb("sq%d" % b, [P, B, PACK], BF16)
             zi = sb("zi%d" % b, [P, 2, B, PACK], BF16)
-            nc.scalar.activation(sq[:], a_sb[:], SQUARE)
-            for z, (src, c) in enumerate(((a_sb, c1_sb), (sq, c2_sb))):
-                nc.vector.tensor_tensor(
-                    zi[:, z].rearrange("p (c i) t -> p c t i", i=4),
-                    src[:].rearrange("p t (c i) -> p c t i", i=4),
-                    c[:].unsqueeze(1).unsqueeze(3).broadcast_to([P, B // 4, PACK, 4]),
-                    MULT,
-                )
+            lines = a_sb[:].rearrange("p t (c i) -> p c t i", i=4)
+            nc.scalar.activation(sq[:].rearrange("p (c i) t -> p c t i", i=4), lines, SQUARE)
+            nc.vector.tensor_tensor(
+                zi[:, 0].rearrange("p (c i) t -> p c t i", i=4), lines,
+                first[:].unsqueeze(1).unsqueeze(3).broadcast_to([P, B // 4, PACK, 4]), MULT,
+            )
+            signed(zi, sq)
             return zi
 
         def multiply(b, zi, number):
@@ -234,8 +276,8 @@ def tile_picked_ace8_none_po_kernel(
                 for z in range(2):
                     nc.tensor.matmul_mx(
                         out=out_ps[:, t * B : (t + 1) * B],
-                        lhsT=w_dealt[1 + z][:, t * P : (t + 1) * P].bitcast(FP8X4),
-                        lhsT_scale=s23[4 + 4 * z : P, t * P : (t + 1) * P],
+                        lhsT=w_dealt[z][:, t * P : (t + 1) * P].bitcast(FP8X4),
+                        lhsT_scale=s23[4 * z : P, t * P : (t + 1) * P],
                         rhs=codes[:, z * B : (z + 1) * B].bitcast(FP8X4),
                         rhs_scale=scales[:, z * B : (z + 1) * B],
                         start=(z == 0),
@@ -261,30 +303,30 @@ def tile_picked_ace8_none_po_kernel(
                 in_=res_i[:].rearrange("p j t -> p (j t)"),
             )
 
-        a_last = sb("a_last", [P, PACK, B], F32)
-        gated_unit(0, 1, 2, 0)
-        plain_unit(1, 1, 2, (1, 3))
-        gated_unit(2, 1, 2, 2)
-        gated_unit(3, 1, 2, 0)
-        plain_unit(1, 0, 1, (1,))
-        plain_unit(0, 0, 1, (3,))
-        plain_unit(2, 0, 1, (2,))
-        plain_unit(3, 0, 1, (0,), "tie_a")
-        deal(w_dealt[1], w_raw[1], 0, 4)
-        deal(w_dealt[2], w_raw[2], 0, 4)
+        gated_sums(0, 1, 2, gated_gathers(0, 1, 2, 0, "ring0"), "ring4")
+        s1 = plain_gathers(1, 1, 2, (1, 3), "ring1")
+        plain_sums(1, 1, s1[0])
+        plain_sums(1, 2, s1[1])
+        gated_sums(2, 1, 2, gated_gathers(2, 1, 2, 2, "ring2"))
+        gated_sums(3, 1, 2, gated_gathers(3, 1, 2, 0, "ring3"))
+        q1 = square(1)
+        plain_sums(1, 0, plain_gathers(1, 0, 1, (1,), "ring0")[0])
+        plain_sums(0, 0, plain_gathers(0, 0, 1, (3,), "ring1")[0])
+        q2 = square(2)
+        plain_sums(2, 0, plain_gathers(2, 0, 1, (2,), "ring2")[0])
+        plain_sums(3, 0, plain_gathers(3, 0, 1, (0,), "ring3")[0], "ring5")
         deal_bytes(s23, s_raw, 0, 4)
-        for t in range(PACK):
-            added_unit(t, 3, a_last)
-        z1 = orders_from_bank(1)
-        z2 = orders_from_bank(2)
-        o1 = multiply(1, z1, 5)
+        a_last = added_block(3, "ring4")
+        z1 = orders(1, q1)
+        z2 = orders(2, q2)
+        o1 = multiply(1, z1, 0)
         z3 = orders_from_planes(3, a_last)
         o2 = multiply(2, z2, 6)
-        z0 = orders_from_bank(0)
+        z0 = orders(0, square(0))
         o3 = multiply(3, z3, 7)
-        leave(1, o1, "tie_a")
+        leave(1, o1, "ring5", False)
         o0 = multiply(0, z0, 4)
-        leave(2, o2)
+        leave(2, o2, None, False)
         leave(3, o3)
         nc.sync.dma_start(out=out_words[:, B:], in_=out_codes[:, B:].bitcast(I32))
         leave(0, o0)

@@ -181,26 +181,13 @@ def tile_picked_ace8_none_po_kernel(
         def picks(t, n, b, blocks):
             return y[t][:].indirect(lists[n][:, b * B // 16 : (b + blocks) * B // 16])
 
-        def gated_gathers(t, b, blocks, number, tag=None):
-            terms = sb("terms%d%d" % (t, b), [P, TERMS, blocks * B], F32, tag)
-            summed = bank("summed%d%d" % (t, b), number)
+        wide = sb("wide", [P, TERMS, PACK, S - B], F32)
+
+        def gated_gathers(t, first_block):
+            cols = slice((first_block - 1) * B, S - B)
             for n in range(TERMS):
                 nc.vector.tensor_tensor(
-                    terms[:, n, :], picks(t, n, b, blocks), gates[n][:, (b - 1) * B : (b - 1 + blocks) * B], MULT
-                )
-                for h in range(blocks):
-                    nc.tensor.matmul(
-                        summed[:, h * P : (h + 1) * P], terms[:, n, h * B : (h + 1) * B], ident[:],
-                        start=(n == 0 and h == 0), stop=(n == TERMS - 1 and h == blocks - 1), is_transpose=True,
-                    )
-            return summed
-
-        def gated_sums(t, b, blocks, summed, tag=None):
-            turned = sb("turned%d%d" % (t, b), [P, blocks * P], F32, tag)
-            nc.scalar.copy(out=turned[:], in_=summed[:, : blocks * P])
-            for h in range(blocks):
-                nc.tensor.transpose(
-                    sums_of(b + h)[:, t * B : (t + 1) * B], turned[:, h * P : (h + 1) * P], ident[:]
+                    wide[:, n, t, cols], picks(t, n, first_block, BLOCKS - first_block), gates[n][:, cols], MULT
                 )
 
         def plain_gathers(t, b, blocks, numbers, tag=None):
@@ -212,7 +199,7 @@ def tile_picked_ace8_none_po_kernel(
                     nc.tensor.transpose(apart[h][:, n * P : (n + 1) * P], terms[:, n, h * B : (h + 1) * B], ident[:])
             return apart
 
-        def plain_sums(t, b, apart, tag=None):
+        def plain_sums(t, b, apart, into, tag=None):
             turned = sb("turned%d%d" % (t, b), [P, TERMS, P], F32, tag)
             for n in range(TERMS):
                 nc.scalar.activation(
@@ -220,7 +207,7 @@ def tile_picked_ace8_none_po_kernel(
                 )
             for n in range(TERMS):
                 nc.tensor.matmul(
-                    sums_of(b)[:, t * B : (t + 1) * B], turned[:, n, :], ident[:],
+                    into, turned[:, n, :], ident[:],
                     start=(n == 0), stop=(n == TERMS - 1), is_transpose=True,
                 )
 
@@ -239,24 +226,17 @@ def tile_picked_ace8_none_po_kernel(
             signed(zi, sq)
             return zi
 
-        def added_block(b, tag):
-            terms = sb("planes", [P, TERMS, PACK, B], F32, tag)
-            pair = sb("pair", [P, PACK, B], F32)
-            total = sb("total", [P, PACK, B], F32)
-            for n in range(TERMS):
-                for t in range(PACK):
-                    nc.vector.tensor_tensor(
-                        terms[:, n, t, :], picks(t, n, b, 1), gates[n][:, (b - 1) * B : b * B], MULT
-                    )
-                if n == 1:
-                    nc.vector.tensor_tensor(pair[:], terms[:, 0], terms[:, 1], ADD)
-            nc.vector.tensor_tensor(total[:], pair[:], terms[:, 2], ADD)
-            return total
+        total = sb("total", [P, PACK, S - B], F32)
 
-        def orders_from_planes(b, a_sb):
-            sq = sb("sq%d" % b, [P, B, PACK], BF16)
+        def added(tiles, cols, name, tag=None):
+            pair = sb(name, [P, len(range(PACK)[tiles]), cols.stop - cols.start], F32, tag)
+            nc.vector.tensor_tensor(pair[:], wide[:, 0, tiles, cols], wide[:, 1, tiles, cols], ADD)
+            nc.vector.tensor_tensor(total[:, tiles, cols], pair[:], wide[:, 2, tiles, cols], ADD)
+
+        def orders_from_planes(b, tag=None):
+            sq = sb("sq%d" % b, [P, B, PACK], BF16, tag)
             zi = sb("zi%d" % b, [P, 2, B, PACK], BF16)
-            lines = a_sb[:].rearrange("p t (c i) -> p c t i", i=4)
+            lines = total[:, :, (b - 1) * B : b * B].rearrange("p t (c i) -> p c t i", i=4)
             nc.scalar.activation(sq[:].rearrange("p (c i) t -> p c t i", i=4), lines, SQUARE)
             nc.vector.tensor_tensor(
                 zi[:, 0].rearrange("p (c i) t -> p c t i", i=4), lines,
@@ -303,34 +283,42 @@ def tile_picked_ace8_none_po_kernel(
                 in_=res_i[:].rearrange("p j t -> p (j t)"),
             )
 
-        gated_sums(0, 1, 2, gated_gathers(0, 1, 2, 0, "ring0"), "ring4")
-        s1 = plain_gathers(1, 1, 2, (1, 3), "ring1")
-        plain_sums(1, 1, s1[0])
-        plain_sums(1, 2, s1[1])
-        gated_sums(2, 1, 2, gated_gathers(2, 1, 2, 2, "ring2"))
-        gated_sums(3, 1, 2, gated_gathers(3, 1, 2, 0, "ring3"))
-        q1 = square(1)
-        plain_sums(1, 0, plain_gathers(1, 0, 1, (1,), "ring0")[0])
-        plain_sums(0, 0, plain_gathers(0, 0, 1, (3,), "ring1")[0])
-        q2 = square(2)
-        plain_sums(2, 0, plain_gathers(2, 0, 1, (2,), "ring2")[0])
-        plain_sums(3, 0, plain_gathers(3, 0, 1, (0,), "ring3")[0], "ring5")
+        gated_gathers(0, 1)
+        u0 = plain_gathers(0, 0, 1, (0,), "ring_a")
+        u1 = plain_gathers(1, 0, 1, (1,), "ring_b")
+        plain_sums(0, 0, u0[0], sums_of(0)[:, :B])
+        u2 = plain_gathers(2, 0, 1, (2,), "ring_a")
+        plain_sums(1, 0, u1[0], sums_of(0)[:, B : 2 * B])
+        u3 = plain_gathers(3, 0, 1, (3,), "ring_b")
+        plain_sums(2, 0, u2[0], sums_of(0)[:, 2 * B : 3 * B])
+        plain_sums(3, 0, u3[0], sums_of(0)[:, 3 * B :])
+        s1 = plain_gathers(1, 1, 2, (0, 1), "ring_b")
+        gated_gathers(2, 1)
+        gated_gathers(3, 1)
+        gated_gathers(1, 3)
+        q0 = square(0)
+        shared = bank("shared", 5)
+        plain_sums(1, 1, s1[0], shared[:, :B])
+        plain_sums(1, 2, s1[1], shared[:, B : 2 * B], "ring_c")
+        nc.scalar.copy(out=total[:, 1, : 2 * B], in_=shared[:, : 2 * B])
         deal_bytes(s23, s_raw, 0, 4)
-        a_last = added_block(3, "ring4")
-        z1 = orders(1, q1)
-        z2 = orders(2, q2)
-        o1 = multiply(1, z1, 0)
-        z3 = orders_from_planes(3, a_last)
-        o2 = multiply(2, z2, 6)
-        z0 = orders(0, square(0))
+        added(slice(0, 4), slice(2 * B, 3 * B), "pair3")
+        z0 = orders(0, q0)
+        o0 = multiply(0, z0, 1)
+        added(slice(0, 1), slice(0, 2 * B), "pair0")
+        added(slice(2, 4), slice(0, 2 * B), "pair2")
+        z3 = orders_from_planes(3, None)
         o3 = multiply(3, z3, 7)
-        leave(1, o1, "ring5", False)
-        o0 = multiply(0, z0, 4)
-        leave(2, o2, None, False)
-        leave(3, o3)
-        nc.sync.dma_start(out=out_words[:, B:], in_=out_codes[:, B:].bitcast(I32))
-        leave(0, o0)
-        nc.sync.dma_start(out=out_words[:, :B], in_=out_codes[:, :B].bitcast(I32))
+        leave(0, o0, "ring_c", False)
+        z1 = orders_from_planes(1)
+        o1 = multiply(1, z1, 6)
+        z2 = orders_from_planes(2)
+        leave(3, o3, None, False)
+        o2 = multiply(2, z2, 0)
+        leave(1, o1)
+        nc.sync.dma_start(out=out_words[:, : 2 * B], in_=out_codes[:, : 2 * B].bitcast(I32))
+        leave(2, o2)
+        nc.sync.dma_start(out=out_words[:, 2 * B :], in_=out_codes[:, 2 * B :].bitcast(I32))
         for q in range(4):
             queue = nc.sync if q % 2 == 0 else nc.scalar
             queue.dma_start(

@@ -190,6 +190,29 @@ def tile_picked_ace8_none_po_kernel(
                     wide[:, n, t, cols], picks(t, n, first_block, BLOCKS - first_block), gates[n][:, cols], MULT
                 )
 
+        def raw_gathers(t, b, tag=None):
+            raw = sb("raw%d%d" % (t, b), [P, TERMS, B], F32, tag)
+            cols = slice((b - 1) * B, b * B)
+            for n in range(TERMS):
+                nc.scalar.activation(raw[:, n, :], picks(t, n, b, 1), COPY)
+            nc.vector.tensor_tensor(wide[:, :, t, cols], raw[:], gate_rows[:, :, cols], MULT)
+
+        def gated_turns(t, number):
+            summed = bank("summed%d" % t, number)
+            for n in range(TERMS):
+                for h in range(2):
+                    nc.tensor.matmul(
+                        summed[:, h * P : (h + 1) * P], wide[:, n, t, h * B : (h + 1) * B], ident[:],
+                        start=(n == 0 and h == 0), stop=(n == TERMS - 1 and h == 1), is_transpose=True,
+                    )
+            return summed
+
+        def gated_back(t, summed, into, tag=None):
+            turned = sb("turned_v%d" % t, [P, 2 * P], F32, tag)
+            nc.scalar.copy(out=turned[:], in_=summed[:, : 2 * P])
+            for h in range(2):
+                nc.tensor.transpose(into[:, h * B : (h + 1) * B], turned[:, h * P : (h + 1) * P], ident[:])
+
         def plain_gathers(t, b, blocks, numbers, tag=None):
             terms = sb("terms%d%d" % (t, b), [P, TERMS, blocks * B], F32, tag)
             apart = [bank("apart%d%d%d" % (t, b, h), numbers[h]) for h in range(blocks)]
@@ -233,15 +256,26 @@ def tile_picked_ace8_none_po_kernel(
             nc.vector.tensor_tensor(pair[:], wide[:, 0, tiles, cols], wide[:, 1, tiles, cols], ADD)
             nc.vector.tensor_tensor(total[:, tiles, cols], pair[:], wide[:, 2, tiles, cols], ADD)
 
-        def orders_from_planes(b, tag=None):
+        def orders_from_planes(b, tag=None, on_scalar=False, ring=None):
             sq = sb("sq%d" % b, [P, B, PACK], BF16, tag)
-            zi = sb("zi%d" % b, [P, 2, B, PACK], BF16)
+            zi = sb("zi%d" % b, [P, 2, B, PACK], BF16, ring)
             lines = total[:, :, (b - 1) * B : b * B].rearrange("p t (c i) -> p c t i", i=4)
             nc.scalar.activation(sq[:].rearrange("p (c i) t -> p c t i", i=4), lines, SQUARE)
-            nc.vector.tensor_tensor(
-                zi[:, 0].rearrange("p (c i) t -> p c t i", i=4), lines,
-                first[:].unsqueeze(1).unsqueeze(3).broadcast_to([P, B // 4, PACK, 4]), MULT,
-            )
+            if on_scalar:
+                flat = sb("flat%d" % b, [P, PACK, B], BF16)
+                for t in range(PACK):
+                    nc.scalar.activation(
+                        flat[:, t, :], total[:, t, (b - 1) * B : b * B], COPY, scale=first[:, t : t + 1]
+                    )
+                nc.vector.tensor_copy(
+                    out=zi[:, 0].rearrange("p (c i) t -> p c t i", i=4),
+                    in_=flat[:].rearrange("p t (c i) -> p c t i", i=4),
+                )
+            else:
+                nc.vector.tensor_tensor(
+                    zi[:, 0].rearrange("p (c i) t -> p c t i", i=4), lines,
+                    first[:].unsqueeze(1).unsqueeze(3).broadcast_to([P, B // 4, PACK, 4]), MULT,
+                )
             signed(zi, sq)
             return zi
 
@@ -265,6 +299,39 @@ def tile_picked_ace8_none_po_kernel(
                     )
             return out_ps
 
+        def last_block(b, zi, numbers):
+            cols = slice(b * B, (b + 1) * B)
+            pairs = [bank("pair_ps%d" % u, numbers[u]) for u in range(2)]
+            for z in range(2):
+                codes = sb("last_codes%d" % z, [P, B], U32)
+                scales = sb("last_scales%d" % z, [P, B], U8)
+                nc.vector.quantize_mx(
+                    out=codes[:].bitcast(FP8X4), scales=scales[:], in_=zi[:, z].rearrange("p j t -> p (j t)")
+                )
+                for t in range(PACK):
+                    nc.tensor.matmul_mx(
+                        out=pairs[t // 2][:, t % 2 * B : (t % 2 + 1) * B],
+                        lhsT=w_dealt[z][:, t * P : (t + 1) * P].bitcast(FP8X4),
+                        lhsT_scale=s23[4 * z : P, t * P : (t + 1) * P],
+                        rhs=codes[:].bitcast(FP8X4),
+                        rhs_scale=scales[:],
+                        start=(z == 0 and t % 2 == 0),
+                        stop=(z == 1 and t % 2 == 1),
+                    )
+            res = sb("res%d" % b, [P, PACK, B], F32)
+            res_i = sb("res_i%d" % b, [P, B, PACK], BF16)
+            for u in range(2):
+                nc.scalar.copy(out=res[:, 2 * u : 2 * u + 2, :].rearrange("p t j -> p (t j)"), in_=pairs[u][:, : 2 * B])
+            nc.sync.dma_start(out=out_rows[:, :, cols], in_=res[:])
+            nc.vector.tensor_copy(
+                out=res_i[:].rearrange("p (c i) t -> p c t i", i=4),
+                in_=res[:].rearrange("p t (c i) -> p c t i", i=4),
+            )
+            nc.vector.quantize_mx(
+                out=out_codes[:, cols].bitcast(FP8X4), scales=out_scales[:, cols],
+                in_=res_i[:].rearrange("p j t -> p (j t)"),
+            )
+
         def leave(b, out_ps, tag=None, on_scalar=False):
             cols = slice(b * B, (b + 1) * B)
             res = sb("res%d" % b, [P, PACK, B], F32, tag)
@@ -284,41 +351,39 @@ def tile_picked_ace8_none_po_kernel(
             )
 
         gated_gathers(0, 1)
-        u0 = plain_gathers(0, 0, 1, (0,), "ring_a")
-        u1 = plain_gathers(1, 0, 1, (1,), "ring_b")
-        plain_sums(0, 0, u0[0], sums_of(0)[:, :B])
-        u2 = plain_gathers(2, 0, 1, (2,), "ring_a")
-        plain_sums(1, 0, u1[0], sums_of(0)[:, B : 2 * B])
-        u3 = plain_gathers(3, 0, 1, (3,), "ring_b")
-        plain_sums(2, 0, u2[0], sums_of(0)[:, 2 * B : 3 * B])
-        plain_sums(3, 0, u3[0], sums_of(0)[:, 3 * B :])
-        s1 = plain_gathers(1, 1, 2, (0, 1), "ring_b")
+        s1 = plain_gathers(1, 1, 2, (1, 3), "ring_b")
+        u1 = plain_gathers(1, 0, 1, (2,), "ring_a")
+        shared = bank("shared", 5)
+        plain_sums(1, 1, s1[0], shared[:, :B])
+        plain_sums(1, 2, s1[1], shared[:, B : 2 * B])
+        u0 = plain_gathers(0, 0, 1, (0,), "ring_b")
+        nc.scalar.copy(out=total[:, 1, : 2 * B], in_=shared[:, : 2 * B])
         gated_gathers(2, 1)
         gated_gathers(3, 1)
         gated_gathers(1, 3)
-        q0 = square(0)
-        shared = bank("shared", 5)
-        plain_sums(1, 1, s1[0], shared[:, :B])
-        plain_sums(1, 2, s1[1], shared[:, B : 2 * B], "ring_c")
-        nc.scalar.copy(out=total[:, 1, : 2 * B], in_=shared[:, : 2 * B])
+        plain_sums(1, 0, u1[0], sums_of(0)[:, B : 2 * B])
+        u2 = plain_gathers(2, 0, 1, (1,), "ring_a")
+        plain_sums(0, 0, u0[0], sums_of(0)[:, :B])
+        u3 = plain_gathers(3, 0, 1, (3,), "ring_b")
+        plain_sums(2, 0, u2[0], sums_of(0)[:, 2 * B : 3 * B])
+        plain_sums(3, 0, u3[0], sums_of(0)[:, 3 * B :])
         deal_bytes(s23, s_raw, 0, 4)
         added(slice(0, 4), slice(2 * B, 3 * B), "pair3")
-        z0 = orders(0, q0)
-        o0 = multiply(0, z0, 1)
         added(slice(0, 1), slice(0, 2 * B), "pair0")
         added(slice(2, 4), slice(0, 2 * B), "pair2")
-        z3 = orders_from_planes(3, None)
-        o3 = multiply(3, z3, 7)
-        leave(0, o0, "ring_c", False)
-        z1 = orders_from_planes(1)
-        o1 = multiply(1, z1, 6)
-        z2 = orders_from_planes(2)
-        leave(3, o3, None, False)
-        o2 = multiply(2, z2, 0)
-        leave(1, o1)
-        nc.sync.dma_start(out=out_words[:, : 2 * B], in_=out_codes[:, : 2 * B].bitcast(I32))
-        leave(2, o2)
-        nc.sync.dma_start(out=out_words[:, 2 * B :], in_=out_codes[:, 2 * B :].bitcast(I32))
+        z3 = orders_from_planes(3, "ring_b", False, "ring_z0")
+        z1 = orders_from_planes(1, None, False, "ring_z1")
+        oa = multiply(3, z3, 6)
+        z2 = orders_from_planes(2, None, False, "ring_z0")
+        ob = multiply(1, z1, 7)
+        z0 = orders(0, square(0), "ring_z1")
+        oc = multiply(2, z2, 5)
+        leave(3, oa)
+        leave(1, ob)
+        leave(2, oc)
+        nc.sync.dma_start(out=out_words[:, B:], in_=out_codes[:, B:].bitcast(I32))
+        last_block(0, z0, (0, 2))
+        nc.sync.dma_start(out=out_words[:, :B], in_=out_codes[:, :B].bitcast(I32))
         for q in range(4):
             queue = nc.sync if q % 2 == 0 else nc.scalar
             queue.dma_start(

@@ -256,26 +256,20 @@ def tile_picked_ace8_none_po_kernel(
             nc.vector.tensor_tensor(pair[:], wide[:, 0, tiles, cols], wide[:, 1, tiles, cols], ADD)
             nc.vector.tensor_tensor(total[:, tiles, cols], pair[:], wide[:, 2, tiles, cols], ADD)
 
-        def orders_from_planes(b, tag=None, on_scalar=False, ring=None):
+        def lines_of(b):
+            return total[:, :, (b - 1) * B : b * B].rearrange("p t (c i) -> p c t i", i=4)
+
+        def square_planes(b, tag=None):
             sq = sb("sq%d" % b, [P, B, PACK], BF16, tag)
+            nc.scalar.activation(sq[:].rearrange("p (c i) t -> p c t i", i=4), lines_of(b), SQUARE)
+            return sq
+
+        def orders_from_planes(b, sq, ring):
             zi = sb("zi%d" % b, [P, 2, B, PACK], BF16, ring)
-            lines = total[:, :, (b - 1) * B : b * B].rearrange("p t (c i) -> p c t i", i=4)
-            nc.scalar.activation(sq[:].rearrange("p (c i) t -> p c t i", i=4), lines, SQUARE)
-            if on_scalar:
-                flat = sb("flat%d" % b, [P, PACK, B], BF16)
-                for t in range(PACK):
-                    nc.scalar.activation(
-                        flat[:, t, :], total[:, t, (b - 1) * B : b * B], COPY, scale=first[:, t : t + 1]
-                    )
-                nc.vector.tensor_copy(
-                    out=zi[:, 0].rearrange("p (c i) t -> p c t i", i=4),
-                    in_=flat[:].rearrange("p t (c i) -> p c t i", i=4),
-                )
-            else:
-                nc.vector.tensor_tensor(
-                    zi[:, 0].rearrange("p (c i) t -> p c t i", i=4), lines,
-                    first[:].unsqueeze(1).unsqueeze(3).broadcast_to([P, B // 4, PACK, 4]), MULT,
-                )
+            nc.vector.tensor_tensor(
+                zi[:, 0].rearrange("p (c i) t -> p c t i", i=4), lines_of(b),
+                first[:].unsqueeze(1).unsqueeze(3).broadcast_to([P, B // 4, PACK, 4]), MULT,
+            )
             signed(zi, sq)
             return zi
 
@@ -367,14 +361,17 @@ def tile_picked_ace8_none_po_kernel(
         u3 = plain_gathers(3, 0, 1, (3,), "ring_b")
         plain_sums(2, 0, u2[0], sums_of(0)[:, 2 * B : 3 * B])
         plain_sums(3, 0, u3[0], sums_of(0)[:, 3 * B :])
+        warm_ps = bank("warm_ps", 3)
+        for i in range(6):
+            nc.tensor.matmul_mx(out=warm_ps[:, i % 2 * HALF : (i % 2 + 1) * HALF], lhsT=w1_rest[:, :P].bitcast(FP8X4), lhsT_scale=s1_rest[:, :P], rhs=xg_w[i % 2][:].bitcast(FP8X4), rhs_scale=xg_s[i % 2][:], start=True, stop=True)
         deal_bytes(s23, s_raw, 0, 4)
         added(slice(0, 4), slice(2 * B, 3 * B), "pair3")
         added(slice(0, 1), slice(0, 2 * B), "pair0")
         added(slice(2, 4), slice(0, 2 * B), "pair2")
-        z3 = orders_from_planes(3, "ring_b", False, "ring_z0")
-        z1 = orders_from_planes(1, None, False, "ring_z1")
+        z3 = orders_from_planes(3, square_planes(3, "ring_b"), "ring_z0")
+        z1 = orders_from_planes(1, square_planes(1), "ring_z1")
         oa = multiply(3, z3, 6)
-        z2 = orders_from_planes(2, None, False, "ring_z0")
+        z2 = orders_from_planes(2, square_planes(2), "ring_z0")
         ob = multiply(1, z1, 7)
         z0 = orders(0, square(0), "ring_z1")
         oc = multiply(2, z2, 5)

@@ -243,9 +243,14 @@ def tile_picked_ace8_none_po_kernel(
             nc.vector.tensor_tensor(zi[:, 1], sq[:], sign[:].unsqueeze(1).broadcast_to([P, B, PACK]), MULT)
 
         def orders(b, sq, tag=None):
-            a = a_ps[b][:].rearrange("p (t j) -> p j t", t=PACK)
             zi = sb("zi%d" % b, [P, 2, B, PACK], BF16, tag)
-            nc.vector.tensor_tensor(zi[:, 0], a, first[:].unsqueeze(1).broadcast_to([P, B, PACK]), MULT)
+            flat = sb("flat", [P, PACK, B], BF16)
+            for t in range(PACK):
+                nc.scalar.activation(flat[:, t, :], a_ps[b][:, t * B : (t + 1) * B], COPY, scale=first[:, t : t + 1])
+            nc.vector.tensor_copy(
+                out=zi[:, 0].rearrange("p (c i) t -> p c t i", i=4),
+                in_=flat[:].rearrange("p t (c i) -> p c t i", i=4),
+            )
             signed(zi, sq)
             return zi
 

@@ -131,10 +131,10 @@ def tile_picked_ace8_none_po_kernel(
         deal(w_dealt[0], w23_raw[:, 0, :], 0, PACK)
         deal(w_dealt[1], w23_raw[:, 1, :], 0, PACK)
         gate_tile = sb("gate_tile", [P, TERMS, 8], F32, "xs")
-        gate_cols = [gate_tile[:, n, : BLOCKS - 1] for n in range(TERMS)]
+        gate_cols = [gate_tile[:, n, :2] for n in range(TERMS)]
         for n, g in enumerate((g1, g2, g3)):
             nc.sync.dma_start(
-                out=gate_cols[n], in_=g[0, : S - B].rearrange("(b p) -> p b", p=P), allow_slow_non_contiguous=True
+                out=gate_cols[n], in_=g[0, : 2 * B].rearrange("(b p) -> p b", p=P), allow_slow_non_contiguous=True
             )
         s_raw = sb("s_raw", [P, N], U8, "w1_raw")
         nc.gpsimd.memset(s_raw[:].bitcast(I32), 0)
@@ -190,48 +190,22 @@ def tile_picked_ace8_none_po_kernel(
                     wide[:, n, t, cols], picks(t, n, first_block, BLOCKS - first_block), gates[n][:, cols], MULT
                 )
 
-        def raw_gathers(t, b, tag=None):
-            raw = sb("raw%d%d" % (t, b), [P, TERMS, B], F32, tag)
-            cols = slice((b - 1) * B, b * B)
-            for n in range(TERMS):
-                nc.scalar.activation(raw[:, n, :], picks(t, n, b, 1), COPY)
-            nc.vector.tensor_tensor(wide[:, :, t, cols], raw[:], gate_rows[:, :, cols], MULT)
-
-        def gated_turns(t, number):
-            summed = bank("summed%d" % t, number)
-            for n in range(TERMS):
-                for h in range(2):
-                    nc.tensor.matmul(
-                        summed[:, h * P : (h + 1) * P], wide[:, n, t, h * B : (h + 1) * B], ident[:],
-                        start=(n == 0 and h == 0), stop=(n == TERMS - 1 and h == 1), is_transpose=True,
-                    )
-            return summed
-
-        def gated_back(t, summed, into, tag=None):
-            turned = sb("turned_v%d" % t, [P, 2 * P], F32, tag)
-            nc.scalar.copy(out=turned[:], in_=summed[:, : 2 * P])
-            for h in range(2):
-                nc.tensor.transpose(into[:, h * B : (h + 1) * B], turned[:, h * P : (h + 1) * P], ident[:])
-
-        def plain_gathers(t, b, blocks, numbers, tag=None):
-            terms = sb("terms%d%d" % (t, b), [P, TERMS, blocks * B], F32, tag)
-            apart = [bank("apart%d%d%d" % (t, b, h), numbers[h]) for h in range(blocks)]
-            for n in range(TERMS):
-                nc.scalar.activation(terms[:, n, :], picks(t, n, b, blocks), COPY)
-                for h in range(blocks):
-                    nc.tensor.transpose(apart[h][:, n * P : (n + 1) * P], terms[:, n, h * B : (h + 1) * B], ident[:])
+        def plain_gathers(n, tiles, b, number, tag):
+            terms = sb("terms%d%d" % (n, b), [P, len(tiles), B], F32, tag)
+            apart = bank("apart%d%d" % (n, b), number)
+            for k, t in enumerate(tiles):
+                nc.scalar.activation(terms[:, k, :], picks(t, n, b, 1), COPY)
+                nc.tensor.transpose(apart[:, k * P : (k + 1) * P], terms[:, k, :], ident[:])
             return apart
 
-        def plain_sums(t, b, apart, into, tag=None):
-            turned = sb("turned%d%d" % (t, b), [P, TERMS, P], F32, tag)
-            for n in range(TERMS):
-                nc.scalar.activation(
-                    turned[:, n, :], apart[:, n * P : (n + 1) * P], COPY, scale=gate_cols[n][:, b : b + 1]
-                )
-            for n in range(TERMS):
+        def plain_sums(n, tiles, b, apart, into):
+            count = len(tiles)
+            turned = sb("turned%d%d" % (n, b), [P, count * P], F32, "turned%d%d" % (n, b))
+            nc.scalar.activation(turned[:], apart[:, : count * P], COPY, scale=gate_cols[n][:, b : b + 1])
+            for k in range(count):
                 nc.tensor.matmul(
-                    into, turned[:, n, :], ident[:],
-                    start=(n == 0), stop=(n == TERMS - 1), is_transpose=True,
+                    into[:, k * B : (k + 1) * B], turned[:, k * P : (k + 1) * P], ident[:],
+                    start=(n == 0 and k == 0), stop=(n == TERMS - 1 and k == count - 1), is_transpose=True,
                 )
 
         def square(b, tag=None):
@@ -269,12 +243,24 @@ def tile_picked_ace8_none_po_kernel(
             nc.scalar.activation(sq[:].rearrange("p (c i) t -> p c t i", i=4), lines_of(b), SQUARE)
             return sq
 
-        def orders_from_planes(b, sq, ring):
-            zi = sb("zi%d" % b, [P, 2, B, PACK], BF16, ring)
-            nc.vector.tensor_tensor(
-                zi[:, 0].rearrange("p (c i) t -> p c t i", i=4), lines_of(b),
-                first[:].unsqueeze(1).unsqueeze(3).broadcast_to([P, B // 4, PACK, 4]), MULT,
+        def first_by_scalar(b, zi, source):
+            flat = sb("flat%d" % b, [P, PACK, B], BF16)
+            for t in range(PACK):
+                nc.scalar.activation(flat[:, t, :], source[:, t, :], COPY, scale=first[:, t : t + 1])
+            nc.vector.tensor_copy(
+                out=zi[:, 0].rearrange("p (c i) t -> p c t i", i=4),
+                in_=flat[:].rearrange("p t (c i) -> p c t i", i=4),
             )
+
+        def orders_from_planes(b, sq, ring, on_scalar=False):
+            zi = sb("zi%d" % b, [P, 2, B, PACK], BF16, ring)
+            if on_scalar:
+                first_by_scalar(b, zi, total[:, :, (b - 1) * B : b * B])
+            else:
+                nc.vector.tensor_tensor(
+                    zi[:, 0].rearrange("p (c i) t -> p c t i", i=4), lines_of(b),
+                    first[:].unsqueeze(1).unsqueeze(3).broadcast_to([P, B // 4, PACK, 4]), MULT,
+                )
             signed(zi, sq)
             return zi
 
@@ -349,42 +335,34 @@ def tile_picked_ace8_none_po_kernel(
                 in_=res_i[:].rearrange("p j t -> p (j t)"),
             )
 
-        gated_gathers(0, 1)
-        s1 = plain_gathers(1, 1, 2, (1, 3), "ring_b")
-        u1 = plain_gathers(1, 0, 1, (2,), "ring_a")
+        for t in range(PACK):
+            gated_gathers(t, 2 if t in (1, 3) else 1)
         shared = bank("shared", 5)
-        plain_sums(1, 1, s1[0], shared[:, :B])
-        plain_sums(1, 2, s1[1], shared[:, B : 2 * B])
-        u0 = plain_gathers(0, 0, 1, (0,), "ring_b")
-        nc.scalar.copy(out=total[:, 1, : 2 * B], in_=shared[:, : 2 * B])
-        gated_gathers(2, 1)
-        gated_gathers(3, 1)
-        gated_gathers(1, 3)
-        plain_sums(1, 0, u1[0], sums_of(0)[:, B : 2 * B])
-        u2 = plain_gathers(2, 0, 1, (1,), "ring_a")
-        plain_sums(0, 0, u0[0], sums_of(0)[:, :B])
-        u3 = plain_gathers(3, 0, 1, (3,), "ring_b")
-        plain_sums(2, 0, u2[0], sums_of(0)[:, 2 * B : 3 * B])
-        plain_sums(3, 0, u3[0], sums_of(0)[:, 3 * B :])
-        warm_ps = bank("warm_ps", 3)
-        for i in range(6):
-            nc.tensor.matmul_mx(out=warm_ps[:, i % 2 * HALF : (i % 2 + 1) * HALF], lhsT=w1_rest[:, :P].bitcast(FP8X4), lhsT_scale=s1_rest[:, :P], rhs=xg_w[i % 2][:].bitcast(FP8X4), rhs_scale=xg_s[i % 2][:], start=True, stop=True)
-        deal_bytes(s23, s_raw, 0, 4)
+        groups = [(n, (1, 3), 1, shared) for n in range(TERMS)] + [(n, (0, 1, 2, 3), 0, sums_of(0)) for n in range(TERMS)]
+        turning = []
+        for i, (n, tiles, b, into) in enumerate(groups):
+            turning.append((n, tiles, b, plain_gathers(n, tiles, b, 1 + i % 3, "ring%d" % (i % 2)), into))
+            if i > 0:
+                plain_sums(*turning[i - 1])
+            if i == TERMS:
+                nc.scalar.copy(out=total[:, slice(1, 4, 2), :B], in_=shared[:, : 2 * B].rearrange("p (t j) -> p t j", j=B))
+        plain_sums(*turning[-1])
         added(slice(0, 4), slice(2 * B, 3 * B), "pair3")
-        added(slice(0, 1), slice(0, 2 * B), "pair0")
-        added(slice(2, 4), slice(0, 2 * B), "pair2")
-        z3 = orders_from_planes(3, square_planes(3, "ring_b"), "ring_z0")
-        z1 = orders_from_planes(1, square_planes(1), "ring_z1")
-        oa = multiply(3, z3, 6)
-        z2 = orders_from_planes(2, square_planes(2), "ring_z0")
-        ob = multiply(1, z1, 7)
+        deal_bytes(s23, s_raw, 0, 4)
+        za = orders_from_planes(3, square_planes(3, "ring0"), "ring_z0")
+        oa = multiply(3, za, 6)
+        added(slice(0, 4), slice(B, 2 * B), "pair2")
+        added(slice(0, 3, 2), slice(0, B), "pair1")
+        zb = orders_from_planes(2, square_planes(2, "turned10"), "ring_z1")
+        ob = multiply(2, zb, 7)
+        zc = orders_from_planes(1, square_planes(1), "ring_z0", False)
+        oc = multiply(1, zc, 5)
         z0 = orders(0, square(0), "ring_z1")
-        oc = multiply(2, z2, 5)
         leave(3, oa)
-        leave(1, ob)
-        leave(2, oc)
+        leave(2, ob)
+        leave(1, oc)
         nc.sync.dma_start(out=out_words[:, B:], in_=out_codes[:, B:].bitcast(I32))
-        last_block(0, z0, (0, 2))
+        last_block(0, z0, (0, 1))
         nc.sync.dma_start(out=out_words[:, :B], in_=out_codes[:, :B].bitcast(I32))
         for q in range(4):
             queue = nc.sync if q % 2 == 0 else nc.scalar

@@ -190,6 +190,13 @@ def tile_picked_ace8_none_po_kernel(
                     wide[:, n, t, cols], picks(t, n, first_block, BLOCKS - first_block), gates[n][:, cols], MULT
                 )
 
+        def raw_gathers(t, b, tag):
+            raw = sb("raw", [P, TERMS, B], F32, tag)
+            cols = slice((b - 1) * B, b * B)
+            for n in range(TERMS):
+                nc.scalar.activation(raw[:, n, :], picks(t, n, b, 1), COPY)
+            nc.vector.tensor_tensor(wide[:, :, t, cols], raw[:], gate_rows[:, :, cols], MULT)
+
         def plain_gathers(n, tiles, b, number, tag):
             terms = sb("terms%d%d" % (n, b), [P, len(tiles), B], F32, tag)
             apart = bank("apart%d%d" % (n, b), number)
@@ -336,7 +343,7 @@ def tile_picked_ace8_none_po_kernel(
             )
 
         for t in range(PACK):
-            gated_gathers(t, 2 if t in (1, 3) else 1)
+            gated_gathers(t, (1, 2, 1, 3)[t])
         shared = bank("shared", 5)
         groups = [(n, (1, 3), 1, shared) for n in range(TERMS)] + [(n, (0, 1, 2, 3), 0, sums_of(0)) for n in range(TERMS)]
         turning = []
@@ -351,6 +358,7 @@ def tile_picked_ace8_none_po_kernel(
         deal_bytes(s23, s_raw, 0, 4)
         za = orders_from_planes(3, square_planes(3, "ring0"), "ring_z0")
         oa = multiply(3, za, 6)
+        raw_gathers(3, 2, None)
         added(slice(0, 4), slice(B, 2 * B), "pair2")
         added(slice(0, 3, 2), slice(0, B), "pair1")
         zb = orders_from_planes(2, square_planes(2, "turned10"), "ring_z1")

@@ -16,9 +16,10 @@ FP8X4 = mybir.dt.float8_e4m3fn_x4
 MULT = mybir.AluOpType.mult
 ADD = mybir.AluOpType.add
 MAX = mybir.AluOpType.max
-MIN = mybir.AluOpType.min
 COPY = mybir.ActivationFunctionType.Copy
 SQRT = mybir.ActivationFunctionType.Sqrt
+IDENTITY = mybir.ActivationFunctionType.Identity
+SIGN = mybir.ActivationFunctionType.Sign
 SQUARE = mybir.ActivationFunctionType.Square
 
 P = 128
@@ -36,6 +37,7 @@ def tile_picked_ace8_none_po_kernel(
     nc = tc.nc
     with ExitStack() as ctx:
         keep = ctx.enter_context(tc.tile_pool(name="keep", bufs=1))
+        laid = ctx.enter_context(tc.tile_pool(name="laid", bufs=1))
         psum = ctx.enter_context(tc.psum_pool(name="psum", bufs=1))
 
         def sb(name, shape, dtype, tag=None):
@@ -54,9 +56,9 @@ def tile_picked_ace8_none_po_kernel(
                     in_=src[0, 4 * q : 4 * q + 4, :].bitcast(I32),
                 )
 
-        def deal(dst, src, t0, t1):
-            nc.vector.tensor_copy(
-                out=dst[:].rearrange("p (t c i) -> p c t i", t=t1 - t0, i=4),
+        def deal(move, dst, src, t0, t1):
+            move(
+                out=dst.rearrange("p (t c i) -> p c t i", t=t1 - t0, i=4),
                 in_=src.rearrange("p (c i t) -> p c t i", t=PACK, i=4)[:, :, t0:t1, :],
             )
 
@@ -70,73 +72,75 @@ def tile_picked_ace8_none_po_kernel(
         lists = [sb("list%d" % n, [P, S // 16], U16) for n in range(TERMS)]
         xw = sb("xw", [P, T], I32)
         xs = sb("xs", [P, T], U8)
+        xs_raw = laid.tile([P, T], U8, name="xs_raw", offset=1024)
         w1_raw = sb("w1_raw", [P, H], I32)
         s1_raw = sb("s1_raw", [P, H], U8)
-        c1_sb = sb("c1_sb", [P, PACK], F32)
         c2_sb = sb("c2_sb", [P, PACK], F32)
         ident = sb("ident", [P, P], F32)
 
-        nc.vector.memset(xs[:].bitcast(I32), 0)
-        nc.vector.memset(s1_raw[:].bitcast(I32), 0)
-        nc.scalar.dma_start(out=c2_sb[:], in_=c2.rearrange("(p t) o -> p (t o)", t=PACK))
-        nc.scalar.dma_start(out=c1_sb[:], in_=c1.rearrange("(p t) o -> p (t o)", t=PACK))
+        nc.sync.dma_start(out=c2_sb[:], in_=c2.rearrange("(p t) o -> p (t o)", t=PACK))
+        load_scales([nc.scalar] * 2 + [nc.sync] * 2, xs_raw, 0, x_scales)
         nc.sync.dma_start(offs_sb[:], offs)
-        for n, p in enumerate((p1, p2, p3)):
-            nc.sync.dma_start(lists[n][:], p)
+        nc.sync.dma_start(lists[0][:], p1)
         nc.sync.dma_start(out=xw[:], in_=words_of(x_words))
-        load_scales([nc.sync] * 4, xs, 0, x_scales)
-        load_scales([nc.sync] * 4, s1_raw, 0, w1_scales)
+        nc.sync.dma_start(lists[1][:], p2)
+        nc.sync.dma_start(lists[2][:], p3)
         nc.sync.dma_start(out=w1_raw[:], in_=words_of(w1_words))
+        nc.vector.memset(s1_raw[:].bitcast(I32), 0)
+        nc.vector.memset(xs[:].bitcast(I32), 0)
+        load_scales([nc.sync] * 4, s1_raw, 0, w1_scales)
         make_identity(nc, ident[:])
 
         def small(name, dtype=F32):
             return sb(name, [P, PACK], dtype)
 
-        size, held, guess, inv_guess, other, twice, root, inv_held = (
-            small(name) for name in ("size", "held", "guess", "inv_guess", "other", "twice", "root", "inv_held")
-        )
+        size, guess, inv_guess, twice = (small(name) for name in ("size", "guess", "inv_guess", "twice"))
         first, sign = small("first"), small("sign", BF16)
         nc.vector.scalar_tensor_tensor(size[:], c2_sb[:], -1.0, c2_sb[:], MULT, MAX)
-        nc.vector.tensor_scalar(held[:], size[:], 2.0**-100, 2.0**100, MAX, MIN)
-        nc.scalar.activation(guess[:], held[:], SQRT)
-        nc.vector.reciprocal(inv_held[:], held[:])
-        nc.vector.tensor_tensor(sign[:], c2_sb[:], inv_held[:], MULT)
+        nc.scalar.activation(guess[:], size[:], SQRT, bias=2.0**-100)
         nc.vector.reciprocal(inv_guess[:], guess[:])
-        nc.vector.tensor_tensor(other[:], held[:], inv_guess[:], MULT)
-        nc.vector.tensor_tensor(twice[:], other[:], guess[:], ADD)
-        nc.vector.tensor_scalar(root[:], twice[:], 0.5, None, MULT)
-        w23_raw = sb("w23_raw", [P, 2, H], I32, "size")
-        nc.sync.dma_start(out=w23_raw[:, 0, :], in_=words_of(w2_words))
-        nc.sync.dma_start(out=w23_raw[:, 1, :], in_=words_of(w3_words))
-
-        xg_w = [sb("xg_w%d" % h, [P, HALF], U32) for h in range(2)]
-        xg_s = [sb("xg_s%d" % h, [P, HALF], U8) for h in range(2)]
-        w1_first = sb("w1_first", [P, P], I32)
-        s1_first, s1_rest = sb("s1_first", [P, P], U8), sb("s1_rest", [P, H - P], U8)
-        w_dealt = [sb("w_dealt%d" % i, [P, N], I32) for i in range(2)]
-        picked = [offs_sb[:, h * HALF // 16 : (h + 1) * HALF // 16] for h in range(2)]
-        for h in range(2):
-            nc.vector.tensor_copy(out=xg_w[h][:], in_=xw[:].bitcast(U32).indirect(picked[h]))
-        deal(w1_first, w1_raw[:], 0, 1)
-        for h in range(2):
-            nc.vector.tensor_copy(out=xg_s[h][:], in_=xs[:].indirect(picked[h]))
-        deal_bytes(s1_first, s1_raw, 0, 1)
-        deal_bytes(s1_rest, s1_raw, 1, PACK)
-        w1_rest = sb("w1_rest", [P, H - P], I32, "s1_raw")
-        deal(w1_rest, w1_raw[:], 1, PACK)
-        gate_rows = sb("gate_rows", [P, TERMS, S - B], F32, "xw")
+        for t in range(PACK):
+            col = slice(t, t + 1)
+            nc.scalar.activation(twice[:, col], inv_guess[:, col], IDENTITY, bias=guess[:, col], scale=size[:, col])
+        nc.scalar.activation(sign[:], c2_sb[:], SIGN, scale=guess[:, 0:1])
+        for q in range(4):
+            rows = slice(32 * q, 32 * q + 4)
+            nc.vector.tensor_copy(out=xs[rows, :].bitcast(I32), in_=xs_raw[rows, :].bitcast(I32))
+        w2_raw = laid.tile([P, N], I32, name="w2_raw", offset=0)
+        nc.sync.dma_start(out=w2_raw[:], in_=words_of(w2_words))
+        gate_rows = laid.tile([P, TERMS, S - B], F32, name="gate_rows", offset=2048)
         gates = [gate_rows[:, n, :] for n in range(TERMS)]
         for n, g in enumerate((g1, g2, g3)):
             nc.sync.dma_start(out=gates[n], in_=g[:, B:])
-        deal(w_dealt[0], w23_raw[:, 0, :], 0, PACK)
-        deal(w_dealt[1], w23_raw[:, 1, :], 0, PACK)
-        gate_tile = sb("gate_tile", [P, TERMS, 8], F32, "xs")
+
+        xg_s = sb("xg_s", [P, S], U8)
+        nc.vector.tensor_copy(out=xg_s[:], in_=xs[:].indirect(offs_sb[:]))
+        xg_w = sb("xg_w", [P, S], U32)
+        w1_first, w1_rest = sb("w1_first", [P, P], U32), sb("w1_rest", [P, H - P], U32)
+        s1_first = sb("s1_first", [P, P], U8)
+        for h in range(2):
+            nc.vector.tensor_copy(
+                out=xg_w[:, h * HALF : (h + 1) * HALF],
+                in_=xw[:].bitcast(U32).indirect(offs_sb[:, h * HALF // 16 : (h + 1) * HALF // 16]),
+            )
+        deal(nc.scalar.copy, w1_first[:], w1_raw[:].bitcast(U32), 0, 1)
+        deal(nc.scalar.copy, w1_rest[:], w1_raw[:].bitcast(U32), 1, PACK)
+        deal_bytes(s1_first, s1_raw, 0, 1)
+        s1_rest = sb("s1_rest", [P, H - P], U8)
+        deal_bytes(s1_rest, s1_raw, 1, PACK)
+        w3_raw = sb("w3_raw", [P, N], I32, "xs")
+        nc.sync.dma_start(out=w3_raw[:], in_=words_of(w3_words))
+        w_dealt = [sb("w_dealt%d" % z, [P, N], I32, ("s1_raw", "xg_w")[z]) for z in range(2)]
+        deal(nc.vector.tensor_copy, w_dealt[0][:], w2_raw[:], 0, PACK)
+        gate_tile = sb("gate_tile", [P, TERMS, 8], F32, "w1_raw")
         gate_cols = [gate_tile[:, n, :2] for n in range(TERMS)]
         for n, g in enumerate((g1, g2, g3)):
             nc.sync.dma_start(
                 out=gate_cols[n], in_=g[0, : 2 * B].rearrange("(b p) -> p b", p=P), allow_slow_non_contiguous=True
             )
-        s_raw = sb("s_raw", [P, N], U8, "w1_raw")
+        c1_sb = sb("c1_sb", [P, PACK], F32, "size")
+        nc.sync.dma_start(out=c1_sb[:], in_=c1.rearrange("(p t) o -> p (t o)", t=PACK))
+        s_raw = sb("s_raw", [P, N], U8, "xw")
         nc.gpsimd.memset(s_raw[:].bitcast(I32), 0)
         load_scales([nc.sync] * 4, s_raw, 0, w2_scales)
         load_scales([nc.sync] * 4, s_raw, 4, w3_scales)
@@ -146,23 +150,18 @@ def tile_picked_ace8_none_po_kernel(
             y_t = sb("y%d" % t, [P, S], F32)
             rest = slice((t - 1) * P, t * P)
             w1_t, s1_t = (w1_first[:], s1_first[:]) if t == 0 else (w1_rest[:, rest], s1_rest[:, rest])
-            y_ps = bank("y_ps%d" % t, t)
-            for h in range(2):
-                cols = slice(h * HALF, (h + 1) * HALF)
-                if t == 0 and h == 1:
-                    y_ps = bank("y_ps0_late", 4)
+            for h, cols in enumerate([slice(0, HALF), slice(HALF, S)] if t == 0 else [slice(0, S)]):
+                y_ps = bank("y_ps%d%d" % (t, h), 4 if h == 1 else t)
                 nc.tensor.matmul_mx(
                     out=y_ps[:, cols], lhsT=w1_t.bitcast(FP8X4), lhsT_scale=s1_t,
-                    rhs=xg_w[h][:].bitcast(FP8X4), rhs_scale=xg_s[h][:], start=True, stop=True,
+                    rhs=xg_w[:, cols].bitcast(FP8X4), rhs_scale=xg_s[:, cols], start=True, stop=True,
                 )
-                if t == 0:
-                    nc.scalar.activation(y_t[:, cols], y_ps[:, cols], COPY, scale=root[:, t : t + 1])
-            if t > 0:
-                nc.scalar.activation(y_t[:], y_ps[:], COPY, scale=root[:, t : t + 1])
+                nc.scalar.activation(y_t[:, cols], y_ps[:, cols], COPY, scale=twice[:, t : t + 1])
             y.append(y_t)
 
+        deal(nc.vector.tensor_copy, w_dealt[1][:], w3_raw[:], 0, PACK)
         inv_root = sb("inv_root", [P, PACK], F32, "w1_first")
-        nc.vector.reciprocal(inv_root[:], root[:])
+        nc.vector.reciprocal(inv_root[:], twice[:])
         nc.vector.tensor_tensor(first[:], c1_sb[:], inv_root[:], MULT)
 
         out_codes = sb("out_codes", [P, S], U32)
@@ -190,8 +189,8 @@ def tile_picked_ace8_none_po_kernel(
                     wide[:, n, t, cols], picks(t, n, first_block, BLOCKS - first_block), gates[n][:, cols], MULT
                 )
 
-        def raw_gathers(t, b, tag):
-            raw = sb("raw", [P, TERMS, B], F32, tag)
+        def raw_gathers(t, b):
+            raw = sb("raw%d%d" % (t, b), [P, TERMS, B], F32)
             cols = slice((b - 1) * B, b * B)
             for n in range(TERMS):
                 nc.scalar.activation(raw[:, n, :], picks(t, n, b, 1), COPY)
@@ -217,7 +216,7 @@ def tile_picked_ace8_none_po_kernel(
 
         def square(b, tag=None):
             sq = sb("sq%d" % b, [P, B, PACK], BF16, tag)
-            nc.scalar.activation(sq[:], a_ps[b][:].rearrange("p (t j) -> p j t", t=PACK), SQUARE)
+            nc.scalar.activation(sq[:], a_ps[b][:].rearrange("p (t j) -> p j t", t=PACK), SQUARE, scale=0.5)
             return sq
 
         def signed(zi, sq):
@@ -247,28 +246,15 @@ def tile_picked_ace8_none_po_kernel(
 
         def square_planes(b, tag=None):
             sq = sb("sq%d" % b, [P, B, PACK], BF16, tag)
-            nc.scalar.activation(sq[:].rearrange("p (c i) t -> p c t i", i=4), lines_of(b), SQUARE)
+            nc.scalar.activation(sq[:].rearrange("p (c i) t -> p c t i", i=4), lines_of(b), SQUARE, scale=0.5)
             return sq
 
-        def first_by_scalar(b, zi, source):
-            flat = sb("flat%d" % b, [P, PACK, B], BF16)
-            for t in range(PACK):
-                nc.scalar.activation(flat[:, t, :], source[:, t, :], COPY, scale=first[:, t : t + 1])
-            nc.vector.tensor_copy(
-                out=zi[:, 0].rearrange("p (c i) t -> p c t i", i=4),
-                in_=flat[:].rearrange("p t (c i) -> p c t i", i=4),
+        def first_from_planes(b):
+            zi = sb("zi%d" % b, [P, 2, B, PACK], BF16)
+            nc.vector.tensor_tensor(
+                zi[:, 0].rearrange("p (c i) t -> p c t i", i=4), lines_of(b),
+                first[:].unsqueeze(1).unsqueeze(3).broadcast_to([P, B // 4, PACK, 4]), MULT,
             )
-
-        def orders_from_planes(b, sq, ring, on_scalar=False):
-            zi = sb("zi%d" % b, [P, 2, B, PACK], BF16, ring)
-            if on_scalar:
-                first_by_scalar(b, zi, total[:, :, (b - 1) * B : b * B])
-            else:
-                nc.vector.tensor_tensor(
-                    zi[:, 0].rearrange("p (c i) t -> p c t i", i=4), lines_of(b),
-                    first[:].unsqueeze(1).unsqueeze(3).broadcast_to([P, B // 4, PACK, 4]), MULT,
-                )
-            signed(zi, sq)
             return zi
 
         def multiply(b, zi, number):
@@ -354,18 +340,18 @@ def tile_picked_ace8_none_po_kernel(
             if i == TERMS:
                 nc.scalar.copy(out=total[:, slice(1, 4, 2), :B], in_=shared[:, : 2 * B].rearrange("p (t j) -> p t j", j=B))
         plain_sums(*turning[-1])
-        added(slice(0, 4), slice(2 * B, 3 * B), "pair3")
-        deal_bytes(s23, s_raw, 0, 4)
-        za = orders_from_planes(3, square_planes(3, "ring0"), "ring_z0")
-        oa = multiply(3, za, 6)
-        raw_gathers(3, 2, None)
-        added(slice(0, 4), slice(B, 2 * B), "pair2")
+        raw_gathers(3, 2)
+        added(slice(0, 4), slice(B, 3 * B), "pair23")
         added(slice(0, 3, 2), slice(0, B), "pair1")
-        zb = orders_from_planes(2, square_planes(2, "turned10"), "ring_z1")
-        ob = multiply(2, zb, 7)
-        zc = orders_from_planes(1, square_planes(1), "ring_z0", False)
-        oc = multiply(1, zc, 5)
-        z0 = orders(0, square(0), "ring_z1")
+        zi = {b: first_from_planes(b) for b in (3, 2, 1)}
+        deal_bytes(s23, s_raw, 0, 4)
+        sq = {b: square_planes(b, tag) for b, tag in ((3, "ring1"), (2, "turned10"), (1, "turned20"))}
+        products = []
+        for b, number in ((3, 6), (2, 7), (1, 5)):
+            signed(zi[b], sq[b])
+            products.append(multiply(b, zi[b], number))
+        oa, ob, oc = products
+        z0 = orders(0, square(0))
         leave(3, oa)
         leave(2, ob)
         leave(1, oc)

@@ -37,7 +37,6 @@ def tile_picked_ace8_none_po_kernel(
     nc = tc.nc
     with ExitStack() as ctx:
         keep = ctx.enter_context(tc.tile_pool(name="keep", bufs=1))
-        laid = ctx.enter_context(tc.tile_pool(name="laid", bufs=1))
         psum = ctx.enter_context(tc.psum_pool(name="psum", bufs=1))
 
         def sb(name, shape, dtype, tag=None):
@@ -64,7 +63,7 @@ def tile_picked_ace8_none_po_kernel(
 
         def deal_bytes(dst, src, t0, t1):
             nc.vector.tensor_copy(
-                out=dst[:].rearrange("p (t m) -> p m t", t=t1 - t0),
+                out=dst.rearrange("p (t m) -> p m t", t=t1 - t0),
                 in_=src[:].rearrange("p (m t) -> p m t", t=PACK)[:, :, t0:t1],
             )
 
@@ -72,75 +71,70 @@ def tile_picked_ace8_none_po_kernel(
         lists = [sb("list%d" % n, [P, S // 16], U16) for n in range(TERMS)]
         xw = sb("xw", [P, T], I32)
         xs = sb("xs", [P, T], U8)
-        xs_raw = laid.tile([P, T], U8, name="xs_raw", offset=1024)
+        c1_sb = sb("c1_sb", [P, PACK], F32)
         w1_raw = sb("w1_raw", [P, H], I32)
         s1_raw = sb("s1_raw", [P, H], U8)
         c2_sb = sb("c2_sb", [P, PACK], F32)
         ident = sb("ident", [P, P], F32)
 
-        nc.sync.dma_start(out=c2_sb[:], in_=c2.rearrange("(p t) o -> p (t o)", t=PACK))
-        load_scales([nc.scalar] * 2 + [nc.sync] * 2, xs_raw, 0, x_scales)
-        nc.sync.dma_start(offs_sb[:], offs)
-        nc.sync.dma_start(lists[0][:], p1)
-        nc.sync.dma_start(out=xw[:], in_=words_of(x_words))
-        nc.sync.dma_start(lists[1][:], p2)
-        nc.sync.dma_start(lists[2][:], p3)
-        nc.sync.dma_start(out=w1_raw[:], in_=words_of(w1_words))
-        nc.vector.memset(s1_raw[:].bitcast(I32), 0)
         nc.vector.memset(xs[:].bitcast(I32), 0)
+        nc.vector.memset(s1_raw[:].bitcast(I32), 0)
+        nc.scalar.dma_start(out=c2_sb[:], in_=c2.rearrange("(p t) o -> p (t o)", t=PACK))
+        nc.scalar.dma_start(out=c1_sb[:], in_=c1.rearrange("(p t) o -> p (t o)", t=PACK))
+        nc.sync.dma_start(offs_sb[:], offs)
+        for n, p in enumerate((p1, p2, p3)):
+            nc.sync.dma_start(lists[n][:], p)
+        nc.sync.dma_start(out=xw[:], in_=words_of(x_words))
+        load_scales([nc.sync] * 4, xs, 0, x_scales)
         load_scales([nc.sync] * 4, s1_raw, 0, w1_scales)
+        nc.sync.dma_start(out=w1_raw[:], in_=words_of(w1_words))
         make_identity(nc, ident[:])
 
         def small(name, dtype=F32):
             return sb(name, [P, PACK], dtype)
 
         size, guess, inv_guess, twice = (small(name) for name in ("size", "guess", "inv_guess", "twice"))
-        first, sign = small("first"), small("sign", BF16)
+        first, sign = small("first"), sb("sign", [P, B, PACK], BF16)
         nc.vector.scalar_tensor_tensor(size[:], c2_sb[:], -1.0, c2_sb[:], MULT, MAX)
         nc.scalar.activation(guess[:], size[:], SQRT, bias=2.0**-100)
         nc.vector.reciprocal(inv_guess[:], guess[:])
         for t in range(PACK):
             col = slice(t, t + 1)
             nc.scalar.activation(twice[:, col], inv_guess[:, col], IDENTITY, bias=guess[:, col], scale=size[:, col])
-        nc.scalar.activation(sign[:], c2_sb[:], SIGN, scale=guess[:, 0:1])
-        for q in range(4):
-            rows = slice(32 * q, 32 * q + 4)
-            nc.vector.tensor_copy(out=xs[rows, :].bitcast(I32), in_=xs_raw[rows, :].bitcast(I32))
-        w2_raw = laid.tile([P, N], I32, name="w2_raw", offset=0)
-        nc.sync.dma_start(out=w2_raw[:], in_=words_of(w2_words))
-        gate_rows = laid.tile([P, TERMS, S - B], F32, name="gate_rows", offset=2048)
-        gates = [gate_rows[:, n, :] for n in range(TERMS)]
-        for n, g in enumerate((g1, g2, g3)):
-            nc.sync.dma_start(out=gates[n], in_=g[:, B:])
+        nc.scalar.activation(sign[:], c2_sb[:].unsqueeze(1).broadcast_to([P, B, PACK]), SIGN, scale=guess[:, 0:1])
+        w23_raw = sb("w23_raw", [P, 2, H], I32, "size")
+        nc.sync.dma_start(out=w23_raw[:, 0, :], in_=words_of(w2_words))
+        nc.sync.dma_start(out=w23_raw[:, 1, :], in_=words_of(w3_words))
 
-        xg_s = sb("xg_s", [P, S], U8)
-        nc.vector.tensor_copy(out=xg_s[:], in_=xs[:].indirect(offs_sb[:]))
-        xg_w = sb("xg_w", [P, S], U32)
+        xg_w, xg_s = sb("xg_w", [P, S], U32), sb("xg_s", [P, S], U8)
         w1_first, w1_rest = sb("w1_first", [P, P], U32), sb("w1_rest", [P, H - P], U32)
-        s1_first = sb("s1_first", [P, P], U8)
         for h in range(2):
             nc.vector.tensor_copy(
                 out=xg_w[:, h * HALF : (h + 1) * HALF],
                 in_=xw[:].bitcast(U32).indirect(offs_sb[:, h * HALF // 16 : (h + 1) * HALF // 16]),
             )
+        nc.vector.tensor_copy(out=xg_s[:], in_=xs[:].indirect(offs_sb[:]))
         deal(nc.scalar.copy, w1_first[:], w1_raw[:].bitcast(U32), 0, 1)
         deal(nc.scalar.copy, w1_rest[:], w1_raw[:].bitcast(U32), 1, PACK)
+        s1_dealt = sb("s1_dealt", [P, H], U8)
+        s1_first, s1_rest = s1_dealt[:, :P], s1_dealt[:, P:]
         deal_bytes(s1_first, s1_raw, 0, 1)
-        s1_rest = sb("s1_rest", [P, H - P], U8)
         deal_bytes(s1_rest, s1_raw, 1, PACK)
-        w3_raw = sb("w3_raw", [P, N], I32, "xs")
-        nc.sync.dma_start(out=w3_raw[:], in_=words_of(w3_words))
-        w_dealt = [sb("w_dealt%d" % z, [P, N], I32, ("s1_raw", "xg_w")[z]) for z in range(2)]
-        deal(nc.vector.tensor_copy, w_dealt[0][:], w2_raw[:], 0, PACK)
-        gate_tile = sb("gate_tile", [P, TERMS, 8], F32, "w1_raw")
+        gate_rows = sb("gate_rows", [P, TERMS, S - B], F32, "xw")
+        gates = [gate_rows[:, n, :] for n in range(TERMS)]
+        for n, g in enumerate((g1, g2, g3)):
+            nc.sync.dma_start(out=gates[n], in_=g[:, B:])
+        w_both = sb("w_both", [P, 2, N], I32, "s1_raw")
+        w_dealt = [w_both[:, z, :] for z in range(2)]
+        for z in range(2):
+            deal(nc.vector.tensor_copy, w_dealt[z], w23_raw[:, z, :], 0, PACK)
+        gate_tile = sb("gate_tile", [P, TERMS, 8], F32, "xs")
         gate_cols = [gate_tile[:, n, :2] for n in range(TERMS)]
         for n, g in enumerate((g1, g2, g3)):
             nc.sync.dma_start(
                 out=gate_cols[n], in_=g[0, : 2 * B].rearrange("(b p) -> p b", p=P), allow_slow_non_contiguous=True
             )
-        c1_sb = sb("c1_sb", [P, PACK], F32, "size")
-        nc.sync.dma_start(out=c1_sb[:], in_=c1.rearrange("(p t) o -> p (t o)", t=PACK))
-        s_raw = sb("s_raw", [P, N], U8, "xw")
+        s_raw = sb("s_raw", [P, N], U8, "w1_raw")
         nc.gpsimd.memset(s_raw[:].bitcast(I32), 0)
         load_scales([nc.sync] * 4, s_raw, 0, w2_scales)
         load_scales([nc.sync] * 4, s_raw, 4, w3_scales)
@@ -149,7 +143,7 @@ def tile_picked_ace8_none_po_kernel(
         for t in range(PACK):
             y_t = sb("y%d" % t, [P, S], F32)
             rest = slice((t - 1) * P, t * P)
-            w1_t, s1_t = (w1_first[:], s1_first[:]) if t == 0 else (w1_rest[:, rest], s1_rest[:, rest])
+            w1_t, s1_t = (w1_first[:], s1_first) if t == 0 else (w1_rest[:, rest], s1_rest[:, rest])
             for h, cols in enumerate([slice(0, HALF), slice(HALF, S)] if t == 0 else [slice(0, S)]):
                 y_ps = bank("y_ps%d%d" % (t, h), 4 if h == 1 else t)
                 nc.tensor.matmul_mx(
@@ -159,7 +153,6 @@ def tile_picked_ace8_none_po_kernel(
                 nc.scalar.activation(y_t[:, cols], y_ps[:, cols], COPY, scale=twice[:, t : t + 1])
             y.append(y_t)
 
-        deal(nc.vector.tensor_copy, w_dealt[1][:], w3_raw[:], 0, PACK)
         inv_root = sb("inv_root", [P, PACK], F32, "w1_first")
         nc.vector.reciprocal(inv_root[:], twice[:])
         nc.vector.tensor_tensor(first[:], c1_sb[:], inv_root[:], MULT)
@@ -220,7 +213,7 @@ def tile_picked_ace8_none_po_kernel(
             return sq
 
         def signed(zi, sq):
-            nc.vector.tensor_tensor(zi[:, 1], sq[:], sign[:].unsqueeze(1).broadcast_to([P, B, PACK]), MULT)
+            nc.vector.tensor_tensor(zi[:, 1], sq[:], sign[:], MULT)
 
         def orders(b, sq, tag=None):
             zi = sb("zi%d" % b, [P, 2, B, PACK], BF16, tag)
@@ -329,22 +322,22 @@ def tile_picked_ace8_none_po_kernel(
             )
 
         for t in range(PACK):
-            gated_gathers(t, (1, 2, 1, 3)[t])
+            gated_gathers(t, (2, 3, 1, 1)[t])
         shared = bank("shared", 5)
-        groups = [(n, (1, 3), 1, shared) for n in range(TERMS)] + [(n, (0, 1, 2, 3), 0, sums_of(0)) for n in range(TERMS)]
+        groups = [(n, (0, 1), 1, shared) for n in range(TERMS)] + [(n, (0, 1, 2, 3), 0, sums_of(0)) for n in range(TERMS)]
         turning = []
         for i, (n, tiles, b, into) in enumerate(groups):
             turning.append((n, tiles, b, plain_gathers(n, tiles, b, 1 + i % 3, "ring%d" % (i % 2)), into))
             if i > 0:
                 plain_sums(*turning[i - 1])
             if i == TERMS:
-                nc.scalar.copy(out=total[:, slice(1, 4, 2), :B], in_=shared[:, : 2 * B].rearrange("p (t j) -> p t j", j=B))
+                nc.scalar.copy(out=total[:, :2, :B], in_=shared[:, : 2 * B].rearrange("p (t j) -> p t j", j=B))
         plain_sums(*turning[-1])
-        raw_gathers(3, 2)
+        raw_gathers(1, 2)
         added(slice(0, 4), slice(B, 3 * B), "pair23")
-        added(slice(0, 3, 2), slice(0, B), "pair1")
+        added(slice(2, 4), slice(0, B), "pair1")
         zi = {b: first_from_planes(b) for b in (3, 2, 1)}
-        deal_bytes(s23, s_raw, 0, 4)
+        deal_bytes(s23[:], s_raw, 0, 4)
         sq = {b: square_planes(b, tag) for b, tag in ((3, "ring1"), (2, "turned10"), (1, "turned20"))}
         products = []
         for b, number in ((3, 6), (2, 7), (1, 5)):

@@ -242,8 +242,8 @@ def tile_picked_ace8_none_po_kernel(
             nc.scalar.activation(sq[:].rearrange("p (c i) t -> p c t i", i=4), lines_of(b), SQUARE, scale=0.5)
             return sq
 
-        def first_from_planes(b):
-            zi = sb("zi%d" % b, [P, 2, B, PACK], BF16)
+        def first_from_planes(b, ring):
+            zi = sb("zi%d" % b, [P, 2, B, PACK], BF16, ring)
             nc.vector.tensor_tensor(
                 zi[:, 0].rearrange("p (c i) t -> p c t i", i=4), lines_of(b),
                 first[:].unsqueeze(1).unsqueeze(3).broadcast_to([P, B // 4, PACK, 4]), MULT,
@@ -271,7 +271,6 @@ def tile_picked_ace8_none_po_kernel(
             return out_ps
 
         def last_block(b, zi, numbers):
-            cols = slice(b * B, (b + 1) * B)
             pairs = [bank("pair_ps%d" % u, numbers[u]) for u in range(2)]
             for z in range(2):
                 codes = sb("last_codes%d" % z, [P, B], U32)
@@ -289,6 +288,10 @@ def tile_picked_ace8_none_po_kernel(
                         start=(z == 0 and t % 2 == 0),
                         stop=(z == 1 and t % 2 == 1),
                     )
+            return pairs
+
+        def leave_last(b, pairs):
+            cols = slice(b * B, (b + 1) * B)
             res = sb("res%d" % b, [P, PACK, B], F32)
             res_i = sb("res_i%d" % b, [P, B, PACK], BF16)
             for u in range(2):
@@ -322,34 +325,38 @@ def tile_picked_ace8_none_po_kernel(
             )
 
         for t in range(PACK):
-            gated_gathers(t, (2, 3, 1, 1)[t])
+            gated_gathers(t, (1, 2, 1, 3)[t])
         shared = bank("shared", 5)
-        groups = [(n, (0, 1), 1, shared) for n in range(TERMS)] + [(n, (0, 1, 2, 3), 0, sums_of(0)) for n in range(TERMS)]
+        groups = [(n, (1, 3), 1, shared) for n in range(TERMS)] + [(n, (0, 1, 2, 3), 0, sums_of(0)) for n in range(TERMS)]
         turning = []
         for i, (n, tiles, b, into) in enumerate(groups):
             turning.append((n, tiles, b, plain_gathers(n, tiles, b, 1 + i % 3, "ring%d" % (i % 2)), into))
             if i > 0:
                 plain_sums(*turning[i - 1])
             if i == TERMS:
-                nc.scalar.copy(out=total[:, :2, :B], in_=shared[:, : 2 * B].rearrange("p (t j) -> p t j", j=B))
+                nc.scalar.copy(out=total[:, slice(1, 4, 2), :B], in_=shared[:, : 2 * B].rearrange("p (t j) -> p t j", j=B))
         plain_sums(*turning[-1])
-        raw_gathers(1, 2)
-        added(slice(0, 4), slice(B, 3 * B), "pair23")
-        added(slice(2, 4), slice(0, B), "pair1")
-        zi = {b: first_from_planes(b) for b in (3, 2, 1)}
+        def finish(b, square_tag, ring, number):
+            sq = square_planes(b, square_tag)
+            zi = first_from_planes(b, ring)
+            signed(zi, sq)
+            return multiply(b, zi, number)
+
+        added(slice(0, 4), slice(2 * B, 3 * B), "pair3")
         deal_bytes(s23[:], s_raw, 0, 4)
-        sq = {b: square_planes(b, tag) for b, tag in ((3, "ring1"), (2, "turned10"), (1, "turned20"))}
-        products = []
-        for b, number in ((3, 6), (2, 7), (1, 5)):
-            signed(zi[b], sq[b])
-            products.append(multiply(b, zi[b], number))
-        oa, ob, oc = products
-        z0 = orders(0, square(0))
+        oa = finish(3, "ring0", "ring_z0", 6)
+        raw_gathers(3, 2)
+        added(slice(0, 4), slice(B, 2 * B), "pair2")
+        added(slice(0, 3, 2), slice(0, B), "pair1")
+        ob = finish(2, "turned10", "ring_z1", 7)
+        oc = finish(1, None, "ring_z0", 5)
+        z0 = orders(0, square(0), "ring_z1")
+        pairs = last_block(0, z0, (0, 1))
         leave(3, oa)
         leave(2, ob)
         leave(1, oc)
         nc.sync.dma_start(out=out_words[:, B:], in_=out_codes[:, B:].bitcast(I32))
-        last_block(0, z0, (0, 1))
+        leave_last(0, pairs)
         nc.sync.dma_start(out=out_words[:, :B], in_=out_codes[:, :B].bitcast(I32))
         for q in range(4):
             queue = nc.sync if q % 2 == 0 else nc.scalar

@@ -25,7 +25,6 @@ SQUARE = mybir.ActivationFunctionType.Square
 P = 128
 PACK = 4
 B = 128
-BLOCKS = S // B
 HALF = S // 2
 TERMS = 3
 
@@ -48,10 +47,10 @@ def tile_picked_ace8_none_po_kernel(
         def words_of(w):
             return w[0].rearrange("p n t -> p (n t)").bitcast(I32)
 
-        def load_scales(queues, tile, first, src):
+        def load_scales(tile, first_row, src):
             for q in range(4):
-                queues[q].dma_start(
-                    out=tile[32 * q + first : 32 * q + first + 4, :].bitcast(I32),
+                nc.sync.dma_start(
+                    out=tile[32 * q + first_row : 32 * q + first_row + 4, :].bitcast(I32),
                     in_=src[0, 4 * q : 4 * q + 4, :].bitcast(I32),
                 )
 
@@ -61,40 +60,55 @@ def tile_picked_ace8_none_po_kernel(
                 in_=src.rearrange("p (c i t) -> p c t i", t=PACK, i=4)[:, :, t0:t1, :],
             )
 
-        def deal_bytes(dst, src, t0, t1):
+        def deal_bytes(dst, src):
             nc.vector.tensor_copy(
-                out=dst.rearrange("p (t m) -> p m t", t=t1 - t0),
-                in_=src[:].rearrange("p (m t) -> p m t", t=PACK)[:, :, t0:t1],
+                out=dst.rearrange("p (t m) -> p t m", t=PACK), in_=src.rearrange("p (m t) -> p t m", t=PACK)
             )
 
         offs_sb = sb("offs_sb", [P, S // 16], U16)
         lists = [sb("list%d" % n, [P, S // 16], U16) for n in range(TERMS)]
         xw = sb("xw", [P, T], I32)
         xs = sb("xs", [P, T], U8)
-        c1_sb = sb("c1_sb", [P, PACK], F32)
-        w1_raw = sb("w1_raw", [P, H], I32)
         s1_raw = sb("s1_raw", [P, H], U8)
-        c2_sb = sb("c2_sb", [P, PACK], F32)
+        s23_raw = sb("s23_raw", [P, N], U8)
+        w1_raw = sb("w1_raw", [P, H], I32)
+        w_raw = [sb("w_raw%d" % z, [P, N], I32) for z in range(2)]
+        c1_sb, c2_sb = sb("c1_sb", [P, PACK], F32), sb("c2_sb", [P, PACK], F32)
+        gate_rows = [sb("gate_row%d" % n, [P, HALF], F32) for n in range(TERMS)]
+        gate_cols = [sb("gate_col%d" % n, [P, 2], F32) for n in range(TERMS)]
         ident = sb("ident", [P, P], F32)
 
+        def load_column(n, g):
+            nc.sync.dma_start(
+                out=gate_cols[n][:], in_=g[0, :HALF].rearrange("(b p) -> p b", p=P), allow_slow_non_contiguous=True
+            )
+
+        nc.gpsimd.memset(s1_raw[:].bitcast(I32), 0)
         nc.vector.memset(xs[:].bitcast(I32), 0)
-        nc.vector.memset(s1_raw[:].bitcast(I32), 0)
+        nc.gpsimd.memset(s23_raw[:].bitcast(I32), 0)
         nc.scalar.dma_start(out=c2_sb[:], in_=c2.rearrange("(p t) o -> p (t o)", t=PACK))
-        nc.scalar.dma_start(out=c1_sb[:], in_=c1.rearrange("(p t) o -> p (t o)", t=PACK))
         nc.sync.dma_start(offs_sb[:], offs)
-        for n, p in enumerate((p1, p2, p3)):
-            nc.sync.dma_start(lists[n][:], p)
+        load_scales(s1_raw, 0, w1_scales)
         nc.sync.dma_start(out=xw[:], in_=words_of(x_words))
-        load_scales([nc.sync] * 4, xs, 0, x_scales)
-        load_scales([nc.sync] * 4, s1_raw, 0, w1_scales)
+        load_scales(xs, 0, x_scales)
         nc.sync.dma_start(out=w1_raw[:], in_=words_of(w1_words))
+        load_column(0, g1)
+        nc.sync.dma_start(out=w_raw[0][:], in_=words_of(w2_words))
+        nc.sync.dma_start(lists[0][:], p1)
+        nc.sync.dma_start(out=w_raw[1][:], in_=words_of(w3_words))
+        nc.sync.dma_start(out=gate_rows[0][:], in_=g1[:, HALF:])
+        for n, p, g in ((1, p2, g2), (2, p3, g3)):
+            nc.sync.dma_start(lists[n][:], p)
+            nc.sync.dma_start(out=gate_rows[n][:], in_=g[:, HALF:])
+        load_column(1, g2)
+        load_column(2, g3)
+        nc.sync.dma_start(out=c1_sb[:], in_=c1.rearrange("(p t) o -> p (t o)", t=PACK))
+        load_scales(s23_raw, 0, w2_scales)
+        load_scales(s23_raw, 4, w3_scales)
         make_identity(nc, ident[:])
 
-        def small(name, dtype=F32):
-            return sb(name, [P, PACK], dtype)
-
-        size, guess, inv_guess, twice = (small(name) for name in ("size", "guess", "inv_guess", "twice"))
-        first, sign = small("first"), sb("sign", [P, B, PACK], BF16)
+        size, guess, inv_guess, twice = (sb(name, [P, PACK], F32) for name in ("size", "guess", "inv_guess", "twice"))
+        sign = sb("sign", [P, B, PACK], BF16)
         nc.vector.scalar_tensor_tensor(size[:], c2_sb[:], -1.0, c2_sb[:], MULT, MAX)
         nc.scalar.activation(guess[:], size[:], SQRT, bias=2.0**-100)
         nc.vector.reciprocal(inv_guess[:], guess[:])
@@ -102,261 +116,198 @@ def tile_picked_ace8_none_po_kernel(
             col = slice(t, t + 1)
             nc.scalar.activation(twice[:, col], inv_guess[:, col], IDENTITY, bias=guess[:, col], scale=size[:, col])
         nc.scalar.activation(sign[:], c2_sb[:].unsqueeze(1).broadcast_to([P, B, PACK]), SIGN, scale=guess[:, 0:1])
-        w23_raw = sb("w23_raw", [P, 2, H], I32, "size")
-        nc.sync.dma_start(out=w23_raw[:, 0, :], in_=words_of(w2_words))
-        nc.sync.dma_start(out=w23_raw[:, 1, :], in_=words_of(w3_words))
+        inv_twice = sb("inv_twice", [P, PACK], F32)
+        nc.vector.reciprocal(inv_twice[:], twice[:])
 
-        xg_w, xg_s = sb("xg_w", [P, S], U32), sb("xg_s", [P, S], U8)
-        w1_first, w1_rest = sb("w1_first", [P, P], U32), sb("w1_rest", [P, H - P], U32)
-        for h in range(2):
-            nc.vector.tensor_copy(
-                out=xg_w[:, h * HALF : (h + 1) * HALF],
-                in_=xw[:].bitcast(U32).indirect(offs_sb[:, h * HALF // 16 : (h + 1) * HALF // 16]),
-            )
+        s1 = sb("s1", [P, H], U8)
+        deal_bytes(s1[:], s1_raw[:])
+        xg_s = sb("xg_s", [P, S], U8)
+        xg_w = [sb("xg_w0", [P, HALF], U32)]
+        nc.vector.tensor_copy(out=xg_w[0][:], in_=xw[:].bitcast(U32).indirect(offs_sb[:, : HALF // 16]))
         nc.vector.tensor_copy(out=xg_s[:], in_=xs[:].indirect(offs_sb[:]))
+        xg_w.append(sb("xg_w1", [P, HALF], U32, "xs"))
+        nc.vector.tensor_copy(out=xg_w[1][:], in_=xw[:].bitcast(U32).indirect(offs_sb[:, HALF // 16 :]))
+        w1_first, w1_rest = sb("w1_first", [P, P], U32), sb("w1_rest", [P, H - P], U32)
         deal(nc.scalar.copy, w1_first[:], w1_raw[:].bitcast(U32), 0, 1)
         deal(nc.scalar.copy, w1_rest[:], w1_raw[:].bitcast(U32), 1, PACK)
-        s1_dealt = sb("s1_dealt", [P, H], U8)
-        s1_first, s1_rest = s1_dealt[:, :P], s1_dealt[:, P:]
-        deal_bytes(s1_first, s1_raw, 0, 1)
-        deal_bytes(s1_rest, s1_raw, 1, PACK)
-        gate_rows = sb("gate_rows", [P, TERMS, S - B], F32, "xw")
-        gates = [gate_rows[:, n, :] for n in range(TERMS)]
-        for n, g in enumerate((g1, g2, g3)):
-            nc.sync.dma_start(out=gates[n], in_=g[:, B:])
-        w_both = sb("w_both", [P, 2, N], I32, "s1_raw")
-        w_dealt = [w_both[:, z, :] for z in range(2)]
+        w_both = sb("w_both", [P, 2, N], I32, "xw")
         for z in range(2):
-            deal(nc.vector.tensor_copy, w_dealt[z], w23_raw[:, z, :], 0, PACK)
-        gate_tile = sb("gate_tile", [P, TERMS, 8], F32, "xs")
-        gate_cols = [gate_tile[:, n, :2] for n in range(TERMS)]
-        for n, g in enumerate((g1, g2, g3)):
-            nc.sync.dma_start(
-                out=gate_cols[n], in_=g[0, : 2 * B].rearrange("(b p) -> p b", p=P), allow_slow_non_contiguous=True
+            deal(nc.vector.tensor_copy, w_both[:, z, :], w_raw[z][:], 0, PACK)
+
+        y = [sb("y%d" % t, [P, S], F32) for t in range(PACK)]
+        for number, (t, h) in enumerate([(0, 0), (1, 0), (0, 1), (1, 1), (2, 0), (2, 1), (3, 0), (3, 1)]):
+            cols = slice(h * HALF, (h + 1) * HALF)
+            w1_t = w1_first[:] if t == 0 else w1_rest[:, (t - 1) * P : t * P]
+            y_ps = bank("y_ps%d%d" % (t, h), number)
+            nc.tensor.matmul_mx(
+                out=y_ps[:, :HALF], lhsT=w1_t.bitcast(FP8X4), lhsT_scale=s1[:, t * P : (t + 1) * P],
+                rhs=xg_w[h][:].bitcast(FP8X4), rhs_scale=xg_s[:, cols], start=True, stop=True,
             )
-        s_raw = sb("s_raw", [P, N], U8, "w1_raw")
-        nc.gpsimd.memset(s_raw[:].bitcast(I32), 0)
-        load_scales([nc.sync] * 4, s_raw, 0, w2_scales)
-        load_scales([nc.sync] * 4, s_raw, 4, w3_scales)
+            nc.scalar.activation(y[t][:, cols], y_ps[:, :HALF], COPY, scale=twice[:, t : t + 1])
 
-        y = []
-        for t in range(PACK):
-            y_t = sb("y%d" % t, [P, S], F32)
-            rest = slice((t - 1) * P, t * P)
-            w1_t, s1_t = (w1_first[:], s1_first) if t == 0 else (w1_rest[:, rest], s1_rest[:, rest])
-            for h, cols in enumerate([slice(0, HALF), slice(HALF, S)] if t == 0 else [slice(0, S)]):
-                y_ps = bank("y_ps%d%d" % (t, h), 4 if h == 1 else t)
-                nc.tensor.matmul_mx(
-                    out=y_ps[:, cols], lhsT=w1_t.bitcast(FP8X4), lhsT_scale=s1_t,
-                    rhs=xg_w[:, cols].bitcast(FP8X4), rhs_scale=xg_s[:, cols], start=True, stop=True,
+        def picks(t, n, start, count):
+            return y[t][:].indirect(lists[n][:, start // 16 : (start + count) // 16])
+
+        wide = sb("wide", [P, TERMS, PACK, HALF], F32)
+        for pair in range(0, PACK, 2):
+            for n in range(TERMS):
+                for t in (pair, pair + 1):
+                    nc.vector.tensor_tensor(wide[:, n, t, :], picks(t, n, HALF, HALF), gate_rows[n][:], MULT)
+        first = sb("first", [P, PACK], F32, "gate_row1")
+        nc.vector.tensor_tensor(first[:], c1_sb[:], inv_twice[:], MULT)
+
+        def gather_and_turn(n, numbers, tag):
+            terms = sb("terms%d" % n, [P, PACK, HALF], F32, tag)
+            apart = [bank("apart%d%d" % (b, n), numbers[b]) for b in range(2)]
+            for t in range(PACK):
+                nc.scalar.activation(terms[:, t, :], picks(t, n, 0, HALF), COPY)
+                for b in (1, 0):
+                    nc.tensor.transpose(apart[b][:, t * P : (t + 1) * P], terms[:, t, b * B : (b + 1) * B], ident[:])
+            return apart
+
+        def gate_turned(b, n, apart):
+            turned = sb("turned%d%d" % (b, n), [P, PACK * P], F32)
+            nc.scalar.activation(turned[:], apart[:], COPY, scale=gate_cols[n][:, b : b + 1])
+            return turned
+
+        def gate_onto(b, n, apart, earlier, tag):
+            turned = sb("turned%d%d" % (b, n), [P, PACK * P], F32, tag)
+            nc.vector.scalar_tensor_tensor(turned[:], apart[:], gate_cols[n][:, b : b + 1], earlier[:], MULT, ADD)
+            return turned
+
+        def turn_back(turned, into, opens, closes):
+            for t in range(PACK):
+                nc.tensor.matmul(
+                    into[:, t * B : (t + 1) * B], turned[:, t * P : (t + 1) * P], ident[:],
+                    start=(opens and t == 0), stop=(closes and t == PACK - 1), is_transpose=True,
                 )
-                nc.scalar.activation(y_t[:, cols], y_ps[:, cols], COPY, scale=twice[:, t : t + 1])
-            y.append(y_t)
 
-        inv_root = sb("inv_root", [P, PACK], F32, "w1_first")
-        nc.vector.reciprocal(inv_root[:], twice[:])
-        nc.vector.tensor_tensor(first[:], c1_sb[:], inv_root[:], MULT)
+        def own(b):
+            return slice(b * B - HALF, (b + 1) * B - HALF)
+
+        def add_third(b, pair):
+            total = sb("total%d" % b, [P, PACK, B], F32)
+            nc.vector.tensor_tensor(total[:], pair[:, :, own(b)], wide[:, 2, :, own(b)], ADD)
+            return total
+
+        def by_lines(planes):
+            return planes[:].rearrange("p t (c i) -> p c t i", i=4)
+
+        def woven_lines(woven):
+            return woven[:].rearrange("p (c i) t -> p c t i", i=4)
+
+        def first_of_planes(b, total):
+            z2 = sb("z2_%d" % b, [P, B, PACK], BF16)
+            factor = first[:].unsqueeze(1).unsqueeze(3).broadcast_to([P, B // 4, PACK, 4])
+            nc.vector.tensor_tensor(woven_lines(z2), by_lines(total), factor, MULT)
+            return z2
+
+        def square_of_planes(b, total, tag):
+            sq = sb("sq%d" % b, [P, B, PACK], BF16, tag)
+            nc.scalar.activation(woven_lines(sq), by_lines(total), SQUARE, scale=0.5)
+            return sq
+
+        def across(sums):
+            return sums[:].rearrange("p (t j) -> p j t", t=PACK)
+
+        def first_of_bank(b, sums, tag=None):
+            z2 = sb("z2_%d" % b, [P, B, PACK], BF16, tag)
+            nc.vector.tensor_tensor(z2[:], across(sums), first[:].unsqueeze(1).broadcast_to([P, B, PACK]), MULT)
+            return z2
+
+        def square_of_bank(b, sums, tag=None):
+            sq = sb("sq%d" % b, [P, B, PACK], BF16, tag)
+            nc.scalar.activation(sq[:], across(sums), SQUARE, scale=0.5)
+            return sq
+
+        def signed(b, sq):
+            z = sb("z_%d" % b, [P, B, PACK], BF16)
+            nc.vector.tensor_tensor(z[:], sq[:], sign[:], MULT)
+            return z
+
+        s23 = sb("s23", [P, N], U8, "gate_row0")
+
+        def multiply(b, order, values, banks, tag=None):
+            codes = sb("codes%d%d" % (b, order), [P, B], U32, tag)
+            scales = sb("scales%d%d" % (b, order), [P, B], U8)
+            nc.vector.quantize_mx(
+                out=codes[:].bitcast(FP8X4), scales=scales[:], in_=values[:].rearrange("p j t -> p (j t)")
+            )
+            share = PACK // len(banks)
+            for t in range(PACK):
+                nc.tensor.matmul_mx(
+                    out=banks[t // share][:, t % share * B : (t % share + 1) * B],
+                    lhsT=w_both[:, order, t * P : (t + 1) * P].bitcast(FP8X4),
+                    lhsT_scale=s23[4 * order : P, t * P : (t + 1) * P],
+                    rhs=codes[:].bitcast(FP8X4),
+                    rhs_scale=scales[:],
+                    start=(order == 0 and t % share == 0),
+                    stop=(order == 1 and t % share == share - 1),
+                )
 
         out_codes = sb("out_codes", [P, S], U32)
         out_scales = sb("out_scales", [P, S], U8)
         out_rows = out_0.rearrange("(p t) j -> p t j", t=PACK)
         out_words = words_of(out_1)
-        s23 = sb("s23", [P, N], U8)
 
-        a_ps = [None] * BLOCKS
-
-        def sums_of(b):
-            if a_ps[b] is None:
-                a_ps[b] = bank("a_ps%d" % b, 4 + b)
-            return a_ps[b]
-
-        def picks(t, n, b, blocks):
-            return y[t][:].indirect(lists[n][:, b * B // 16 : (b + blocks) * B // 16])
-
-        wide = sb("wide", [P, TERMS, PACK, S - B], F32)
-
-        def gated_gathers(t, first_block):
-            cols = slice((first_block - 1) * B, S - B)
-            for n in range(TERMS):
-                nc.vector.tensor_tensor(
-                    wide[:, n, t, cols], picks(t, n, first_block, BLOCKS - first_block), gates[n][:, cols], MULT
-                )
-
-        def raw_gathers(t, b):
-            raw = sb("raw%d%d" % (t, b), [P, TERMS, B], F32)
-            cols = slice((b - 1) * B, b * B)
-            for n in range(TERMS):
-                nc.scalar.activation(raw[:, n, :], picks(t, n, b, 1), COPY)
-            nc.vector.tensor_tensor(wide[:, :, t, cols], raw[:], gate_rows[:, :, cols], MULT)
-
-        def plain_gathers(n, tiles, b, number, tag):
-            terms = sb("terms%d%d" % (n, b), [P, len(tiles), B], F32, tag)
-            apart = bank("apart%d%d" % (n, b), number)
-            for k, t in enumerate(tiles):
-                nc.scalar.activation(terms[:, k, :], picks(t, n, b, 1), COPY)
-                nc.tensor.transpose(apart[:, k * P : (k + 1) * P], terms[:, k, :], ident[:])
-            return apart
-
-        def plain_sums(n, tiles, b, apart, into):
-            count = len(tiles)
-            turned = sb("turned%d%d" % (n, b), [P, count * P], F32, "turned%d%d" % (n, b))
-            nc.scalar.activation(turned[:], apart[:, : count * P], COPY, scale=gate_cols[n][:, b : b + 1])
-            for k in range(count):
-                nc.tensor.matmul(
-                    into[:, k * B : (k + 1) * B], turned[:, k * P : (k + 1) * P], ident[:],
-                    start=(n == 0 and k == 0), stop=(n == TERMS - 1 and k == count - 1), is_transpose=True,
-                )
-
-        def square(b, tag=None):
-            sq = sb("sq%d" % b, [P, B, PACK], BF16, tag)
-            nc.scalar.activation(sq[:], a_ps[b][:].rearrange("p (t j) -> p j t", t=PACK), SQUARE, scale=0.5)
-            return sq
-
-        def signed(zi, sq):
-            nc.vector.tensor_tensor(zi[:, 1], sq[:], sign[:], MULT)
-
-        def orders(b, sq, tag=None):
-            zi = sb("zi%d" % b, [P, 2, B, PACK], BF16, tag)
-            flat = sb("flat", [P, PACK, B], BF16)
-            for t in range(PACK):
-                nc.scalar.activation(flat[:, t, :], a_ps[b][:, t * B : (t + 1) * B], COPY, scale=first[:, t : t + 1])
-            nc.vector.tensor_copy(
-                out=zi[:, 0].rearrange("p (c i) t -> p c t i", i=4),
-                in_=flat[:].rearrange("p t (c i) -> p c t i", i=4),
-            )
-            signed(zi, sq)
-            return zi
-
-        total = sb("total", [P, PACK, S - B], F32)
-
-        def added(tiles, cols, name, tag=None):
-            pair = sb(name, [P, len(range(PACK)[tiles]), cols.stop - cols.start], F32, tag)
-            nc.vector.tensor_tensor(pair[:], wide[:, 0, tiles, cols], wide[:, 1, tiles, cols], ADD)
-            nc.vector.tensor_tensor(total[:, tiles, cols], pair[:], wide[:, 2, tiles, cols], ADD)
-
-        def lines_of(b):
-            return total[:, :, (b - 1) * B : b * B].rearrange("p t (c i) -> p c t i", i=4)
-
-        def square_planes(b, tag=None):
-            sq = sb("sq%d" % b, [P, B, PACK], BF16, tag)
-            nc.scalar.activation(sq[:].rearrange("p (c i) t -> p c t i", i=4), lines_of(b), SQUARE, scale=0.5)
-            return sq
-
-        def first_from_planes(b, ring):
-            zi = sb("zi%d" % b, [P, 2, B, PACK], BF16, ring)
-            nc.vector.tensor_tensor(
-                zi[:, 0].rearrange("p (c i) t -> p c t i", i=4), lines_of(b),
-                first[:].unsqueeze(1).unsqueeze(3).broadcast_to([P, B // 4, PACK, 4]), MULT,
-            )
-            return zi
-
-        def multiply(b, zi, number):
-            codes = sb("codes%d" % b, [P, 2 * B], U32)
-            scales = sb("scales%d" % b, [P, 2 * B], U8)
-            nc.vector.quantize_mx(
-                out=codes[:].bitcast(FP8X4), scales=scales[:], in_=zi[:].rearrange("p z j t -> p (z j t)")
-            )
-            out_ps = bank("out_ps%d" % b, number)
-            for t in range(PACK):
-                for z in range(2):
-                    nc.tensor.matmul_mx(
-                        out=out_ps[:, t * B : (t + 1) * B],
-                        lhsT=w_dealt[z][:, t * P : (t + 1) * P].bitcast(FP8X4),
-                        lhsT_scale=s23[4 * z : P, t * P : (t + 1) * P],
-                        rhs=codes[:, z * B : (z + 1) * B].bitcast(FP8X4),
-                        rhs_scale=scales[:, z * B : (z + 1) * B],
-                        start=(z == 0),
-                        stop=(z == 1),
-                    )
-            return out_ps
-
-        def last_block(b, zi, numbers):
-            pairs = [bank("pair_ps%d" % u, numbers[u]) for u in range(2)]
-            for z in range(2):
-                codes = sb("last_codes%d" % z, [P, B], U32)
-                scales = sb("last_scales%d" % z, [P, B], U8)
-                nc.vector.quantize_mx(
-                    out=codes[:].bitcast(FP8X4), scales=scales[:], in_=zi[:, z].rearrange("p j t -> p (j t)")
-                )
-                for t in range(PACK):
-                    nc.tensor.matmul_mx(
-                        out=pairs[t // 2][:, t % 2 * B : (t % 2 + 1) * B],
-                        lhsT=w_dealt[z][:, t * P : (t + 1) * P].bitcast(FP8X4),
-                        lhsT_scale=s23[4 * z : P, t * P : (t + 1) * P],
-                        rhs=codes[:].bitcast(FP8X4),
-                        rhs_scale=scales[:],
-                        start=(z == 0 and t % 2 == 0),
-                        stop=(z == 1 and t % 2 == 1),
-                    )
-            return pairs
-
-        def leave_last(b, pairs):
+        def leave(b, banks):
             cols = slice(b * B, (b + 1) * B)
             res = sb("res%d" % b, [P, PACK, B], F32)
             res_i = sb("res_i%d" % b, [P, B, PACK], BF16)
-            for u in range(2):
-                nc.scalar.copy(out=res[:, 2 * u : 2 * u + 2, :].rearrange("p t j -> p (t j)"), in_=pairs[u][:, : 2 * B])
-            nc.sync.dma_start(out=out_rows[:, :, cols], in_=res[:])
-            nc.vector.tensor_copy(
-                out=res_i[:].rearrange("p (c i) t -> p c t i", i=4),
-                in_=res[:].rearrange("p t (c i) -> p c t i", i=4),
-            )
-            nc.vector.quantize_mx(
-                out=out_codes[:, cols].bitcast(FP8X4), scales=out_scales[:, cols],
-                in_=res_i[:].rearrange("p j t -> p (j t)"),
-            )
-
-        def leave(b, out_ps, tag=None, on_scalar=False):
-            cols = slice(b * B, (b + 1) * B)
-            res = sb("res%d" % b, [P, PACK, B], F32, tag)
-            res_i = sb("res_i%d" % b, [P, B, PACK], BF16)
-            nc.scalar.copy(out=res[:].rearrange("p t j -> p (t j)"), in_=out_ps[:])
-            nc.sync.dma_start(out=out_rows[:, :, cols], in_=res[:])
-            if on_scalar:
-                nc.scalar.copy(out=res_i[:], in_=out_ps[:].rearrange("p (t j) -> p j t", t=PACK))
-            else:
-                nc.vector.tensor_copy(
-                    out=res_i[:].rearrange("p (c i) t -> p c t i", i=4),
-                    in_=res[:].rearrange("p t (c i) -> p c t i", i=4),
+            share = PACK // len(banks)
+            for u, held in enumerate(banks):
+                nc.scalar.copy(
+                    out=res[:, u * share : (u + 1) * share, :].rearrange("p t j -> p (t j)"), in_=held[:, : share * B]
                 )
+            nc.sync.dma_start(out=out_rows[:, :, cols], in_=res[:])
+            nc.vector.tensor_copy(out=woven_lines(res_i), in_=by_lines(res))
             nc.vector.quantize_mx(
                 out=out_codes[:, cols].bitcast(FP8X4), scales=out_scales[:, cols],
                 in_=res_i[:].rearrange("p j t -> p (j t)"),
             )
 
-        for t in range(PACK):
-            gated_gathers(t, (1, 2, 1, 3)[t])
-        shared = bank("shared", 5)
-        groups = [(n, (1, 3), 1, shared) for n in range(TERMS)] + [(n, (0, 1, 2, 3), 0, sums_of(0)) for n in range(TERMS)]
-        turning = []
-        for i, (n, tiles, b, into) in enumerate(groups):
-            turning.append((n, tiles, b, plain_gathers(n, tiles, b, 1 + i % 3, "ring%d" % (i % 2)), into))
-            if i > 0:
-                plain_sums(*turning[i - 1])
-            if i == TERMS:
-                nc.scalar.copy(out=total[:, slice(1, 4, 2), :B], in_=shared[:, : 2 * B].rearrange("p (t j) -> p t j", j=B))
-        plain_sums(*turning[-1])
-        def finish(b, square_tag, ring, number):
-            sq = square_planes(b, square_tag)
-            zi = first_from_planes(b, ring)
-            signed(zi, sq)
-            return multiply(b, zi, number)
-
-        added(slice(0, 4), slice(2 * B, 3 * B), "pair3")
-        deal_bytes(s23[:], s_raw, 0, 4)
-        oa = finish(3, "ring0", "ring_z0", 6)
-        raw_gathers(3, 2)
-        added(slice(0, 4), slice(B, 2 * B), "pair2")
-        added(slice(0, 3, 2), slice(0, B), "pair1")
-        ob = finish(2, "turned10", "ring_z1", 7)
-        oc = finish(1, None, "ring_z0", 5)
-        z0 = orders(0, square(0), "ring_z1")
-        pairs = last_block(0, z0, (0, 1))
-        leave(3, oa)
-        leave(2, ob)
-        leave(1, oc)
+        apart0 = gather_and_turn(0, (1, 0), "ring_a")
+        apart1 = gather_and_turn(1, (3, 2), "ring_b")
+        sums = [bank("sums0", 5), bank("sums1", 4)]
+        sums0, sums1 = sums
+        for b in (1, 0):
+            turn_back(gate_turned(b, 0, apart0[b]), sums[b], True, False)
+        apart2 = gather_and_turn(2, (1, 0), "ring_a")
+        turned = [gate_turned(b, 1, apart1[b]) for b in (1, 0)]
+        deal_bytes(s23[:], s23_raw[:])
+        pair = sb("pair", [P, PACK, HALF], F32, "s23_raw")
+        nc.vector.tensor_tensor(pair[:], wide[:, 0], wide[:, 1], ADD)
+        total3 = add_third(3, pair)
+        total2 = add_third(2, pair)
+        turn_back(gate_onto(1, 2, apart2[1], turned[0], "wide"), sums1, False, True)
+        turn_back(gate_onto(0, 2, apart2[0], turned[1], "s23_raw"), sums0, False, True)
+        sq3 = square_of_planes(3, total3, None)
+        sq2 = square_of_planes(2, total2, None)
+        z2_3 = first_of_planes(3, total3)
+        z2_2 = first_of_planes(2, total2)
+        out3, out2, out1 = [bank("out3", 6)], [bank("out2", 7)], [bank("out1", 2)]
+        multiply(3, 0, z2_3, out3)
+        z2_1 = first_of_bank(1, sums1)
+        multiply(2, 0, z2_2, out2)
+        sq1 = square_of_bank(1, sums1)
+        z_3 = signed(3, sq3)
+        multiply(1, 0, z2_1, out1)
+        z2_0 = first_of_bank(0, sums0, "total3")
+        multiply(3, 1, z_3, out3)
+        sq0 = square_of_bank(0, sums0, "sq3")
+        z_2 = signed(2, sq2)
+        out0 = [bank("out0a", 3), bank("out0b", 0)]
+        multiply(0, 0, z2_0, out0)
+        z_1 = signed(1, sq1)
+        multiply(2, 1, z_2, out2)
+        z_0 = signed(0, sq0)
+        multiply(1, 1, z_1, out1)
+        multiply(0, 1, z_0, out0)
+        leave(3, out3)
+        leave(2, out2)
+        leave(1, out1)
         nc.sync.dma_start(out=out_words[:, B:], in_=out_codes[:, B:].bitcast(I32))
-        leave_last(0, pairs)
+        leave(0, out0)
         nc.sync.dma_start(out=out_words[:, :B], in_=out_codes[:, :B].bitcast(I32))
         for q in range(4):
             queue = nc.sync if q % 2 == 0 else nc.scalar

@@ -54,6 +54,9 @@ def tile_picked_ace8_none_po_kernel(
                     in_=src[0, 4 * q : 4 * q + 4, :].bitcast(I32),
                 )
 
+        def load_column(dst, g):
+            nc.sync.dma_start(out=dst, in_=g[0, :HALF].rearrange("(b p) -> p b", p=P), allow_slow_non_contiguous=True)
+
         def deal(move, dst, src, t0, t1):
             move(
                 out=dst.rearrange("p (t c i) -> p c t i", t=t1 - t0, i=4),
@@ -70,41 +73,21 @@ def tile_picked_ace8_none_po_kernel(
         xw = sb("xw", [P, T], I32)
         xs = sb("xs", [P, T], U8)
         s1_raw = sb("s1_raw", [P, H], U8)
-        s23_raw = sb("s23_raw", [P, N], U8)
         w1_raw = sb("w1_raw", [P, H], I32)
-        w_raw = [sb("w_raw%d" % z, [P, N], I32) for z in range(2)]
         c1_sb, c2_sb = sb("c1_sb", [P, PACK], F32), sb("c2_sb", [P, PACK], F32)
-        gate_rows = [sb("gate_row%d" % n, [P, HALF], F32) for n in range(TERMS)]
-        gate_cols = [sb("gate_col%d" % n, [P, 2], F32) for n in range(TERMS)]
         ident = sb("ident", [P, P], F32)
 
-        def load_column(n, g):
-            nc.sync.dma_start(
-                out=gate_cols[n][:], in_=g[0, :HALF].rearrange("(b p) -> p b", p=P), allow_slow_non_contiguous=True
-            )
-
-        nc.gpsimd.memset(s1_raw[:].bitcast(I32), 0)
         nc.vector.memset(xs[:].bitcast(I32), 0)
-        nc.gpsimd.memset(s23_raw[:].bitcast(I32), 0)
+        nc.vector.memset(s1_raw[:].bitcast(I32), 0)
         nc.scalar.dma_start(out=c2_sb[:], in_=c2.rearrange("(p t) o -> p (t o)", t=PACK))
+        nc.scalar.dma_start(out=c1_sb[:], in_=c1.rearrange("(p t) o -> p (t o)", t=PACK))
         nc.sync.dma_start(offs_sb[:], offs)
-        load_scales(s1_raw, 0, w1_scales)
+        for n, p in enumerate((p1, p2, p3)):
+            nc.sync.dma_start(lists[n][:], p)
         nc.sync.dma_start(out=xw[:], in_=words_of(x_words))
         load_scales(xs, 0, x_scales)
+        load_scales(s1_raw, 0, w1_scales)
         nc.sync.dma_start(out=w1_raw[:], in_=words_of(w1_words))
-        load_column(0, g1)
-        nc.sync.dma_start(out=w_raw[0][:], in_=words_of(w2_words))
-        nc.sync.dma_start(lists[0][:], p1)
-        nc.sync.dma_start(out=w_raw[1][:], in_=words_of(w3_words))
-        nc.sync.dma_start(out=gate_rows[0][:], in_=g1[:, HALF:])
-        for n, p, g in ((1, p2, g2), (2, p3, g3)):
-            nc.sync.dma_start(lists[n][:], p)
-            nc.sync.dma_start(out=gate_rows[n][:], in_=g[:, HALF:])
-        load_column(1, g2)
-        load_column(2, g3)
-        nc.sync.dma_start(out=c1_sb[:], in_=c1.rearrange("(p t) o -> p (t o)", t=PACK))
-        load_scales(s23_raw, 0, w2_scales)
-        load_scales(s23_raw, 4, w3_scales)
         make_identity(nc, ident[:])
 
         size, guess, inv_guess, twice = (sb(name, [P, PACK], F32) for name in ("size", "guess", "inv_guess", "twice"))
@@ -119,41 +102,64 @@ def tile_picked_ace8_none_po_kernel(
         inv_twice = sb("inv_twice", [P, PACK], F32)
         nc.vector.reciprocal(inv_twice[:], twice[:])
 
-        s1 = sb("s1", [P, H], U8)
-        deal_bytes(s1[:], s1_raw[:])
-        xg_s = sb("xg_s", [P, S], U8)
-        xg_w = [sb("xg_w0", [P, HALF], U32)]
-        nc.vector.tensor_copy(out=xg_w[0][:], in_=xw[:].bitcast(U32).indirect(offs_sb[:, : HALF // 16]))
+        w_raw = sb("w_raw", [P, 2, N], I32, "size")
+        for z, w in enumerate((w2_words, w3_words)):
+            nc.sync.dma_start(out=w_raw[:, z, :], in_=words_of(w))
+
+        xg_w, xg_s = sb("xg_w", [P, S], U32), sb("xg_s", [P, S], U8)
+        for h in range(2):
+            nc.vector.tensor_copy(
+                out=xg_w[:, h * HALF : (h + 1) * HALF],
+                in_=xw[:].bitcast(U32).indirect(offs_sb[:, h * HALF // 16 : (h + 1) * HALF // 16]),
+            )
         nc.vector.tensor_copy(out=xg_s[:], in_=xs[:].indirect(offs_sb[:]))
-        xg_w.append(sb("xg_w1", [P, HALF], U32, "xs"))
-        nc.vector.tensor_copy(out=xg_w[1][:], in_=xw[:].bitcast(U32).indirect(offs_sb[:, HALF // 16 :]))
         w1_first, w1_rest = sb("w1_first", [P, P], U32), sb("w1_rest", [P, H - P], U32)
         deal(nc.scalar.copy, w1_first[:], w1_raw[:].bitcast(U32), 0, 1)
         deal(nc.scalar.copy, w1_rest[:], w1_raw[:].bitcast(U32), 1, PACK)
-        w_both = sb("w_both", [P, 2, N], I32, "xw")
+        s1 = sb("s1", [P, H], U8)
+        for t0, t1 in ((0, 1), (1, PACK)):
+            nc.vector.tensor_copy(
+                out=s1[:, t0 * P : t1 * P].rearrange("p (t m) -> p m t", t=t1 - t0),
+                in_=s1_raw[:].rearrange("p (m t) -> p m t", t=PACK)[:, :, t0:t1],
+            )
+        gate_tile = sb("gate_tile", [P, TERMS, HALF], F32, "xw")
+        gate_rows = [gate_tile[:, n, :] for n in range(TERMS)]
+        for n, g in enumerate((g1, g2, g3)):
+            nc.sync.dma_start(out=gate_rows[n], in_=g[:, HALF:])
+        w_both = sb("w_both", [P, 2, N], I32, "s1_raw")
         for z in range(2):
-            deal(nc.vector.tensor_copy, w_both[:, z, :], w_raw[z][:], 0, PACK)
+            deal(nc.vector.tensor_copy, w_both[:, z, :], w_raw[:, z, :], 0, PACK)
+        gate_cols = [sb("column0", [P, 2], F32, "xs")[:]]
+        load_column(gate_cols[0], g1)
 
         y = [sb("y%d" % t, [P, S], F32) for t in range(PACK)]
-        for number, (t, h) in enumerate([(0, 0), (1, 0), (0, 1), (1, 1), (2, 0), (2, 1), (3, 0), (3, 1)]):
-            cols = slice(h * HALF, (h + 1) * HALF)
+        for t in range(PACK):
             w1_t = w1_first[:] if t == 0 else w1_rest[:, (t - 1) * P : t * P]
-            y_ps = bank("y_ps%d%d" % (t, h), number)
-            nc.tensor.matmul_mx(
-                out=y_ps[:, :HALF], lhsT=w1_t.bitcast(FP8X4), lhsT_scale=s1[:, t * P : (t + 1) * P],
-                rhs=xg_w[h][:].bitcast(FP8X4), rhs_scale=xg_s[:, cols], start=True, stop=True,
-            )
-            nc.scalar.activation(y[t][:, cols], y_ps[:, :HALF], COPY, scale=twice[:, t : t + 1])
+            for h, cols in enumerate([slice(0, HALF), slice(HALF, S)] if t == 0 else [slice(0, S)]):
+                y_ps = bank("y_ps%d%d" % (t, h), 4 if h == 1 else t)
+                nc.tensor.matmul_mx(
+                    out=y_ps[:, cols], lhsT=w1_t.bitcast(FP8X4), lhsT_scale=s1[:, t * P : (t + 1) * P],
+                    rhs=xg_w[:, cols].bitcast(FP8X4), rhs_scale=xg_s[:, cols], start=True, stop=True,
+                )
+                nc.scalar.activation(y[t][:, cols], y_ps[:, cols], COPY, scale=twice[:, t : t + 1])
+
+        column_tile = sb("column_tile", [P, 2, 8], F32, "w1_first")
+        for n, g in enumerate((g2, g3)):
+            gate_cols.append(column_tile[:, n, :2])
+            load_column(gate_cols[n + 1], g)
+        s23_raw = sb("s23_raw", [P, N], U8, "w1_raw")
+        nc.gpsimd.memset(s23_raw[:].bitcast(I32), 0)
+        load_scales(s23_raw, 0, w2_scales)
+        load_scales(s23_raw, 4, w3_scales)
 
         def picks(t, n, start, count):
             return y[t][:].indirect(lists[n][:, start // 16 : (start + count) // 16])
 
         wide = sb("wide", [P, TERMS, PACK, HALF], F32)
-        for pair in range(0, PACK, 2):
+        for t in range(PACK):
             for n in range(TERMS):
-                for t in (pair, pair + 1):
-                    nc.vector.tensor_tensor(wide[:, n, t, :], picks(t, n, HALF, HALF), gate_rows[n][:], MULT)
-        first = sb("first", [P, PACK], F32, "gate_row1")
+                nc.vector.tensor_tensor(wide[:, n, t, :], picks(t, n, HALF, HALF), gate_rows[n], MULT)
+        first = sb("first", [P, PACK], F32)
         nc.vector.tensor_tensor(first[:], c1_sb[:], inv_twice[:], MULT)
 
         def gather_and_turn(n, numbers, tag):
@@ -225,7 +231,7 @@ def tile_picked_ace8_none_po_kernel(
             nc.vector.tensor_tensor(z[:], sq[:], sign[:], MULT)
             return z
 
-        s23 = sb("s23", [P, N], U8, "gate_row0")
+        s23 = sb("s23", [P, N], U8, "xw")
 
         def multiply(b, order, values, banks, tag=None):
             codes = sb("codes%d%d" % (b, order), [P, B], U32, tag)
@@ -272,15 +278,15 @@ def tile_picked_ace8_none_po_kernel(
         sums0, sums1 = sums
         for b in (1, 0):
             turn_back(gate_turned(b, 0, apart0[b]), sums[b], True, False)
-        apart2 = gather_and_turn(2, (1, 0), "ring_a")
+        apart2 = gather_and_turn(2, (1, 0), "xs")
         turned = [gate_turned(b, 1, apart1[b]) for b in (1, 0)]
         deal_bytes(s23[:], s23_raw[:])
-        pair = sb("pair", [P, PACK, HALF], F32, "s23_raw")
+        pair = sb("pair", [P, PACK, HALF], F32, "w1_raw")
         nc.vector.tensor_tensor(pair[:], wide[:, 0], wide[:, 1], ADD)
         total3 = add_third(3, pair)
         total2 = add_third(2, pair)
         turn_back(gate_onto(1, 2, apart2[1], turned[0], "wide"), sums1, False, True)
-        turn_back(gate_onto(0, 2, apart2[0], turned[1], "s23_raw"), sums0, False, True)
+        turn_back(gate_onto(0, 2, apart2[0], turned[1], "w1_raw"), sums0, False, True)
         sq3 = square_of_planes(3, total3, None)
         sq2 = square_of_planes(2, total2, None)
         z2_3 = first_of_planes(3, total3)

@@ -77,17 +77,31 @@ def tile_picked_ace8_none_po_kernel(
         c1_sb, c2_sb = sb("c1_sb", [P, PACK], F32), sb("c2_sb", [P, PACK], F32)
         ident = sb("ident", [P, P], F32)
 
-        nc.vector.memset(xs[:].bitcast(I32), 0)
+        s23_raw = sb("s23_raw", [P, N], U8)
+        w_raw = [sb("w_raw%d" % z, [P, N], I32) for z in range(2)]
+        gate_rows = [sb("gate_row%d" % n, [P, S - B], F32)[:] for n in range(TERMS)]
+        gate_cols = [sb("column%d" % n, [P, 2], F32)[:] for n in range(TERMS)]
+        nc.gpsimd.memset(xs[:].bitcast(I32), 0)
         nc.vector.memset(s1_raw[:].bitcast(I32), 0)
+        nc.vector.memset(s23_raw[:].bitcast(I32), 0)
         nc.scalar.dma_start(out=c2_sb[:], in_=c2.rearrange("(p t) o -> p (t o)", t=PACK))
-        nc.scalar.dma_start(out=c1_sb[:], in_=c1.rearrange("(p t) o -> p (t o)", t=PACK))
-        nc.sync.dma_start(offs_sb[:], offs)
-        for n, p in enumerate((p1, p2, p3)):
-            nc.sync.dma_start(lists[n][:], p)
         nc.sync.dma_start(out=xw[:], in_=words_of(x_words))
+        nc.sync.dma_start(offs_sb[:], offs)
+        nc.sync.dma_start(out=w1_raw[:], in_=words_of(w1_words))
         load_scales(xs, 0, x_scales)
         load_scales(s1_raw, 0, w1_scales)
-        nc.sync.dma_start(out=w1_raw[:], in_=words_of(w1_words))
+        nc.sync.dma_start(lists[0][:], p1)
+        for z, w in enumerate((w2_words, w3_words)):
+            nc.sync.dma_start(out=w_raw[z][:], in_=words_of(w))
+        nc.sync.dma_start(out=gate_rows[0], in_=g1[:, B:])
+        for n, p, g in ((1, p2, g2), (2, p3, g3)):
+            nc.sync.dma_start(lists[n][:], p)
+            nc.sync.dma_start(out=gate_rows[n], in_=g[:, B:])
+        nc.sync.dma_start(out=c1_sb[:], in_=c1.rearrange("(p t) o -> p (t o)", t=PACK))
+        for n, g in enumerate((g1, g2, g3)):
+            load_column(gate_cols[n], g)
+        load_scales(s23_raw, 0, w2_scales)
+        load_scales(s23_raw, 4, w3_scales)
         make_identity(nc, ident[:])
 
         size, guess, inv_guess, twice = (sb(name, [P, PACK], F32) for name in ("size", "guess", "inv_guess", "twice"))
@@ -102,9 +116,6 @@ def tile_picked_ace8_none_po_kernel(
         inv_twice = sb("inv_twice", [P, PACK], F32)
         nc.vector.reciprocal(inv_twice[:], twice[:])
 
-        w_raw = sb("w_raw", [P, 2, N], I32, "size")
-        for z, w in enumerate((w2_words, w3_words)):
-            nc.sync.dma_start(out=w_raw[:, z, :], in_=words_of(w))
 
         xg_w, xg_s = sb("xg_w", [P, S], U32), sb("xg_s", [P, S], U8)
         for h in range(2):
@@ -122,15 +133,9 @@ def tile_picked_ace8_none_po_kernel(
                 out=s1[:, t0 * P : t1 * P].rearrange("p (t m) -> p m t", t=t1 - t0),
                 in_=s1_raw[:].rearrange("p (m t) -> p m t", t=PACK)[:, :, t0:t1],
             )
-        gate_tile = sb("gate_tile", [P, TERMS, HALF], F32, "xw")
-        gate_rows = [gate_tile[:, n, :] for n in range(TERMS)]
-        for n, g in enumerate((g1, g2, g3)):
-            nc.sync.dma_start(out=gate_rows[n], in_=g[:, HALF:])
         w_both = sb("w_both", [P, 2, N], I32, "s1_raw")
         for z in range(2):
-            deal(nc.vector.tensor_copy, w_both[:, z, :], w_raw[:, z, :], 0, PACK)
-        gate_cols = [sb("column0", [P, 2], F32, "xs")[:]]
-        load_column(gate_cols[0], g1)
+            deal(nc.vector.tensor_copy, w_both[:, z, :], w_raw[z][:], 0, PACK)
 
         y = [sb("y%d" % t, [P, S], F32) for t in range(PACK)]
         for t in range(PACK):
@@ -143,57 +148,59 @@ def tile_picked_ace8_none_po_kernel(
                 )
                 nc.scalar.activation(y[t][:, cols], y_ps[:, cols], COPY, scale=twice[:, t : t + 1])
 
-        column_tile = sb("column_tile", [P, 2, 8], F32, "w1_first")
-        for n, g in enumerate((g2, g3)):
-            gate_cols.append(column_tile[:, n, :2])
-            load_column(gate_cols[n + 1], g)
-        s23_raw = sb("s23_raw", [P, N], U8, "w1_raw")
-        nc.gpsimd.memset(s23_raw[:].bitcast(I32), 0)
-        load_scales(s23_raw, 0, w2_scales)
-        load_scales(s23_raw, 4, w3_scales)
-
         def picks(t, n, start, count):
             return y[t][:].indirect(lists[n][:, start // 16 : (start + count) // 16])
 
-        wide = sb("wide", [P, TERMS, PACK, HALF], F32)
-        for t in range(PACK):
-            for n in range(TERMS):
-                nc.vector.tensor_tensor(wide[:, n, t, :], picks(t, n, HALF, HALF), gate_rows[n], MULT)
         first = sb("first", [P, PACK], F32)
         nc.vector.tensor_tensor(first[:], c1_sb[:], inv_twice[:], MULT)
+
+        def gated_gather(into, t, n):
+            start = B if t == 0 else HALF
+            nc.vector.tensor_tensor(
+                into[:, t, start - B :], picks(t, n, start, S - start), gate_rows[n][:, start - B :], MULT
+            )
+
+        wide = sb("wide", [P, 2, PACK, S - B], F32)
+        for t in range(PACK):
+            for n in range(2):
+                gated_gather(wide[:, n], t, n)
+        pair1 = sb("pair1", [P, B], F32)
+        nc.vector.tensor_tensor(pair1[:], wide[:, 0, 0, :B], wide[:, 1, 0, :B], ADD)
+        pair = sb("pair", [P, PACK, HALF], F32)
+        nc.vector.tensor_tensor(pair[:], wide[:, 0, :, B:], wide[:, 1, :, B:], ADD)
+        s23 = sb("s23", [P, N], U8)
+        deal_bytes(s23[:], s23_raw[:])
+        third = sb("third", [P, PACK, S - B], F32, "s23_raw")
+        for t in range(PACK):
+            gated_gather(third, t, 2)
 
         def gather_and_turn(n, numbers, tag):
             terms = sb("terms%d" % n, [P, PACK, HALF], F32, tag)
             apart = [bank("apart%d%d" % (b, n), numbers[b]) for b in range(2)]
             for t in range(PACK):
-                nc.scalar.activation(terms[:, t, :], picks(t, n, 0, HALF), COPY)
-                for b in (1, 0):
+                blocks = 1 if t == 0 else 2
+                nc.scalar.activation(terms[:, t, : blocks * B], picks(t, n, 0, blocks * B), COPY)
+                for b in range(blocks):
                     nc.tensor.transpose(apart[b][:, t * P : (t + 1) * P], terms[:, t, b * B : (b + 1) * B], ident[:])
             return apart
 
-        def gate_turned(b, n, apart):
-            turned = sb("turned%d%d" % (b, n), [P, PACK * P], F32)
-            nc.scalar.activation(turned[:], apart[:], COPY, scale=gate_cols[n][:, b : b + 1])
-            return turned
-
-        def gate_onto(b, n, apart, earlier, tag):
-            turned = sb("turned%d%d" % (b, n), [P, PACK * P], F32, tag)
-            nc.vector.scalar_tensor_tensor(turned[:], apart[:], gate_cols[n][:, b : b + 1], earlier[:], MULT, ADD)
-            return turned
-
-        def turn_back(turned, into, opens, closes):
-            for t in range(PACK):
-                nc.tensor.matmul(
-                    into[:, t * B : (t + 1) * B], turned[:, t * P : (t + 1) * P], ident[:],
-                    start=(opens and t == 0), stop=(closes and t == PACK - 1), is_transpose=True,
+        def gate_and_turn_back(n, apart):
+            for b in range(2):
+                turned = sb("turned%d%d" % (b, n), [P, PACK * P], F32)
+                nc.scalar.activation(
+                    turned[:, b * P :], apart[b][:, b * P :], COPY, scale=gate_cols[n][:, b : b + 1]
                 )
-
-        def own(b):
-            return slice(b * B - HALF, (b + 1) * B - HALF)
+                for t in range(b, PACK):
+                    nc.tensor.matmul(
+                        sums[b][:, t * B : (t + 1) * B], turned[:, t * P : (t + 1) * P], ident[:],
+                        start=(n == 0 and t == b), stop=(n == TERMS - 1 and t == PACK - 1), is_transpose=True,
+                    )
 
         def add_third(b, pair):
             total = sb("total%d" % b, [P, PACK, B], F32)
-            nc.vector.tensor_tensor(total[:], pair[:, :, own(b)], wide[:, 2, :, own(b)], ADD)
+            nc.vector.tensor_tensor(
+                total[:], pair[:, :, (b - 2) * B : (b - 1) * B], third[:, :, (b - 1) * B : b * B], ADD
+            )
             return total
 
         def by_lines(planes):
@@ -216,22 +223,23 @@ def tile_picked_ace8_none_po_kernel(
         def across(sums):
             return sums[:].rearrange("p (t j) -> p j t", t=PACK)
 
-        def first_of_bank(b, sums, tag=None):
-            z2 = sb("z2_%d" % b, [P, B, PACK], BF16, tag)
-            nc.vector.tensor_tensor(z2[:], across(sums), first[:].unsqueeze(1).broadcast_to([P, B, PACK]), MULT)
-            return z2
-
         def square_of_bank(b, sums, tag=None):
             sq = sb("sq%d" % b, [P, B, PACK], BF16, tag)
             nc.scalar.activation(sq[:], across(sums), SQUARE, scale=0.5)
             return sq
 
+        def first_by_scalar(b, sums_b, tag):
+            flat = sb("flat%d" % b, [P, PACK, B], BF16, tag)
+            for t in range(PACK):
+                nc.scalar.activation(flat[:, t, :], sums_b[:, t * B : (t + 1) * B], COPY, scale=first[:, t : t + 1])
+            z2 = sb("z2_%d" % b, [P, B, PACK], BF16)
+            nc.vector.tensor_copy(out=woven_lines(z2), in_=by_lines(flat))
+            return z2
+
         def signed(b, sq):
             z = sb("z_%d" % b, [P, B, PACK], BF16)
             nc.vector.tensor_tensor(z[:], sq[:], sign[:], MULT)
             return z
-
-        s23 = sb("s23", [P, N], U8, "xw")
 
         def multiply(b, order, values, banks, tag=None):
             codes = sb("codes%d%d" % (b, order), [P, B], U32, tag)
@@ -272,49 +280,46 @@ def tile_picked_ace8_none_po_kernel(
                 in_=res_i[:].rearrange("p j t -> p (j t)"),
             )
 
-        apart0 = gather_and_turn(0, (1, 0), "ring_a")
-        apart1 = gather_and_turn(1, (3, 2), "ring_b")
-        sums = [bank("sums0", 5), bank("sums1", 4)]
-        sums0, sums1 = sums
-        for b in (1, 0):
-            turn_back(gate_turned(b, 0, apart0[b]), sums[b], True, False)
-        apart2 = gather_and_turn(2, (1, 0), "xs")
-        turned = [gate_turned(b, 1, apart1[b]) for b in (1, 0)]
-        deal_bytes(s23[:], s23_raw[:])
-        pair = sb("pair", [P, PACK, HALF], F32, "w1_raw")
-        nc.vector.tensor_tensor(pair[:], wide[:, 0], wide[:, 1], ADD)
+        apart0 = gather_and_turn(0, (0, 1), None)
+        apart1 = gather_and_turn(1, (2, 3), None)
+        sums = [bank("sums0", 4), bank("sums1", 5)]
+        gate_and_turn_back(0, apart0)
+        apart2 = gather_and_turn(2, (0, 1), "column0")
+        gate_and_turn_back(1, apart1)
+        gate_and_turn_back(2, apart2)
         total3 = add_third(3, pair)
         total2 = add_third(2, pair)
-        turn_back(gate_onto(1, 2, apart2[1], turned[0], "wide"), sums1, False, True)
-        turn_back(gate_onto(0, 2, apart2[0], turned[1], "w1_raw"), sums0, False, True)
         sq3 = square_of_planes(3, total3, None)
         sq2 = square_of_planes(2, total2, None)
         z2_3 = first_of_planes(3, total3)
-        z2_2 = first_of_planes(2, total2)
-        out3, out2, out1 = [bank("out3", 6)], [bank("out2", 7)], [bank("out1", 2)]
-        multiply(3, 0, z2_3, out3)
-        z2_1 = first_of_bank(1, sums1)
-        multiply(2, 0, z2_2, out2)
-        sq1 = square_of_bank(1, sums1)
+        total1 = sb("total1", [P, PACK, B], F32, "pair")
+        nc.vector.tensor_tensor(total1[:, 0, :], pair1[:], third[:, 0, :B], ADD)
         z_3 = signed(3, sq3)
-        multiply(1, 0, z2_1, out1)
-        z2_0 = first_of_bank(0, sums0, "total3")
+        out3, out2, out0 = [bank("out3", 6)], [bank("out2", 7)], [bank("out0", 2)]
+        multiply(3, 0, z2_3, out3)
+        z2_2 = first_of_planes(2, total2)
         multiply(3, 1, z_3, out3)
-        sq0 = square_of_bank(0, sums0, "sq3")
         z_2 = signed(2, sq2)
-        out0 = [bank("out0a", 3), bank("out0b", 0)]
-        multiply(0, 0, z2_0, out0)
-        z_1 = signed(1, sq1)
+        multiply(2, 0, z2_2, out2)
+        z2_0 = first_by_scalar(0, sums[0], "total3")
         multiply(2, 1, z_2, out2)
+        sq0 = square_of_bank(0, sums[0], "sq3")
+        nc.scalar.copy(out=total1[:, 1:, :].rearrange("p t j -> p (t j)"), in_=sums[1][:, B:])
+        sq1 = square_of_planes(1, total1, None)
         z_0 = signed(0, sq0)
-        multiply(1, 1, z_1, out1)
+        multiply(0, 0, z2_0, out0)
+        z2_1 = first_of_planes(1, total1)
         multiply(0, 1, z_0, out0)
+        z_1 = signed(1, sq1)
+        out1 = [bank("out1a", 0), bank("out1b", 1)]
+        multiply(1, 0, z2_1, out1)
+        multiply(1, 1, z_1, out1)
         leave(3, out3)
         leave(2, out2)
-        leave(1, out1)
-        nc.sync.dma_start(out=out_words[:, B:], in_=out_codes[:, B:].bitcast(I32))
+        nc.sync.dma_start(out=out_words[:, HALF:], in_=out_codes[:, HALF:].bitcast(I32))
         leave(0, out0)
-        nc.sync.dma_start(out=out_words[:, :B], in_=out_codes[:, :B].bitcast(I32))
+        leave(1, out1)
+        nc.sync.dma_start(out=out_words[:, :HALF], in_=out_codes[:, :HALF].bitcast(I32))
         for q in range(4):
             queue = nc.sync if q % 2 == 0 else nc.scalar
             queue.dma_start(

@@ -48,10 +48,9 @@ def tile_picked_ace8_none_po_kernel(
             return w[0].rearrange("p n t -> p (n t)").bitcast(I32)
 
         def load_scales(tile, first_row, src):
-            for q in range(4):
+            for r in range(4):
                 nc.sync.dma_start(
-                    out=tile[32 * q + first_row : 32 * q + first_row + 4, :].bitcast(I32),
-                    in_=src[0, 4 * q : 4 * q + 4, :].bitcast(I32),
+                    out=tile[first_row + r : P : 32, :].bitcast(I32), in_=src[0, r:16:4, :].bitcast(I32)
                 )
 
         def load_column(dst, g):
@@ -65,7 +64,7 @@ def tile_picked_ace8_none_po_kernel(
 
         def deal_bytes(dst, src):
             nc.vector.tensor_copy(
-                out=dst.rearrange("p (t m) -> p t m", t=PACK), in_=src.rearrange("p (m t) -> p t m", t=PACK)
+                out=dst.rearrange("p (t m) -> p m t", t=PACK), in_=src.rearrange("p (m t) -> p m t", t=PACK)
             )
 
         offs_sb = sb("offs_sb", [P, S // 16], U16)
@@ -82,19 +81,20 @@ def tile_picked_ace8_none_po_kernel(
         gate_rows = [sb("gate_row%d" % n, [P, S - B], F32)[:] for n in range(TERMS)]
         gate_cols = [sb("column%d" % n, [P, 2], F32)[:] for n in range(TERMS)]
         nc.gpsimd.memset(xs[:].bitcast(I32), 0)
-        nc.vector.memset(s1_raw[:].bitcast(I32), 0)
         nc.vector.memset(s23_raw[:].bitcast(I32), 0)
-        nc.scalar.dma_start(out=c2_sb[:], in_=c2.rearrange("(p t) o -> p (t o)", t=PACK))
-        nc.sync.dma_start(out=xw[:], in_=words_of(x_words))
+        for q in range(4):
+            rows = w1_scales[0, 4 * q : 4 * q + 4, :].bitcast(I32)
+            nc.scalar.dma_start(
+                out=s1_raw[32 * q : 32 * q + 32, :].bitcast(I32), in_=rows.unsqueeze(0).broadcast_to([8, 4, H // 4])
+            )
         nc.sync.dma_start(offs_sb[:], offs)
-        nc.sync.dma_start(out=w1_raw[:], in_=words_of(w1_words))
+        nc.sync.dma_start(out=c2_sb[:], in_=c2.rearrange("(p t) o -> p (t o)", t=PACK))
+        nc.sync.dma_start(out=xw[:], in_=words_of(x_words))
         load_scales(xs, 0, x_scales)
-        load_scales(s1_raw, 0, w1_scales)
-        nc.sync.dma_start(lists[0][:], p1)
+        nc.sync.dma_start(out=w1_raw[:], in_=words_of(w1_words))
         for z, w in enumerate((w2_words, w3_words)):
             nc.sync.dma_start(out=w_raw[z][:], in_=words_of(w))
-        nc.sync.dma_start(out=gate_rows[0], in_=g1[:, B:])
-        for n, p, g in ((1, p2, g2), (2, p3, g3)):
+        for n, (p, g) in enumerate(((p1, g1), (p2, g2), (p3, g3))):
             nc.sync.dma_start(lists[n][:], p)
             nc.sync.dma_start(out=gate_rows[n], in_=g[:, B:])
         nc.sync.dma_start(out=c1_sb[:], in_=c1.rearrange("(p t) o -> p (t o)", t=PACK))
@@ -117,6 +117,8 @@ def tile_picked_ace8_none_po_kernel(
         nc.vector.reciprocal(inv_twice[:], twice[:])
 
 
+        s1 = sb("s1", [P, H], U8)
+        deal_bytes(s1[:], s1_raw[:])
         xg_w, xg_s = sb("xg_w", [P, S], U32), sb("xg_s", [P, S], U8)
         for h in range(2):
             nc.vector.tensor_copy(
@@ -127,13 +129,7 @@ def tile_picked_ace8_none_po_kernel(
         w1_first, w1_rest = sb("w1_first", [P, P], U32), sb("w1_rest", [P, H - P], U32)
         deal(nc.scalar.copy, w1_first[:], w1_raw[:].bitcast(U32), 0, 1)
         deal(nc.scalar.copy, w1_rest[:], w1_raw[:].bitcast(U32), 1, PACK)
-        s1 = sb("s1", [P, H], U8)
-        for t0, t1 in ((0, 1), (1, PACK)):
-            nc.vector.tensor_copy(
-                out=s1[:, t0 * P : t1 * P].rearrange("p (t m) -> p m t", t=t1 - t0),
-                in_=s1_raw[:].rearrange("p (m t) -> p m t", t=PACK)[:, :, t0:t1],
-            )
-        w_both = sb("w_both", [P, 2, N], I32, "s1_raw")
+        w_both = sb("w_both", [P, 2, N], I32, "xs")
         for z in range(2):
             deal(nc.vector.tensor_copy, w_both[:, z, :], w_raw[z][:], 0, PACK)
 

@@ -27,6 +27,7 @@ PACK = 4
 B = 128
 HALF = S // 2
 TERMS = 3
+SUM_BYTES = PACK * B * 4
 
 
 def tile_picked_ace8_none_po_kernel(
@@ -36,6 +37,7 @@ def tile_picked_ace8_none_po_kernel(
     nc = tc.nc
     with ExitStack() as ctx:
         keep = ctx.enter_context(tc.tile_pool(name="keep", bufs=1))
+        tied = ctx.enter_context(tc.tile_pool(name="tied", bufs=1))
         psum = ctx.enter_context(tc.psum_pool(name="psum", bufs=1))
 
         def sb(name, shape, dtype, tag=None):
@@ -76,7 +78,7 @@ def tile_picked_ace8_none_po_kernel(
         c1_sb, c2_sb = sb("c1_sb", [P, PACK], F32), sb("c2_sb", [P, PACK], F32)
         ident = sb("ident", [P, P], F32)
 
-        s23_raw = sb("s23_raw", [P, N], U8)
+        s23_raw = tied.tile([P, N], U8, name="s23_raw", align_bytes=64, offset=SUM_BYTES - N // 2)
         w_raw = [sb("w_raw%d" % z, [P, N], I32) for z in range(2)]
         gate_rows = [sb("gate_row%d" % n, [P, S - B], F32)[:] for n in range(TERMS)]
         gate_cols = [sb("column%d" % n, [P, 2], F32)[:] for n in range(TERMS)]
@@ -94,9 +96,11 @@ def tile_picked_ace8_none_po_kernel(
         nc.sync.dma_start(out=w1_raw[:], in_=words_of(w1_words))
         for z, w in enumerate((w2_words, w3_words)):
             nc.sync.dma_start(out=w_raw[z][:], in_=words_of(w))
-        for n, (p, g) in enumerate(((p1, g1), (p2, g2), (p3, g3))):
+        for n, (p, g) in enumerate(((p1, g1), (p2, g2))):
             nc.sync.dma_start(lists[n][:], p)
             nc.sync.dma_start(out=gate_rows[n], in_=g[:, B:])
+        nc.sync.dma_start(lists[2][:], p3)
+        nc.sync.dma_start(out=gate_rows[2], in_=g3[:, B:])
         nc.sync.dma_start(out=c1_sb[:], in_=c1.rearrange("(p t) o -> p (t o)", t=PACK))
         for n, g in enumerate((g1, g2, g3)):
             load_column(gate_cols[n], g)
@@ -164,11 +168,11 @@ def tile_picked_ace8_none_po_kernel(
         nc.vector.tensor_tensor(pair1[:], wide[:, 0, 0, :B], wide[:, 1, 0, :B], ADD)
         pair = sb("pair", [P, PACK, HALF], F32)
         nc.vector.tensor_tensor(pair[:], wide[:, 0, :, B:], wide[:, 1, :, B:], ADD)
-        s23 = sb("s23", [P, N], U8)
-        deal_bytes(s23[:], s23_raw[:])
-        third = sb("third", [P, PACK, S - B], F32, "s23_raw")
+        third = sb("third", [P, PACK, S - B], F32)
         for t in range(PACK):
             gated_gather(third, t, 2)
+        s23 = sb("s23", [P, N], U8)
+        deal_bytes(s23[:], s23_raw[:])
 
         def gather_and_turn(n, numbers, tag):
             terms = sb("terms%d" % n, [P, PACK, HALF], F32, tag)
@@ -193,14 +197,14 @@ def tile_picked_ace8_none_po_kernel(
                     )
 
         def add_third(b, pair):
-            total = sb("total%d" % b, [P, PACK, B], F32)
+            total = tied.tile([P, PACK, B], F32, name="total%d" % b, align_bytes=64, offset=(3 - b) * SUM_BYTES)[:]
             nc.vector.tensor_tensor(
-                total[:], pair[:, :, (b - 2) * B : (b - 1) * B], third[:, :, (b - 1) * B : b * B], ADD
+                total, pair[:, :, (b - 2) * B : (b - 1) * B], third[:, :, (b - 1) * B : b * B], ADD
             )
             return total
 
         def by_lines(planes):
-            return planes[:].rearrange("p t (c i) -> p c t i", i=4)
+            return planes.rearrange("p t (c i) -> p c t i", i=4)
 
         def woven_lines(woven):
             return woven[:].rearrange("p (c i) t -> p c t i", i=4)
@@ -224,12 +228,12 @@ def tile_picked_ace8_none_po_kernel(
             nc.scalar.activation(sq[:], across(sums), SQUARE, scale=0.5)
             return sq
 
-        def first_by_scalar(b, sums_b, tag):
-            flat = sb("flat%d" % b, [P, PACK, B], BF16, tag)
+        def first_by_scalar(b, sums_b):
+            flat = tied.tile([P, PACK, B], BF16, name="flat%d" % b, align_bytes=64, offset=0)
             for t in range(PACK):
                 nc.scalar.activation(flat[:, t, :], sums_b[:, t * B : (t + 1) * B], COPY, scale=first[:, t : t + 1])
             z2 = sb("z2_%d" % b, [P, B, PACK], BF16)
-            nc.vector.tensor_copy(out=woven_lines(z2), in_=by_lines(flat))
+            nc.vector.tensor_copy(out=woven_lines(z2), in_=by_lines(flat[:]))
             return z2
 
         def signed(b, sq):
@@ -270,7 +274,7 @@ def tile_picked_ace8_none_po_kernel(
                     out=res[:, u * share : (u + 1) * share, :].rearrange("p t j -> p (t j)"), in_=held[:, : share * B]
                 )
             nc.sync.dma_start(out=out_rows[:, :, cols], in_=res[:])
-            nc.vector.tensor_copy(out=woven_lines(res_i), in_=by_lines(res))
+            nc.vector.tensor_copy(out=woven_lines(res_i), in_=by_lines(res[:]))
             nc.vector.quantize_mx(
                 out=out_codes[:, cols].bitcast(FP8X4), scales=out_scales[:, cols],
                 in_=res_i[:].rearrange("p j t -> p (j t)"),
@@ -297,14 +301,14 @@ def tile_picked_ace8_none_po_kernel(
         multiply(3, 1, z_3, out3)
         z_2 = signed(2, sq2)
         multiply(2, 0, z2_2, out2)
-        z2_0 = first_by_scalar(0, sums[0], "total3")
+        z2_0 = first_by_scalar(0, sums[0])
         multiply(2, 1, z_2, out2)
         sq0 = square_of_bank(0, sums[0], "sq3")
         nc.scalar.copy(out=total1[:, 1:, :].rearrange("p t j -> p (t j)"), in_=sums[1][:, B:])
-        sq1 = square_of_planes(1, total1, None)
+        sq1 = square_of_planes(1, total1[:], None)
         z_0 = signed(0, sq0)
         multiply(0, 0, z2_0, out0)
-        z2_1 = first_of_planes(1, total1)
+        z2_1 = first_of_planes(1, total1[:])
         multiply(0, 1, z_0, out0)
         z_1 = signed(1, sq1)
         out1 = [bank("out1a", 0), bank("out1b", 1)]

@@ -129,7 +129,11 @@ def tile_picked_ace8_none_po_kernel(
                 out=xg_w[:, h * HALF : (h + 1) * HALF],
                 in_=xw[:].bitcast(U32).indirect(offs_sb[:, h * HALF // 16 : (h + 1) * HALF // 16]),
             )
-        nc.vector.tensor_copy(out=xg_s[:], in_=xs[:].indirect(offs_sb[:]))
+        for h in range(2):
+            nc.vector.tensor_copy(
+                out=xg_s[:, h * HALF : (h + 1) * HALF],
+                in_=xs[:].indirect(offs_sb[:, h * HALF // 16 : (h + 1) * HALF // 16]),
+            )
         w1_first, w1_rest = sb("w1_first", [P, P], U32), sb("w1_rest", [P, H - P], U32)
         deal(nc.scalar.copy, w1_first[:], w1_raw[:].bitcast(U32), 0, 1)
         deal(nc.scalar.copy, w1_rest[:], w1_raw[:].bitcast(U32), 1, PACK)

from contextlib import ExitStack

import concourse.mybir as mybir
from concourse.masks import make_identity

K, T, S, N, H = 512, 2048, 512, 512, 512
FLOPS = 3 * 2 * 512 * 512 * 512

F32 = mybir.dt.float32
BF16 = mybir.dt.bfloat16
I32 = mybir.dt.int32
U32 = mybir.dt.uint32
U16 = mybir.dt.uint16
U8 = mybir.dt.uint8
FP8X4 = mybir.dt.float8_e4m3fn_x4
MULT = mybir.AluOpType.mult
ADD = mybir.AluOpType.add
MAX = mybir.AluOpType.max
COPY = mybir.ActivationFunctionType.Copy
SQRT = mybir.ActivationFunctionType.Sqrt
IDENTITY = mybir.ActivationFunctionType.Identity
SIGN = mybir.ActivationFunctionType.Sign
SQUARE = mybir.ActivationFunctionType.Square

P = 128
PACK = 4
B = 128
HALF = S // 2
TERMS = 3
SUM_BYTES = PACK * B * 4


def tile_picked_ace8_none_po_kernel(
    tc, x_words, x_scales, w1_words, w1_scales, g1, g2, g3, c2, c1,
    w2_words, w2_scales, w3_words, w3_scales, offs, p1, p2, p3, out_0, out_1, out_2,
):
    nc = tc.nc
    with ExitStack() as ctx:
        keep = ctx.enter_context(tc.tile_pool(name="keep", bufs=1))
        tied = ctx.enter_context(tc.tile_pool(name="tied", bufs=1))
        psum = ctx.enter_context(tc.psum_pool(name="psum", bufs=1))

        def sb(name, shape, dtype, tag=None):
            return keep.tile(shape, dtype, name=name, tag=tag or name, align_bytes=64)

        def bank(name, number):
            return psum.tile([P, 512], F32, name=name, tag="bank%d" % number)

        def words_of(w):
            return w[0].rearrange("p n t -> p (n t)").bitcast(I32)

        def load_scales(tile, first_row, src):
            for r in range(4):
                nc.sync.dma_start(
                    out=tile[first_row + r : P : 32, :].bitcast(I32), in_=src[0, r:16:4, :].bitcast(I32)
                )

        def load_column(dst, g):
            nc.sync.dma_start(out=dst, in_=g[0, :HALF].rearrange("(b p) -> p b", p=P), allow_slow_non_contiguous=True)

        def deal(move, dst, src, t0, t1):
            move(
                out=dst.rearrange("p (t c i) -> p c t i", t=t1 - t0, i=4),
                in_=src.rearrange("p (c i t) -> p c t i", t=PACK, i=4)[:, :, t0:t1, :],
            )

        def deal_bytes(dst, src):
            nc.vector.tensor_copy(
                out=dst.rearrange("p (t m) -> p m t", t=PACK), in_=src.rearrange("p (m t) -> p m t", t=PACK)
            )

        offs_sb = sb("offs_sb", [P, S // 16], U16)
        lists = [sb("list%d" % n, [P, S // 16], U16) for n in range(TERMS)]
        xw = sb("xw", [P, T], I32)
        xs = sb("xs", [P, T], U8)
        s1_raw = sb("s1_raw", [P, H], U8)
        w1_raw = sb("w1_raw", [P, H], I32)
        c1_sb, c2_sb = sb("c1_sb", [P, PACK], F32), sb("c2_sb", [P, PACK], F32)
        ident = sb("ident", [P, P], F32)

        s23_raw = tied.tile([P, N], U8, name="s23_raw", align_bytes=64, offset=SUM_BYTES - N // 2)
        w_raw = [sb("w_raw%d" % z, [P, N], I32) for z in range(2)]
        gate_rows = [sb("gate_row%d" % n, [P, S - B], F32)[:] for n in range(TERMS)]
        gate_cols = [sb("column%d" % n, [P, 2], F32)[:] for n in range(TERMS)]
        nc.gpsimd.memset(xs[:].bitcast(I32), 0)
        nc.vector.memset(s23_raw[:].bitcast(I32), 0)
        for q in range(4):
            rows = w1_scales[0, 4 * q : 4 * q + 4, :].bitcast(I32)
            nc.scalar.dma_start(
                out=s1_raw[32 * q : 32 * q + 32, :].bitcast(I32), in_=rows.unsqueeze(0).broadcast_to([8, 4, H // 4])
            )
        nc.sync.dma_start(offs_sb[:], offs)
        nc.sync.dma_start(out=c2_sb[:], in_=c2.rearrange("(p t) o -> p (t o)", t=PACK))
        nc.sync.dma_start(out=xw[:], in_=words_of(x_words))
        load_scales(xs, 0, x_scales)
        nc.sync.dma_start(out=w1_raw[:], in_=words_of(w1_words))
        for z, w in enumerate((w2_words, w3_words)):
            nc.sync.dma_start(out=w_raw[z][:], in_=words_of(w))
        for n, (p, g) in enumerate(((p1, g1), (p2, g2))):
            nc.sync.dma_start(lists[n][:], p)
            nc.sync.dma_start(out=gate_rows[n], in_=g[:, B:])
        nc.sync.dma_start(lists[2][:], p3)
        nc.sync.dma_start(out=gate_rows[2], in_=g3[:, B:])
        nc.sync.dma_start(out=c1_sb[:], in_=c1.rearrange("(p t) o -> p (t o)", t=PACK))
        for n, g in enumerate((g1, g2, g3)):
            load_column(gate_cols[n], g)
        load_scales(s23_raw, 0, w2_scales)
        load_scales(s23_raw, 4, w3_scales)
        make_identity(nc, ident[:])

        size, guess, inv_guess, twice = (sb(name, [P, PACK], F32) for name in ("size", "guess", "inv_guess", "twice"))
        sign = sb("sign", [P, B, PACK], BF16)
        nc.vector.scalar_tensor_tensor(size[:], c2_sb[:], -1.0, c2_sb[:], MULT, MAX)
        nc.scalar.activation(guess[:], size[:], SQRT, bias=2.0**-100)
        nc.vector.reciprocal(inv_guess[:], guess[:])
        for t in range(PACK):
            col = slice(t, t + 1)
            nc.scalar.activation(twice[:, col], inv_guess[:, col], IDENTITY, bias=guess[:, col], scale=size[:, col])
        nc.scalar.activation(sign[:], c2_sb[:].unsqueeze(1).broadcast_to([P, B, PACK]), SIGN, scale=guess[:, 0:1])
        inv_twice = sb("inv_twice", [P, PACK], F32)
        nc.vector.reciprocal(inv_twice[:], twice[:])


        s1 = sb("s1", [P, H], U8)
        deal_bytes(s1[:], s1_raw[:])
        xg_w, xg_s = sb("xg_w", [P, S], U32), sb("xg_s", [P, S], U8)
        for h in range(2):
            nc.vector.tensor_copy(
                out=xg_w[:, h * HALF : (h + 1) * HALF],
                in_=xw[:].bitcast(U32).indirect(offs_sb[:, h * HALF // 16 : (h + 1) * HALF // 16]),
            )
        for h in range(2):
            nc.vector.tensor_copy(
                out=xg_s[:, h * HALF : (h + 1) * HALF],
                in_=xs[:].indirect(offs_sb[:, h * HALF // 16 : (h + 1) * HALF // 16]),
            )
        w1_first, w1_rest = sb("w1_first", [P, P], U32), sb("w1_rest", [P, H - P], U32)
        deal(nc.scalar.copy, w1_first[:], w1_raw[:].bitcast(U32), 0, 1)
        deal(nc.scalar.copy, w1_rest[:], w1_raw[:].bitcast(U32), 1, PACK)
        w_both = sb("w_both", [P, 2, N], I32, "xs")
        for z in range(2):
            deal(nc.vector.tensor_copy, w_both[:, z, :], w_raw[z][:], 0, PACK)

        y = [sb("y%d" % t, [P, S], F32) for t in range(PACK)]
        for t in range(PACK):
            w1_t = w1_first[:] if t == 0 else w1_rest[:, (t - 1) * P : t * P]
            for h, cols in enumerate([slice(0, HALF), slice(HALF, S)] if t == 0 else [slice(0, S)]):
                y_ps = bank("y_ps%d%d" % (t, h), 4 if h == 1 else t)
                nc.tensor.matmul_mx(
                    out=y_ps[:, cols], lhsT=w1_t.bitcast(FP8X4), lhsT_scale=s1[:, t * P : (t + 1) * P],
                    rhs=xg_w[:, cols].bitcast(FP8X4), rhs_scale=xg_s[:, cols], start=True, stop=True,
                )
                nc.scalar.activation(y[t][:, cols], y_ps[:, cols], COPY, scale=twice[:, t : t + 1])

        def picks(t, n, start, count):
            return y[t][:].indirect(lists[n][:, start // 16 : (start + count) // 16])

        first = sb("first", [P, PACK], F32)
        nc.vector.tensor_tensor(first[:], c1_sb[:], inv_twice[:], MULT)

        def gated_gather(into, t, n):
            start = B if t == 0 else HALF
            nc.vector.tensor_tensor(
                into[:, t, start - B :], picks(t, n, start, S - start), gate_rows[n][:, start - B :], MULT
            )

        wide = sb("wide", [P, 2, PACK, S - B], F32)
        for t in range(PACK):
            for n in range(2):
                gated_gather(wide[:, n], t, n)
        pair1 = sb("pair1", [P, B], F32)
        nc.vector.tensor_tensor(pair1[:], wide[:, 0, 0, :B], wide[:, 1, 0, :B], ADD)
        pair = sb("pair", [P, PACK, HALF], F32)
        nc.vector.tensor_tensor(pair[:], wide[:, 0, :, B:], wide[:, 1, :, B:], ADD)
        third = sb("third", [P, PACK, S - B], F32)
        for t in range(PACK):
            gated_gather(third, t, 2)
        s23 = sb("s23", [P, N], U8)
        deal_bytes(s23[:], s23_raw[:])

        def gather_and_turn(n, numbers, tag):
            terms = sb("terms%d" % n, [P, PACK, HALF], F32, tag)
            apart = [bank("apart%d%d" % (b, n), numbers[b]) for b in range(2)]
            for t in range(PACK):
                blocks = 1 if t == 0 else 2
                nc.scalar.activation(terms[:, t, : blocks * B], picks(t, n, 0, blocks * B), COPY)
                for b in range(blocks):
                    nc.tensor.transpose(apart[b][:, t * P : (t + 1) * P], terms[:, t, b * B : (b + 1) * B], ident[:])
            return apart

        def gate_and_turn_back(n, apart):
            for b in range(2):
                turned = sb("turned%d%d" % (b, n), [P, PACK * P], F32)
                nc.scalar.activation(
                    turned[:, b * P :], apart[b][:, b * P :], COPY, scale=gate_cols[n][:, b : b + 1]
                )
                for t in range(b, PACK):
                    nc.tensor.matmul(
                        sums[b][:, t * B : (t + 1) * B], turned[:, t * P : (t + 1) * P], ident[:],
                        start=(n == 0 and t == b), stop=(n == TERMS - 1 and t == PACK - 1), is_transpose=True,
                    )

        def add_third(b, pair):
            total = tied.tile([P, PACK, B], F32, name="total%d" % b, align_bytes=64, offset=(3 - b) * SUM_BYTES)[:]
            nc.vector.tensor_tensor(
                total, pair[:, :, (b - 2) * B : (b - 1) * B], third[:, :, (b - 1) * B : b * B], ADD
            )
            return total

        def by_lines(planes):
            return planes.rearrange("p t (c i) -> p c t i", i=4)

        def woven_lines(woven):
            return woven[:].rearrange("p (c i) t -> p c t i", i=4)

        def first_of_planes(b, total):
            z2 = sb("z2_%d" % b, [P, B, PACK], BF16)
            factor = first[:].unsqueeze(1).unsqueeze(3).broadcast_to([P, B // 4, PACK, 4])
            nc.vector.tensor_tensor(woven_lines(z2), by_lines(total), factor, MULT)
            return z2

        def square_of_planes(b, total, tag):
            sq = sb("sq%d" % b, [P, B, PACK], BF16, tag)
            nc.scalar.activation(woven_lines(sq), by_lines(total), SQUARE, scale=0.5)
            return sq

        def across(sums):
            return sums[:].rearrange("p (t j) -> p j t", t=PACK)

        def square_of_bank(b, sums, tag=None):
            sq = sb("sq%d" % b, [P, B, PACK], BF16, tag)
            nc.scalar.activation(sq[:], across(sums), SQUARE, scale=0.5)
            return sq

        def first_by_scalar(b, sums_b):
            flat = tied.tile([P, PACK, B], BF16, name="flat%d" % b, align_bytes=64, offset=0)
            for t in range(PACK):
                nc.scalar.activation(flat[:, t, :], sums_b[:, t * B : (t + 1) * B], COPY, scale=first[:, t : t + 1])
            z2 = sb("z2_%d" % b, [P, B, PACK], BF16)
            nc.vector.tensor_copy(out=woven_lines(z2), in_=by_lines(flat[:]))
            return z2

        def signed(b, sq):
            z = sb("z_%d" % b, [P, B, PACK], BF16)
            nc.vector.tensor_tensor(z[:], sq[:], sign[:], MULT)
            return z

        def multiply(b, order, values, banks, tag=None):
            codes = sb("codes%d%d" % (b, order), [P, B], U32, tag)
            scales = sb("scales%d%d" % (b, order), [P, B], U8)
            nc.vector.quantize_mx(
                out=codes[:].bitcast(FP8X4), scales=scales[:], in_=values[:].rearrange("p j t -> p (j t)")
            )
            share = PACK // len(banks)
            for t in range(PACK):
                nc.tensor.matmul_mx(
                    out=banks[t // share][:, t % share * B : (t % share + 1) * B],
                    lhsT=w_both[:, order, t * P : (t + 1) * P].bitcast(FP8X4),
                    lhsT_scale=s23[4 * order : P, t * P : (t + 1) * P],
                    rhs=codes[:].bitcast(FP8X4),
                    rhs_scale=scales[:],
                    start=(order == 0 and t % share == 0),
                    stop=(order == 1 and t % share == share - 1),
                )

        out_codes = sb("out_codes", [P, S], U32)
        out_scales = sb("out_scales", [P, S], U8)
        out_rows = out_0.rearrange("(p t) j -> p t j", t=PACK)
        out_words = words_of(out_1)

        def leave(b, banks):
            cols = slice(b * B, (b + 1) * B)
            res = sb("res%d" % b, [P, PACK, B], F32)
            res_i = sb("res_i%d" % b, [P, B, PACK], BF16)
            share = PACK // len(banks)
            for u, held in enumerate(banks):
                nc.scalar.copy(
                    out=res[:, u * share : (u + 1) * share, :].rearrange("p t j -> p (t j)"), in_=held[:, : share * B]
                )
            nc.sync.dma_start(out=out_rows[:, :, cols], in_=res[:])
            nc.vector.tensor_copy(out=woven_lines(res_i), in_=by_lines(res[:]))
            nc.vector.quantize_mx(
                out=out_codes[:, cols].bitcast(FP8X4), scales=out_scales[:, cols],
                in_=res_i[:].rearrange("p j t -> p (j t)"),
            )

        apart0 = gather_and_turn(0, (0, 1), None)
        apart1 = gather_and_turn(1, (2, 3), None)
        sums = [bank("sums0", 4), bank("sums1", 5)]
        gate_and_turn_back(0, apart0)
        apart2 = gather_and_turn(2, (0, 1), "column0")
        gate_and_turn_back(1, apart1)
        gate_and_turn_back(2, apart2)
        total3 = add_third(3, pair)
        total2 = add_third(2, pair)
        sq3 = square_of_planes(3, total3, None)
        sq2 = square_of_planes(2, total2, None)
        z2_3 = first_of_planes(3, total3)
        total1 = sb("total1", [P, PACK, B], F32, "pair")
        nc.vector.tensor_tensor(total1[:, 0, :], pair1[:], third[:, 0, :B], ADD)
        z_3 = signed(3, sq3)
        out3, out2, out0 = [bank("out3", 6)], [bank("out2", 7)], [bank("out0", 2)]
        multiply(3, 0, z2_3, out3)
        z2_2 = first_of_planes(2, total2)
        multiply(3, 1, z_3, out3)
        z_2 = signed(2, sq2)
        multiply(2, 0, z2_2, out2)
        z2_0 = first_by_scalar(0, sums[0])
        multiply(2, 1, z_2, out2)
        sq0 = square_of_bank(0, sums[0], "sq3")
        nc.scalar.copy(out=total1[:, 1:, :].rearrange("p t j -> p (t j)"), in_=sums[1][:, B:])
        sq1 = square_of_planes(1, total1[:], None)
        z_0 = signed(0, sq0)
        multiply(0, 0, z2_0, out0)
        z2_1 = first_of_planes(1, total1[:])
        multiply(0, 1, z_0, out0)
        z_1 = signed(1, sq1)
        out1 = [bank("out1a", 0), bank("out1b", 1)]
        multiply(1, 0, z2_1, out1)
        multiply(1, 1, z_1, out1)
        leave(3, out3)
        leave(2, out2)
        nc.sync.dma_start(out=out_words[:, HALF:], in_=out_codes[:, HALF:].bitcast(I32))
        leave(0, out0)
        leave(1, out1)
        nc.sync.dma_start(out=out_words[:, :HALF], in_=out_codes[:, :HALF].bitcast(I32))
        for q in range(4):
            queue = nc.sync if q % 2 == 0 else nc.scalar
            queue.dma_start(
                out=out_2[0, 4 * q : 4 * q + 4, :].bitcast(I32),
                in_=out_scales[32 * q : 32 * q + 4, :].bitcast(I32),
            )
